import numpy as np, ml_dtypes
CORES = [66,74,82,90,194,202,210,218]
N = 8
import mx_ref
BF = ml_dtypes.bfloat16
def gcols(t, e):
    v = np.concatenate([t.reshape(8, 16, -1, 4), np.zeros((8, 16, 1, 4), BF)], axis=2)
    return np.ascontiguousarray(np.stack([v[g][:, e[g]] for g in range(8)])).reshape(128, -1)
def tile(rs):
    return np.stack(rs, axis=2).reshape(128, -1).astype(BF)
def pick(q, e):
    c = np.concatenate([q[0].reshape(128, -1, 4), np.zeros((128, 1, 4), np.uint8)], axis=1); s = np.concatenate([q[1], np.ones((16, 1), np.uint8)], axis=1)
    return (np.ascontiguousarray(c[:, e].reshape(128, -1)), np.ascontiguousarray(s[:, e]))
def join(*qs):
    return (np.concatenate([q[0] for q in qs], axis=1), np.concatenate([q[1] for q in qs], axis=1))
def put(q, e, v):
    c, s = q[0].reshape(128, -1, 4).copy(), q[1].copy(); c[:, e] = v[0].reshape(128, -1, 4); s[:, e] = v[1]
    return (c.reshape(128, -1), s)
def pk(c, s):
    return (np.ascontiguousarray(c), mx_ref.live(s))
def emit(q):
    return q[0], q[1]
def packed(v, rng):
    q = [mx_ref.quantize(np.ascontiguousarray(v[r])) for r in range(N)]
    return np.stack([a for a, b in q]), np.stack([mx_ref.plane(b, rng) for a, b in q])
def values_of_codes():
    e, c = np.zeros((128, 128, 4), np.float32), np.zeros((128, 2, 4), np.uint8)
    e[np.arange(128), np.arange(128), 0] = 1
    c[:127, :, 0] = np.arange(256).reshape(2, 128).T[:127]
    return mx_ref.matmul(mx_ref.quantize(e.reshape(128, 512).astype(BF)), (c.reshape(128, 8), np.full((16, 2), 127, np.uint8))).T.reshape(-1).astype(np.float64)
CODE_VALUE, SCALE_VALUE = values_of_codes(), 2.0 ** (np.arange(256) - 127.0)
def decode(q):
    return (CODE_VALUE[q[0]].reshape(16, 8, -1, 4) * SCALE_VALUE[q[1]][:, None, :, None] + 0.0).reshape(128, -1).astype(np.float32)
def f(rng, *shape):
    return mx_ref.flush((rng.standard_normal(shape, dtype=np.float32) * np.exp2(rng.integers(-2, 3, shape[:-1] + (1,)))).astype(BF))
def wide(rng, *shape, cols=0):
    v = rng.standard_normal(shape, dtype=np.float32) * np.exp2(rng.integers(-12, 13, shape)).astype(np.float32)
    if cols: v *= np.repeat(np.exp2(rng.integers(-cols, cols + 1, shape[:-2] + (1, shape[-1] // 4))) * (rng.random(shape[:-2] + (1, shape[-1] // 4)) > 0.0625), 4, axis=-1).astype(np.float32)
    return mx_ref.flush(v.astype(BF))
C, I, ST, M, R = 288, 48, 6, 96, 3
def big(v):
    v = v.astype(np.float32)
    v[np.abs(v) < np.float32(2.0 ** -16)] = 0
    return v.astype(BF)
def numbers_of(rng):
    return {"x": big(f(rng, N, 128, 4 * C)), "u": np.array(f(rng, N, 128, 512)), "v": np.array(f(rng, N, 128, 512))}
def layers(rng):
    return big(f(rng, N, 128, 2048)).reshape(N, 8, 16, 4, 8, 16, 4)
def through(w, some):
    for i in some:
        w[:, :, i] = 0
        w[:, :, :, :, :, i] = 0
        for g in range(8):
            for b in range(4): w[:, g, i, b, g, i, b] = 32
    return w
def weights(rng, w):
    c, p = packed(np.ascontiguousarray(w).reshape(N, 128, 2048), rng)
    return {"wc": c, "ws": p}
def setup_inputs(rng):
    return {**numbers_of(rng), **weights(rng, layers(rng))}
def setup_inputs_ties(rng):
    d = numbers_of(rng)
    x = d["x"].astype(np.float32).reshape(N, 8, 16, C, 4)
    x[:, :, 0] = 0
    x[:, :, 0, :, 0] = rng.integers(0, 3, (N, 8, C))
    x[:, :, 0, :, 1] = 1.125
    some = rng.permutation(8)[:4]
    k = np.exp2(rng.integers(-2, 3, (N, 8, 1, C, 1)))
    k[:, some] = 1
    s = (N, 8, 8, C, 4)
    e = rng.integers(-21, -14, s)
    for j in range(4): e[:, some[j]] = j - 21
    x[:, :, 8:] = (129 + 2 * rng.integers(0, 64, s)) * np.exp2(e) * rng.choice([-1.0, 1.0], s) * k
    x[:, :, 8, :, 0] = 1.96875 * k[:, :, 0, :, 0]
    u = d["u"].reshape(N, 128, 128, 4)
    u[:, :, ::16] = 0
    o = rng.permutation(N)
    for r in range(N):
        for h in range(0, 128, 16):
            if r != o[0]:
                if h // 16 in some: u[r, h + 9:h + 16, h] = rng.choice([-1.0, 1.0], (7, 4)).astype(np.float32).astype(BF)
                else: u[r, h, h, 0] = -1.0 if r == o[1] else 1.0
            for i in (1, 2):
                if r == o[2] or r == o[3]: u[r, :, h + i] = 0
                if r == o[3]: u[r, h, h + i, 1] = 1
    w = through(layers(rng), [0])
    for g in some:
        w[:, :, :, :, g, 8:] = 0
        w[:, g, 0, 0, g, 8, 1] = 56
        for i in range(9, 16):
            for b in range(4): w[:, g, i, b, g, i, b] = 16
    return {"x": x.reshape(N, 128, 4 * C).astype(BF), "u": u.reshape(N, 128, 512), "v": d["v"], **weights(rng, w)}
def setup_inputs_near(rng):
    d = numbers_of(rng)
    x = d["x"].astype(np.float32).reshape(N, 8, 16, C, 4)
    x[:, :, 0] = 0
    x[:, :, 8:] = 0
    c = (rng.permutation(8) % 2 * 2.0 - 1.0)[:, None]
    s = rng.integers(0, 16, (N, 8, C))
    x[:, :, 8] = ((s[:, :, :, None] >> np.arange(4)) & 1) * np.exp2(np.arange(4) - 23.0)
    u = d["u"].reshape(N, 128, 128, 4)
    u[:, :, ::16] = 0
    o = rng.permutation(N) % 4
    for r in range(N):
        if o[r] % 2 == 0:
            x[r, :, 0, :, 0] = c
            x[r, :, 11, :, 0] = 2.0 ** -10
        else:
            for g in rng.permutation(8)[:4]: x[r, g, 0, rng.integers(C), 0] = 2.0 ** 26 * rng.choice([-1.0, 1.0])
        k = 1.0 if o[r] < 2 else 2.0 ** -30
        for h in range(0, 128, 16):
            u[r, h, h, 0] = k
            u[r, h + 8, h] = k
            u[r, h + 11, h, 0] = k
    return {"x": x.reshape(N, 128, 4 * C).astype(BF), "u": u.reshape(N, 128, 512), "v": d["v"], **weights(rng, through(layers(rng), [0, 8, 9, 10, 11, 12, 13, 14, 15]))}
def setup_inputs_huge(rng):
    d = numbers_of(rng)
    o = rng.permutation(N)
    c = rng.choice([-1.0, 1.0], (N, 1, 1, C, 1))
    c[o < N // 2] = (rng.permutation(N // 2) % 2 * 2.0 - 1.0).reshape(-1, 1, 1, 1, 1)
    x = 0.9 * 2.0 ** 30 * c * (0.8 + 0.2 * rng.random((N, 1, 1, C, 1))) * (0.95 + 0.05 * rng.random((N, 8, 16, C, 4)))
    x[:, :, 0] = np.abs(x[:, :, 0])
    x[:, :, 1, :, :2] *= rng.choice([-1.0, 1.0], (N, 8, C, 2))
    u = d["u"].reshape(N, 128, 128, 4)
    a = 2.0 ** 30 * (1.0 - 0.1 * rng.random((N, 8, 16, 8, 4))) * (rng.permutation(8) % 2 * 2.0 - 1.0)[:, None]
    a[:, :, :2] = 0
    u[:, :, ::16] = a.reshape(N, 128, 8, 4).astype(np.float32).astype(BF)
    for h in range(0, 128, 16):
        u[:, :, h + 1:h + 3] = 0
        u[:, h + 1, h + 1, 0] = 1
        u[:, h + 1, h + 2, 1] = 1
    w = np.zeros((N, 128, 4, 128, 4), np.float32)
    i = np.arange(128)
    j = i[i % 16 > 1]
    for r in range(N):
        for b in range(4):
            if o[r] < N // 2: w[r, j - j % 16, b, j, b] = -16.0 * c[r, 0, 0, 0, 0]
            else: w[r, i, b, i, b] = -1
    return {"x": x.astype(np.float32).reshape(N, 128, 4 * C).astype(BF), "u": u.reshape(N, 128, 512), "v": d["v"], **weights(rng, w.astype(BF))}
def setup_inputs_few(rng):
    d = numbers_of(rng)
    x = d["x"].reshape(N, 8, 16, C, 4)
    c = np.where(rng.random((N, 8, C, 2)) < 0.0625, 1.0, -1.0)
    e = rng.permutation(N)
    c[e[1], :, :, 0] = 1
    c[e[1], :, :, 1] = -1
    c[e[2]] = -1
    for g in range(8):
        for b in range(2): c[e[2], g, rng.integers(C), b] = 1
    u = d["u"].reshape(N, 128, 128, 4)
    for h in range(0, 128, 16):
        u[:, :, h + 1:h + 3] = 0
        u[:, h + 1, h + 1, 0] = 1
        u[:, h + 1, h + 2, 1] = 1
    w = layers(rng)
    w[:, :, :, :, :, 1] = 0
    for r in e[1::2]:
        c[r] *= 2.0 ** -28
        x[r, :, :8] = 0
        x[r, :, 2:4, :, 0] = (rng.integers(-2, 3, (8, 1, C)) * 2.0 ** -28).astype(np.float32).astype(BF)
        u[r, :, ::16] = 0
        for h in range(0, 128, 16):
            u[r, h + 1, h + 1, 0] = 2.0 ** -30
            u[r, h + 1, h + 2, 1] = 2.0 ** -30
            u[r, h + 2, h, 0] = 1.875 * 2.0 ** -30
            u[r, h + 3, h, 0] = -1.75 * 2.0 ** -30
        w[r, :, :, :, :, :8] = 0
    x[:, :, 1, :, :2] = c.astype(np.float32).astype(BF)
    x[e[0]] = 0
    return {"x": x.reshape(N, 128, 4 * C), "u": u.reshape(N, 128, 512), "v": d["v"], **weights(rng, w)}
def setup_inputs_spread(rng):
    d = setup_inputs(rng)
    d["x"] = big(wide(rng, N, 128, 4 * C, cols=6))
    return d
def check_inputs(d):
    b = []
    for k in ("x", "u", "v"):
        a = np.abs(d[k].astype(np.float32))
        if not (np.isfinite(a).all() and ((a == 0) | (a >= 2.0 ** -30) & (a <= 2.0 ** 30)).all()): b.append("a value of " + k)
    none, least, most = [emit(mx_ref.quantize(np.full((128, 16), k, np.float32).astype(BF)))[1][0, 0] for k in (0.0, 2.0 ** -30, 2.0 ** 30)]
    for r in range(N):
        if ((d["wc"][r] == 0x7F) | (d["wc"][r] == 0xFF)).any(): b.append("wc: a code that is no number")
        s = mx_ref.live(d["ws"][r])
        if ((s != none) & ((s < least) | (s > most))).any(): b.append("ws: a scale out of range")
    return b
def reference(x, u, v, wc, ws):
    qu = [mx_ref.quantize(u[r]) for r in range(N)]
    lay = [pk(wc[r], ws[r]) for r in range(N)]
    now = [x[r] for r in range(N)]
    k = np.arange(I)
    taken = np.zeros((N, 8, C), np.int64)
    half = np.float32(0.5)
    for t in range(R):
        own, mine, sent = [], [], []
        for r in range(N):
            q = mx_ref.quantize(now[r])
            s = mx_ref.matmul(qu[r], q) + np.float32(0.0)
            own.append(decode(q))
            order = np.argsort(-s[::16], axis=1, kind="stable")
            even, odd = (s[1::16] > 0).astype(np.int64), (s[2::16] > 0).astype(np.int64)
            place = np.zeros((8, C), np.int64)
            np.put_along_axis(place, order, np.arange(C)[None] * np.ones((8, 1), np.int64), axis=1)
            j = place // ST
            n = 2 * j + np.where(j % 2 == 0, even, odd)
            m = 2 * ((j + I - 1) % I) + np.where(j % 2 == 0, odd, even)
            mine.append((np.minimum(n, m), np.maximum(n, m)))
            first, last = np.full((8, M), -1), np.full((8, M), -1)
            for i in range(2 * ST):
                for to, at in ((last, i), (first, 2 * ST - 1 - i)):
                    e = order[:, (ST * k + at) % C]
                    c = np.where(k % 2 == 0, np.take_along_axis(even, e, axis=1), np.take_along_axis(odd, e, axis=1))
                    np.put_along_axis(to, 2 * k + c, e, axis=1)
            a = own[r].astype(BF)
            z = ((gcols(a, first).astype(np.float32) + gcols(a, last).astype(np.float32)) * half).astype(BF).astype(np.float32)
            sent.append(mx_ref.quantize(((z + np.roll(z, -8, axis=1)) * half).astype(BF)))
        for r in range(N):
            q = sent[(r + N - 1) % N]
            h = tile([mx_ref.matmul(pick(lay[r], np.arange(128 * b, 128 * b + 128)), q) * np.float32(0.03125) for b in range(4)])
            w = mx_ref.matmul(qu[r], mx_ref.quantize(h))[::16] + np.float32(0.0)
            lo, hi = mine[r]
            taken[r] = np.where(np.take_along_axis(w, hi, axis=1) > np.take_along_axis(w, lo, axis=1), hi, lo)
            now[r] = (own[r] + gcols(h, taken[r]).astype(np.float32)).astype(BF)
    y, nd = np.zeros((N, 128, C), np.float32), np.zeros((N, 8, C), np.float32)
    oc, osc = np.zeros((N, 128, 4 * C), np.uint8), np.zeros((N, 16, C), np.uint8)
    for r in range(N):
        q = mx_ref.quantize(now[r])
        y[r] = mx_ref.matmul(mx_ref.quantize(v[r]), q)
        nd[r] = taken[r]
        oc[r], osc[r] = emit(q)
    return {"y": y, "nd": nd, "oc": oc, "osc": osc}

@@ -1,0 +1,378 @@
+from concourse.mybir import dt, AluOpType, ActivationFunctionType
+
+C, M, R = 288, 96, 3
+NT = C // 16
+BIG = 1.0e29
+FS = 304
+STEP, JUMP, DROP = 512.0, 32768.0, -1048576.0
+MEMBER = 32 * 512 + 1
+WHOLE = 12582912.0
+G0 = (0, 64, 128, 160)
+ON_ACT = (0, 1, 2)
+
+F8, U8, BF, F32, I32, U16 = "float8_e4m3fn_x4", "uint8", "bfloat16", "float32", "int32", "uint16"
+SCRATCH = {}
+
+
+def _buf(name, n, ty, where="sbuf"):
+    SCRATCH[name] = (where, [128, n], ty)
+
+
+for _n, _w, _t in (
+        ("xt", 4 * C, BF), ("ut", 512, BF), ("vt", 512, BF), ("qx", C, F8), ("sx", C, U8),
+        ("qu", 128, F8), ("su", 128, U8), ("qp", 512, F8), ("sp", 512, U8), ("qv", 128, F8), ("sv", 128, U8),
+        ("qw", 512, F8), ("sw", 512, U8), ("qe", 512, F8), ("se", 512, U8), ("qk", 128, F8), ("sk", 128, U8),
+        ("qy", 128, F8), ("sy", 128, U8), ("qh", 128, F8), ("sh", 128, U8),
+        ("zt", 640, BF), ("et", 516, BF), ("bk", 512, BF),
+        ("pi", 8, I32), ("ii", 8, I32), ("cf", 16, F32), ("ul", 24, F32), ("ul16", 32, U16),
+        ("rt", C, BF), ("kp", C, BF), ("k2", C, BF), ("k16", 2 * C, BF), ("p48", 48, F32), ("c48", 48 * 6, F32),
+        ("ca", 296, F32), ("cb", 296, F32), ("jt", C, F32), ("jc", NT, F32), ("jq", NT, F32), ("nt", M, F32),
+        ("d1", C, F32), ("sj", C, F32), ("sg", 4 * C, BF), ("jk", NT * C, BF), ("spc", 96, BF), ("rs", NT, F32), ("rd", C, BF),
+        ("rdj", NT, F32), ("pre", NT, F32), ("x1", C, BF), ("cs", C, BF), ("pl", NT, F32), ("pl16", NT, U16),
+        ("m1", C, BF), ("m2", C, F32), ("val", C, F32), ("srt", 296, F32), ("so", 768, F32),
+        ("ni", 14, I32), ("nj", 14, I32), ("nl16", 14, U16), ("f4", 4 * FS, BF), ("fs", 2 * C, BF),
+        ("ga", 4 * M, BF), ("zh", 4 * M, BF), ("yt", 512, BF), ("ht", 512, BF), ("hp", 4 * M, BF), ("hg", 2 * C, BF),
+        ("col", 2 * C, BF), ("co", 2 * C, BF), ("ab", 2 * NT, F32), ("ar", 2 * NT, F32), ("b4", 2 * NT, F32),
+        ("b3", NT, F32), ("b5", NT, F32), ("zz", NT, F32), ("nn", 2 * NT, F32), ("lh", 2 * NT, F32), ("lh16", 2 * NT, U16),
+        ("vs", M, F32), ("g1", C, F32), ("kc", 2 * C, BF), ("wl", 2 * C, BF), ("ns", 2 * C, BF), ("n16", NT, U16),
+        ("ndu", C, F32), ("ys", C, F32)):
+    _buf(_n, _w, _t)
+for _w in range(4):
+    _buf("gt%d" % _w, 4 * (C - G0[_w]), BF)
+    _buf("qg%d" % _w, C, F8)
+    _buf("sg%d" % _w, C, U8)
+for _r in range(R):
+    _buf("lc%d" % _r, M + 128, F8)
+    _buf("ls%d" % _r, M + 128, U8)
+for _b in range(8):
+    _buf("p%d" % _b, 512, F32, "psum")
+
+SEMAPHORES = ["v", "a", "t", "g", "lx", "lu", "lw", "lv", "sent", "outs"] + ["arr%d" % r for r in range(R)]
+
+
+def rank_program(g, core, T, topo):
+    rank = T.rank_of(core)
+    if rank is None:
+        return
+    A, F = AluOpType, ActivationFunctionType
+    nxt = T.cores[(rank + 1) % len(T.cores)]
+    rid, pid = topo.addr(nxt, core)
+    mask = topo.mask(core, nxt)
+    ne = len(topo.engines(core, nxt))
+    V, S, P = g.vector, g.scalar, g.tensor
+    queue = {"v": V, "a": S, "t": P, "g": g, "s": g.sync}
+    count, known, snap, last, readers = {}, {e: {} for e in queue}, {}, {}, {}
+
+    def wait(e, ev):
+        s, n = ev
+        if known[e].get(s, 0) >= n:
+            return
+        queue[e].wait_ge(T.sem[s], n)
+        for k, x in snap[ev].items():
+            known[e][k] = max(known[e].get(k, 0), x)
+
+    def op(e, call, rd, wr, sem=None):
+        need = []
+        for x in rd:
+            if x in last:
+                need.append(last[x])
+            if x[0] == "P":
+                need += [(s, n) for s, n in readers.get(x, {}).items() if s != e]
+        for x in wr:
+            if x in last:
+                need.append(last[x])
+            need += list(readers.get(x, {}).items())
+        top = {}
+        for s, n in need:
+            if not (e == "t" and s == "t"):
+                top[s] = max(top.get(s, 0), n)
+        for s in sorted(top, key=lambda k: k == e):
+            wait(e, (s, top[s]))
+        s, inc = (e, 1) if sem is None else (sem, 16)
+        call().then_inc(T.sem[s], inc)
+        count[s] = count.get(s, 0) + inc
+        ev = (s, count[s])
+        snap[ev] = dict(known[e])
+        snap[ev][s] = count[s]
+        for x in rd:
+            readers.setdefault(x, {})[s] = count[s]
+        for x in wr:
+            last[x] = ev
+            readers[x] = {}
+
+    def ts(out, in0, s1, op0, rd, wr, s2=None, op1=None):
+        if op1 is None:
+            op("v", lambda: V.tensor_scalar(out, in0, s1, None, op0), rd, wr)
+        else:
+            op("v", lambda: V.tensor_scalar(out, in0, s1, s2, op0, op1), rd, wr)
+
+    def tt(out, a, b, o, rd, wr):
+        op("v", lambda: V.tensor_tensor(out, a, b, o), rd, wr)
+
+    def cp(out, a, rd, wr):
+        op("v", lambda: V.tensor_copy(out, a), rd, wr)
+
+    def scan(out, a, b, o0, o1, rd, wr):
+        op("v", lambda: V.tensor_tensor_scan(out, a, b, 0.0, o0, o1), rd, wr)
+
+    def quant(q, s, a, b, src, rd, wr):
+        op("v", lambda: V.quantize_mx(T[q][:, a:b], T[s][:, a:b], src), rd, wr)
+
+    def act(out, a, f, rd, wr, **kw):
+        op("a", lambda: S.activation(out, a, f, **kw), rd, wr)
+
+    def mm(bank, wq, ws, a, xq, xs, n, rd, start=True, stop=True):
+        op("t", lambda: P.matmul_mx(T["p%d" % bank][:, 0:n], T[wq][:, a:a + 128], T[ws][:, a:a + 128],
+                                    T[xq][:, 0:n], T[xs][:, 0:n], start, stop), rd, ["P%d" % bank])
+
+    def iota(out, pat, base, mult, wr, small=True):
+        if small:
+            op("g", lambda: g.iota(out, pat, base, mult, allow_small_or_imprecise_dtypes=True), [], wr)
+        else:
+            op("g", lambda: g.iota(out, pat, base, mult), [], wr)
+
+    def select(out, a, pat, cmp, x, base, mult, rd, wr):
+        op("g", lambda: g.affine_select(out, a, pat, cmp, x, base, mult), rd, wr)
+
+    def words(name, a, b):
+        return T[name][:, a:b].bitcast(dt.uint32)
+
+    def pick_u(a, b):
+        off = T.ul16[:, a // 16:b // 16]
+        op("v", lambda: V.tensor_copy(words("qp", a, b), words("qu", 0, 128).indirect(off)), ["qu", "ula", "ulb"], ["qp%d" % a])
+        act(T.sp[:, a:b], T.su[:, 0:128].indirect(off), F.Copy, ["qu", "ula", "ulb"], ["sp%d" % a])
+
+    XT = ["xt0", "xt1", "xt2", "xt3"]
+    UC, U0, U1, U2 = 0, 128, 256, 384
+    UA, UB = ["qp0", "sp0"], ["qp256", "sp256"]
+
+    op("s", lambda: g.sync.dma_start(T.xt[:], T.x[:]), [], XT, sem="lx")
+    op("a", lambda: S.dma_start(T.ut[:], T.u[:]), [], ["ut"], sem="lu")
+
+    op("v", lambda: V.memset(T.zt[:], 0.0), [], ["zt"])
+    iota(T.pi[:, 0:1], [[0, 1]], 0, 1, ["pi"], small=False)
+    iota(T.ul[:], [[1, 3], [16, 8]], 0, 0, ["ul"])
+    iota(T.p48[:], [[1, 48]], 48, 0, ["p48"])
+    iota(T.rt[:], [[0, NT], [1, 16]], 0, 0, ["rt"])
+    select(T.et[:], T.zt[:, 0:516], [[-1, 516]], A.not_equal, 1.0, 3, 4, ["zt"], ["et"])
+    select(T.bk[:], T.zt[:, 0:512], [[16, 8], [0, 64]], A.is_gt, 1.0, 0, -1, ["zt"], ["bk"])
+    select(T.bk[:], T.bk[:], [[16, 8], [0, 64]], A.is_ge, 0.0, 15, -1, ["bk"], ["bk"])
+    iota(T.jc[:], [[16, NT]], 0, 0, ["jc"])
+    iota(T.jt[:], [[1, C]], MEMBER, 0, ["jt"])
+    iota(T.f4[:, 0:4 * FS:FS], [[0, 4]], 0, 0, ["f4z"])
+    iota(T.so[:, 294:384], [[0, 90]], 0, 0, ["soz"])
+    iota(T.yt[:, 4 * M:512], [[0, 128]], 0, 0, ["ytz"])
+    iota(T.ht[:, 4 * M:512], [[0, 128]], 0, 0, ["htz"])
+    iota(T.wl[:], [[0, 2 * C]], 0, 0, ["wlw", "wll"])
+    select(T.kc[:], T.zt[:, 0:2 * C], [[0, NT], [1, 32]], A.is_equal, 1.0, 0, 0, ["zt"], ["kc"])
+    select(T.k16[:, C:], T.zt[:, 0:C], [[0, NT], [1, 16]], A.is_equal, 1.0, 0, 0, ["zt"], ["k16b"])
+    iota(T.nt[:], [[1, M]], 0, 0, ["nt"])
+    p1 = T.pi[:, 0:1]
+    ts(T.ii[:, 0:1], p1, 15, A.bitwise_and, ["pi"], ["i0"])
+    ts(T.ii[:, 1:2], p1, 1, A.arith_shift_right, ["pi"], ["i1"], 7, A.bitwise_and)
+    ts(T.ii[:, 2:3], p1, 1, A.bitwise_and, ["pi"], ["i2"])
+    ts(T.ii[:, 3:4], p1, 1, A.arith_shift_right, ["pi"], ["i3"], 1, A.bitwise_and)
+    quant("qg1", "sg1", 0, 128, T.zt[:, 0:512], ["zt"], ["qg1"])
+    cp(T.cf[:, 0:4], T.ii[:, 0:4], ["i0", "i1", "i2", "i3"], ["cf"])
+    cq, ch, cc, cpar = [T.cf[:, k:k + 1] for k in range(4)]
+    h6, sig, mb = T.cf[:, 5:6], T.cf[:, 6:7], T.cf[:, 7:8]
+    cp(T.ul16[:, 8:32], T.ul[:], ["ul"], ["ula"])
+    ts(h6, ch, 6.0, A.mult, ["cf"], ["h6"])
+    ts(T.ul16[:, 0:8], T.ul[:, 8:16], cpar, A.add, ["ul", "cf"], ["ulb"])
+
+    for w in range(4):
+        n = 320 if w == 3 else 192
+        act(T["gt%d" % w][:, 0:n], T.zt[:, 0:n], F.Copy, ["zt"], ["g%d.%d" % (w, e) for e in range(4)])
+    act(sig, cc, F.Identity, ["cf"], ["sig"], scale=2.0, bias=-1.0)
+    act(mb, cc, F.Identity, ["cf"], ["mb"], scale=-2 * JUMP, bias=JUMP)
+    act(T.k16[:, 0:C], T.rt[:], F.Sign, ["rt"], ["k16"])
+    act(T.k2[:], T.k16[:, 0:C], F.Identity, ["k16"], ["k2"], scale=-4 * BIG, bias=4 * BIG)
+
+    c0, c1, c2, c3, c4, c5 = [T.c48[:, 48 * k:48 * k + 48] for k in range(6)]
+    ts(c0, T.p48[:], h6, A.subtract, ["p48", "h6"], ["c0"])
+    quant("qg2", "sg2", 0, 128, T.zt[:, 0:512], ["zt"], ["qg2"])
+    ts(c1, c0, 48.0, A.is_ge, ["c0"], ["c1"], -48.0, A.mult)
+    quant("qg3", "sg3", 0, 160, T.zt[:, 0:640], ["zt"], ["qg3"])
+    tt(c2, c0, c1, A.add, ["c0", "c1"], ["c2"])
+    ts(T.kp[:], T.rt[:], cq, A.not_equal, ["rt", "cf"], ["kp"], BIG, A.mult)
+    ts(c4, c2, 11.0, A.is_equal, ["c2"], ["c4"], JUMP, A.mult)
+    ts(c5, c2, 47.0, A.is_equal, ["c2"], ["c5"], DROP, A.mult)
+    ts(c3, c2, 10.0, A.is_le, ["c2"], ["c3"], STEP, A.mult)
+    tt(c0, c4, c5, A.add, ["c4", "c5"], ["c0"])
+    quant("qu", "su", 0, 128, T.ut[:], ["ut"], ["qu"])
+    tt(T.ca[:, 0:48], c0, c3, A.add, ["c0", "c3"], ["ca"])
+    pick_u(0, 256)
+    tt(T.cb[:, 0:48], c0, c3, A.subtract, ["c0", "c3"], ["cb"])
+    for a, b in ((48, 96), (96, 192), (192, 294)):
+        for n in ("ca", "cb"):
+            act(T[n][:, a:b], T[n][:, 0:b - a], F.Copy, [n], [n])
+
+    wait("s", last["xt0"])
+    op("s", lambda: g.sync.dma_start(T.qw[:].bitcast(dt.uint8), T.wc[:]), [], [], sem="lw")
+    op("s", lambda: g.sync.dma_start(T.sw[:], T.ws[:]), [], ["qw"], sem="lw")
+    op("s", lambda: g.sync.dma_start(T.vt[:], T.v[:]), [], ["vt"], sem="lv")
+
+    def slot(t):
+        w, e = (t + 1) // 4, (t + 1) % 4
+        a = 16 * (t + 1)
+        return a, "g%d.%d" % (w, e), T["gt%d" % w][:, 4 * (a - G0[w]) + e:4 * (C - G0[w]):4]
+
+    def sjc(t):
+        return T.sj[:, 16 * t + 15:16 * t + 16]
+
+    def sign(t):
+        a = 16 * (t + 1)
+        act(T.sg[:, C * t + a:C * t + C], T.p1[:, a:C], F.Sign, ["P1", "sj"], ["sgn%d" % t], scale=-1.0, bias=sjc(t))
+
+    def relu(t):
+        a, name, view = slot(t)
+        act(view, T.sg[:, C * t + a:C * t + C], F.Relu, ["sgn%d" % t], [name, "rs%d" % t], scale=-1.0, accum_out=T.rs[:, t:t + 1])
+
+    def row(t):
+        a, name, view = slot(t)
+        ts(view, T.p0[:, a:C], sjc(t), A.is_gt, ["P0", "sj"], [name])
+        act(T.jk[:, C * t + a:C * t + C], view, F.Identity, [name], ["rs%d" % t], accum_out=T.rs[:, t:t + 1])
+
+    def colsum(w, start, stop):
+        quant("qg%d" % w, "sg%d" % w, G0[w], C, T["gt%d" % w][:], ["g%d.%d" % (w, e) for e in range(4)], ["qg%d" % w])
+        mm(2, "qk", "sk", 0, "qg%d" % w, "sg%d" % w, C, ["qk", "qg%d" % w], start, stop)
+
+    for r in range(R):
+        quant("qx", "sx", 0, C, T.xt[:], XT, ["qx"])
+        mm(0, "qp", "sp", U0, "qx", "sx", C, UA + ["qx"])
+        mm(3, "qp", "sp", UC, "qx", "sx", C, UA + ["qx"])
+        mm(1, "qp", "sp", U0, "qx", "sx", C, UA + ["qx"])
+        if r == 0:
+            for b in range(4):
+                quant("qe", "se", 128 * b, 128 * b + 128, T.et[:, 3 - b:515 - b], ["et"], ["qe%d" % b])
+        for b in range(4):
+            mm(4 + b, "qe", "se", 128 * b, "qx", "sx", C, ["qe%d" % b, "qx"])
+        act(T.m1[:], T.p3[:, 0:C], F.Sign, ["P3", "sig"], ["m1"], scale=sig)
+        act(T.m2[:], T.m1[:], F.Relu, ["m1", "mb"], ["m2"], scale=2 * JUMP, bias=mb)
+        tt(T.d1[:], T.p0[:, 0:C], T.kp[:], A.add, ["P0", "kp"], ["d1"])
+        scan(T.sj[:], T.k2[:], T.d1[:], A.add, A.min, ["k2", "d1"], ["sj"])
+        for k, t in enumerate(ON_ACT):
+            sign(t)
+            if k:
+                relu(ON_ACT[k - 1])
+        relu(ON_ACT[-1])
+        dg = T.gt0[:, 0:4 * C:4]
+        tt(dg, T.p0[:, 0:C], T.sj[:], A.is_gt, ["P0", "sj"], ["g0.0"])
+        for t in range(0, 7):
+            if t not in ON_ACT:
+                row(t)
+        if r == 0:
+            quant("qk", "sk", 0, 128, T.bk[:], ["bk"], ["qk"])
+            ts(T.jq[:], T.jc[:], 240.0, A.min, ["jc", "cf"], ["jq"], cq, A.add)
+        scan(T.rd[:], T.k16[:, 0:C], dg, A.mult, A.add, ["k16", "g0.0"], ["rd"])
+        colsum(1, True, False)
+        for t in range(7, 11):
+            row(t)
+        tt(T.rdj[:], T.rd[:, 15:C:16], T.jq[:], A.add, ["rd", "jq"], ["rdj"])
+        colsum(2, False, False)
+        for t in range(11, 15):
+            row(t)
+        colsum(0, False, False)
+        ts(T.spc[:, 0:32], T.p0[:, 256:288], sjc(15), A.is_gt, ["P0", "sj"], ["spc0"])
+        colsum(3, False, True)
+        ts(T.spc[:, 32:48], T.p0[:, 240:256], sjc(16), A.is_ge, ["P0", "sj"], ["spc1"])
+        ts(T.spc[:, 48:64], T.p0[:, 272:288], sjc(16), A.is_gt, ["P0", "sj"], ["spc1b"])
+        ts(T.spc[:, 64:96], T.p0[:, 240:272], sjc(17), A.is_ge, ["P0", "sj"], ["spc2"])
+        for k in range(3):
+            act(T.jk[:, C * (15 + k):C * (15 + k) + 32], T.spc[:, 32 * k:32 * k + 32], F.Identity,
+                ["spc%d" % k] + (["spc1b"] if k == 1 else []), ["rs%d" % (15 + k)], accum_out=T.rs[:, 15 + k:16 + k])
+        for b in range(4):
+            act(T.f4[:, FS * b + 1:FS * b + 1 + C], T["p%d" % (4 + b)][:, 0:C], F.Copy, ["P%d" % (4 + b)], ["f4%d" % b], scale=0.25)
+        tt(T.x1[:], T.p2[:, 0:C], T.kp[:], A.add, ["P2", "kp"], ["x1"])
+        scan(T.cs[:], T.k2[:], T.x1[:], A.add, A.min, ["k2", "x1"], ["cs"])
+        tt(T.val[:], T.m2[:], T.jt[:], A.min, ["m2", "jt"], ["val"])
+        tt(T.pre[:], T.rs[:], T.rdj[:], A.add, ["rs%d" % t for t in range(NT)] + ["rdj"], ["pre"])
+        tt(T.pl[:], T.pre[:], T.cs[:, 15:C:16], A.subtract, ["pre", "cs"], ["pl"])
+        cp(T.pl16[:], T.pl[:], ["pl"], ["pl16"])
+        act(T.ab[:, 0:NT], T.pl[:], F.Identity, ["pl"], ["ab0"], scale=1.0 / 12, bias=-5.5 / 12)
+        act(T.ab[:, NT:], T.pl[:], F.Identity, ["pl"], ["ab1"], scale=1.0 / 12, bias=-11.5 / 12)
+        act(T.ar[:], T.ab[:], F.Identity, ["ab0", "ab1"], ["ar"], bias=WHOLE)
+        act(T.b3[:], T.ar[:, NT:], F.Identity, ["ar"], ["b3"], bias=-WHOLE)
+        act(T.b4[:, 0:NT], T.ar[:, 0:NT], F.Identity, ["ar"], ["b40"], scale=4.0, bias=-4 * WHOLE)
+        act(T.b5[:], T.b3[:], F.Identity, ["b3"], ["b5"], scale=4.0, bias=2.0)
+        act(T.zz[:], T.b3[:], F.Relu, ["b3"], ["zz"], scale=-float(M))
+        cp(T.srt[:, 0:C].indirect(T.pl16[:]), T.val[:], ["pl16", "val"], ["srt"])
+        cp(T.srt[:, C:C + 6], T.srt[:, 0:6], ["srt"], ["srt6"])
+        scan(T.so[:, 0:294], T.srt[:, 0:294], T.ca[:, 0:294], A.max, A.add, ["srt", "srt6", "ca"], ["so0"])
+        scan(T.so[:, 384:678], T.srt[:, 0:294], T.cb[:, 0:294], A.max, A.add, ["srt", "srt6", "cb"], ["so1"])
+        tt(T.ni[:], T.so[:, 41:678:48], T.so[:, 53:678:48], A.max, ["so0", "so1", "soz"], ["ni"])
+        ts(T.nj[:], T.ni[:], int(STEP) - 1, A.bitwise_and, ["ni"], ["nj"])
+        cp(T.nl16[:], T.nj[:], ["nj"], ["nl16"])
+        for b in range(4):
+            win = T.f4[:, FS * b:FS * b + 1 + C]
+            act(T.ga[:, M * b:M * b + M], win.indirect(T.nl16[:, 0:6]), F.Copy, ["f4%d" % b, "f4z", "nl16"], ["ga%d" % b])
+            tt(T.zh[:, b:4 * M:4], win.indirect(T.nl16[:, 8:14]), T.ga[:, M * b:M * b + M], A.add,
+               ["f4%d" % b, "f4z", "nl16", "ga%d" % b], ["zh%d" % b])
+        ZH = ["zh%d" % b for b in range(4)]
+        tt(T.yt[:, 0:4 * M - 8], T.zh[:, 0:4 * M - 8], T.zh[:, 8:4 * M], A.add, ZH, ["yt0"])
+        tt(T.yt[:, 4 * M - 8:4 * M], T.zh[:, 4 * M - 8:4 * M], T.zh[:, 0:8], A.add, ZH, ["yt1"])
+        quant("qy", "sy", 0, 128, T.yt[:], ["yt0", "yt1", "ytz"], ["qy"])
+        wait("g", last["qy"])
+        lc, ls, arr = "lc%d" % r, "ls%d" % r, "arr%d" % r
+        g.remote_dma(T[lc][:, 0:M].bitcast(dt.uint8), T.qy[:, 0:M].bitcast(dt.uint8), T.sem[arr], T.sem.sent, pid, rid, mask)
+        g.remote_dma(T[ls][:, 0:M], T.sy[:, 0:M], T.sem[arr], T.sem.sent, pid, rid, mask)
+        count["sent"] = 2 * ne * (r + 1)
+        snap[("sent", count["sent"])] = {"sent": count["sent"]}
+        readers["qy"] = {"sent": count["sent"]}
+        snap[(arr, 2 * ne)] = {arr: 2 * ne}
+        last["land%d" % r] = (arr, 2 * ne)
+        if r == 0:
+            pick_u(256, 512)
+        for b in range(2):
+            act(T.fs[:, C * b:C * b + C], T["p%d" % (4 + b)][:, 0:C], F.Copy, ["P%d" % (4 + b)], ["fs%d" % b])
+        mm(0, "qp", "sp", U1, "qx", "sx", C, UB + ["qx"])
+        mm(1, "qp", "sp", U2, "qx", "sx", C, UB + ["qx"])
+        quant(lc, ls, M, M + 128, T.zt[:, 0:512], ["zt"], ["pad%d" % r])
+        tt(T.b4[:, NT:], T.b5[:], T.zz[:], A.add, ["b5", "zz"], ["b41"])
+        tt(T.col[:, 0:C], T.p0[:, 0:C], T.kp[:], A.is_gt, ["P0", "kp"], ["col0"])
+        tt(T.col[:, C:], T.p1[:, 0:C], T.kp[:], A.is_gt, ["P1", "kp"], ["col1"])
+        scan(T.co[:], T.k16[:], T.col[:], A.mult, A.add, ["k16", "k16b", "col0", "col1"], ["co"])
+        tt(T.nn[:], T.b4[:], T.co[:, 15:2 * C:16], A.add, ["b40", "b41", "co"], ["nn"])
+        if r == 1:
+            quant("qv", "sv", 0, 128, T.vt[:], ["vt"], ["qv"])
+        tt(T.lh[:, 0:NT], T.nn[:, 0:NT], T.nn[:, NT:], A.min, ["nn"], ["lo"])
+        tt(T.lh[:, NT:], T.nn[:, 0:NT], T.nn[:, NT:], A.max, ["nn"], ["hi"])
+        tt(T.wl[:, 31:2 * C:32], T.nn[:, 0:NT], T.nn[:, NT:], A.min, ["nn"], ["wll"])
+        cp(T.lh16[:], T.lh[:], ["lo", "hi"], ["lh16"])
+        tt(T.kc[:, 31:2 * C:32], T.lh[:, NT:], T.lh[:, 0:NT], A.subtract, ["lo", "hi", "kc"], ["kcd"])
+        for b in range(4):
+            mm(2 + b, "qw", "sw", 128 * b, lc, ls, 128, ["qw", "land%d" % r, "pad%d" % r])
+            src, dst = T["p%d" % (2 + b)][:, 0:M], T.ht[:, b:4 * M:4]
+            if b % 2 == 0:
+                act(dst, src, F.Copy, ["P%d" % (2 + b)], ["ht%d" % b], scale=0.03125)
+            else:
+                ts(dst, src, 0.03125, A.mult, ["P%d" % (2 + b)], ["ht%d" % b])
+        quant("qh", "sh", 0, 128, T.ht[:], ["ht0", "ht1", "ht2", "ht3", "htz"], ["qh"])
+        mm(0, "qp", "sp", U0, "qh", "sh", 128, UA + ["qh"])
+        for b in range(4):
+            act(T.hp[:, M * b:M * b + M], T.ht[:, b:4 * M:4], F.Copy, ["ht%d" % b], ["hp%d" % b])
+        cp(T.vs[:], T.p0[:, 0:M], ["P0"], ["vs"])
+        tt(T.g1[:], T.vs[:].indirect(T.lh16[:, 0:NT]), T.kp[:], A.add, ["vs", "lh16", "kp"], ["g1"])
+        tt(T.wl[:, 0:2 * C:2], T.vs[:].indirect(T.lh16[:, NT:]), T.g1[:], A.is_gt, ["vs", "lh16", "g1"], ["wlw"])
+        scan(T.ns[:], T.kc[:], T.wl[:], A.mult, A.add, ["kc", "kcd", "wlw", "wll"], ["ns"])
+        cp(T.n16[:], T.ns[:, 31:2 * C:32], ["ns"], ["n16"])
+        for b in (2, 3):
+            act(T.hg[:, C * (b - 2):C * (b - 1)], T.hp[:, M * b:M * b + M].indirect(T.n16[:]), F.Copy, ["hp%d" % b, "n16"], ["hg%d" % b])
+        for b in (0, 1):
+            tt(T.xt[:, b:4 * C:4], T.hp[:, M * b:M * b + M].indirect(T.n16[:]), T.fs[:, C * b:C * b + C], A.add,
+               ["hp%d" % b, "n16", "fs%d" % b], [XT[b]])
+        for b in (2, 3):
+            tt(T.xt[:, b:4 * C:4], T["p%d" % (4 + b)][:, 0:C], T.hg[:, C * (b - 2):C * (b - 1)], A.add,
+               ["P%d" % (4 + b), "hg%d" % b], [XT[b]])
+
+    act(T.ndu[:], T.nt[:].indirect(T.n16[:]), F.Copy, ["nt", "n16"], ["ndu"])
+    op("s", lambda: g.sync.dma_start(T.nd[:], T.ndu[0:128:16, :]), ["ndu"], [], sem="outs")
+    quant("qx", "sx", 0, C, T.xt[:], XT, ["qx"])
+    mm(1, "qv", "sv", 0, "qx", "sx", C, ["qv", "qx"])
+    op("s", lambda: g.sync.dma_start(T.oc[:], T.qx[:].bitcast(dt.uint8)), ["qx"], [], sem="outs")
+    for k in range(4):
+        op("a", lambda: S.dma_start(T.osc[4 * k:4 * k + 4, :], T.sx[32 * k:32 * k + 4, :]), ["qx"], [], sem="outs")
+    cp(T.ys[:], T.p1[:, 0:C], ["P1"], ["ys"])
+    op("s", lambda: g.sync.dma_start(T.y[:], T.ys[:]), ["ys"], [], sem="outs")
+    for s in ("g", "sent", "t", "a", "v", "outs"):
+        wait("s", (s, count[s]))

@@ -2,13 +2,19 @@ from concourse.mybir import dt, AluOpType, ActivationFunctionType
 
 C, M, R = 288, 96, 3
 NT = C // 16
+CA, CB = 160, 192
 BIG = 1.0e29
-FS = 304
-STEP, JUMP, DROP = 512.0, 32768.0, -1048576.0
-MEMBER = 32 * 512 + 1
+TINY = 1.0e-36
+FS, FZ, FO = 592, 289, 224
+STEP, JUMP, DROP = 1024.0, 65536.0, -1048576.0
+MARK = 16 * 1024 + FO + FZ
+LIFT = 16384.0
 WHOLE = 12582912.0
-G0 = (0, 64, 128, 160)
-ON_ACT = (0, 1, 2)
+GW = (288, 224, 160, 128)
+ON_ACT = (17, 16, 15, 14, 13)
+SUM_V = (12, 11, 10, 9, 8)
+GV = 6
+RL = 192
 
 F8, U8, BF, F32, I32, U16 = "float8_e4m3fn_x4", "uint8", "bfloat16", "float32", "int32", "uint16"
 SCRATCH = {}
@@ -23,13 +29,14 @@ for _n, _w, _t in (
         ("qu", 128, F8), ("su", 128, U8), ("qp", 512, F8), ("sp", 512, U8), ("qv", 128, F8), ("sv", 128, U8),
         ("qw", 512, F8), ("sw", 512, U8), ("qe", 512, F8), ("se", 512, U8), ("qk", 128, F8), ("sk", 128, U8),
         ("qy", 128, F8), ("sy", 128, U8), ("qh", 128, F8), ("sh", 128, U8),
-        ("zt", 640, BF), ("et", 516, BF), ("bk", 512, BF),
+        ("zt", 640, BF), ("et", 516, BF), ("bk", 512, BF), ("wt", 512, BF), ("on", RL, BF),
         ("pi", 8, I32), ("ii", 8, I32), ("cf", 16, F32), ("ul", 24, F32), ("ul16", 32, U16),
-        ("rt", C, BF), ("kp", C, BF), ("k2", C, BF), ("k16", 2 * C, BF), ("p48", 48, F32), ("c48", 48 * 6, F32),
+        ("rt", C, BF), ("kp", C, BF), ("k2", C, BF), ("k16", 2 * C, BF), ("cw", C, BF), ("cx", 2 * C, BF),
+        ("p48", 48, F32), ("c48", 48 * 6, F32),
         ("ca", 296, F32), ("cb", 296, F32), ("jt", C, F32), ("jc", NT, F32), ("jq", NT, F32), ("nt", M, F32),
-        ("d1", C, F32), ("sj", C, F32), ("sg", 4 * C, BF), ("jk", NT * C, BF), ("spc", 96, BF), ("rs", NT, F32), ("rd", C, BF),
-        ("rdj", NT, F32), ("pre", NT, F32), ("x1", C, BF), ("cs", C, BF), ("pl", NT, F32), ("pl16", NT, U16),
-        ("m1", C, BF), ("m2", C, F32), ("val", C, F32), ("srt", 296, F32), ("so", 768, F32),
+        ("d1", C, F32), ("sj", C, F32), ("sg", 6 * C, BF), ("jk", 128 * NT, BF), ("spc", 96, BF), ("rs", NT, F32), ("rd", C, BF),
+        ("rl", 32 * RL, BF), ("rdj", NT, F32), ("pre", 2 * NT, F32), ("cs", C, F32), ("pl", NT, F32), ("pl16", NT, U16),
+        ("m1", C, BF), ("val", C, F32), ("srt", 296, F32), ("so", 768, F32),
         ("ni", 14, I32), ("nj", 14, I32), ("nl16", 14, U16), ("f4", 4 * FS, BF), ("fs", 2 * C, BF),
         ("ga", 4 * M, BF), ("zh", 4 * M, BF), ("yt", 512, BF), ("ht", 512, BF), ("hp", 4 * M, BF), ("hg", 2 * C, BF),
         ("col", 2 * C, BF), ("co", 2 * C, BF), ("ab", 2 * NT, F32), ("ar", 2 * NT, F32), ("b4", 2 * NT, F32),
@@ -38,16 +45,16 @@ for _n, _w, _t in (
         ("ndu", C, F32), ("ys", C, F32)):
     _buf(_n, _w, _t)
 for _w in range(4):
-    _buf("gt%d" % _w, 4 * (C - G0[_w]), BF)
-    _buf("qg%d" % _w, C, F8)
-    _buf("sg%d" % _w, C, U8)
+    _buf("gt%d" % _w, 4 * GW[_w], BF)
+    _buf("qg%d" % _w, GW[_w], F8)
+    _buf("sg%d" % _w, GW[_w], U8)
 for _r in range(R):
     _buf("lc%d" % _r, M + 128, F8)
     _buf("ls%d" % _r, M + 128, U8)
 for _b in range(8):
     _buf("p%d" % _b, 512, F32, "psum")
 
-SEMAPHORES = ["v", "a", "t", "g", "lx", "lu", "lw", "lv", "sent", "outs"] + ["arr%d" % r for r in range(R)]
+SEMAPHORES = ["v", "a", "t", "g", "lxa", "lxb", "lu", "lw", "lv", "sent", "outs"] + ["arr%d" % r for r in range(R)]
 
 
 def rank_program(g, core, T, topo):
@@ -112,8 +119,11 @@ def rank_program(g, core, T, topo):
     def cp(out, a, rd, wr):
         op("v", lambda: V.tensor_copy(out, a), rd, wr)
 
-    def scan(out, a, b, o0, o1, rd, wr):
-        op("v", lambda: V.tensor_tensor_scan(out, a, b, 0.0, o0, o1), rd, wr)
+    def fill(out, x, wr):
+        op("v", lambda: V.memset(out, x), [], wr)
+
+    def scan(out, a, b, o0, o1, rd, wr, first=0.0):
+        op("v", lambda: V.tensor_tensor_scan(out, a, b, first, o0, o1), rd, wr)
 
     def quant(q, s, a, b, src, rd, wr):
         op("v", lambda: V.quantize_mx(T[q][:, a:b], T[s][:, a:b], src), rd, wr)
@@ -121,9 +131,9 @@ def rank_program(g, core, T, topo):
     def act(out, a, f, rd, wr, **kw):
         op("a", lambda: S.activation(out, a, f, **kw), rd, wr)
 
-    def mm(bank, wq, ws, a, xq, xs, n, rd, start=True, stop=True):
-        op("t", lambda: P.matmul_mx(T["p%d" % bank][:, 0:n], T[wq][:, a:a + 128], T[ws][:, a:a + 128],
-                                    T[xq][:, 0:n], T[xs][:, 0:n], start, stop), rd, ["P%d" % bank])
+    def mm(bank, wq, ws, a, xq, xs, c0, c1, rd, start=True, stop=True):
+        op("t", lambda: P.matmul_mx(T["p%d" % bank][:, 0:c1 - c0], T[wq][:, a:a + 128], T[ws][:, a:a + 128],
+                                    T[xq][:, c0:c1], T[xs][:, c0:c1], start, stop), rd, ["P%d" % bank])
 
     def iota(out, pat, base, mult, wr, small=True):
         if small:
@@ -143,174 +153,203 @@ def rank_program(g, core, T, topo):
         act(T.sp[:, a:b], T.su[:, 0:128].indirect(off), F.Copy, ["qu", "ula", "ulb"], ["sp%d" % a])
 
     XT = ["xt0", "xt1", "xt2", "xt3"]
-    UC, U0, U1, U2 = 0, 128, 256, 384
-    UA, UB = ["qp0", "sp0"], ["qp256", "sp256"]
+    U0, UC, U1, U2 = 0, 128, 256, 384
+    UA, UB, UD = ["qp0", "sp0"], ["qp128", "sp128"], ["qp256", "sp256"]
+    QX = ["qxa", "qxb"]
 
-    op("s", lambda: g.sync.dma_start(T.xt[:], T.x[:]), [], XT, sem="lx")
     op("a", lambda: S.dma_start(T.ut[:], T.u[:]), [], ["ut"], sem="lu")
+    op("s", lambda: g.sync.dma_start(T.xt[:, 4 * CA:], T.x[:, 4 * CA:]), [], ["xa"], sem="lxa")
+    op("s", lambda: g.sync.dma_start(T.xt[:, 0:4 * CA], T.x[:, 0:4 * CA]), [], ["xb"], sem="lxb")
 
-    op("v", lambda: V.memset(T.zt[:], 0.0), [], ["zt"])
+    fill(T.zt[:], 0.0, ["zt"])
     iota(T.pi[:, 0:1], [[0, 1]], 0, 1, ["pi"], small=False)
     iota(T.ul[:], [[1, 3], [16, 8]], 0, 0, ["ul"])
-    iota(T.p48[:], [[1, 48]], 48, 0, ["p48"])
     iota(T.rt[:], [[0, NT], [1, 16]], 0, 0, ["rt"])
+    iota(T.p48[:], [[1, 48]], 48, 0, ["p48"])
     select(T.et[:], T.zt[:, 0:516], [[-1, 516]], A.not_equal, 1.0, 3, 4, ["zt"], ["et"])
-    select(T.bk[:], T.zt[:, 0:512], [[16, 8], [0, 64]], A.is_gt, 1.0, 0, -1, ["zt"], ["bk"])
+    fill(T.wt[:], 1.0 / LIFT, ["wt"])
+    for e in range(4):
+        op("v", lambda: V.memset(T.wt[:, 60 + e:512:64], 1.0), ["wt"], ["wt%d" % e])
+    select(T.bk[:], T.wt[:], [[-16, 8], [0, 64]], A.is_ge, 0.0, 0, 1, ["wt%d" % e for e in range(4)], ["bk"])
     select(T.bk[:], T.bk[:], [[16, 8], [0, 64]], A.is_ge, 0.0, 15, -1, ["bk"], ["bk"])
-    iota(T.jc[:], [[16, NT]], 0, 0, ["jc"])
-    iota(T.jt[:], [[1, C]], MEMBER, 0, ["jt"])
-    iota(T.f4[:, 0:4 * FS:FS], [[0, 4]], 0, 0, ["f4z"])
-    iota(T.so[:, 294:384], [[0, 90]], 0, 0, ["soz"])
-    iota(T.yt[:, 4 * M:512], [[0, 128]], 0, 0, ["ytz"])
-    iota(T.ht[:, 4 * M:512], [[0, 128]], 0, 0, ["htz"])
-    iota(T.wl[:], [[0, 2 * C]], 0, 0, ["wlw", "wll"])
-    select(T.kc[:], T.zt[:, 0:2 * C], [[0, NT], [1, 32]], A.is_equal, 1.0, 0, 0, ["zt"], ["kc"])
-    select(T.k16[:, C:], T.zt[:, 0:C], [[0, NT], [1, 16]], A.is_equal, 1.0, 0, 0, ["zt"], ["k16b"])
+    iota(T.jc[:], [[16, NT]], 15, 0, ["jc"])
+    iota(T.jt[:], [[1, C]], MARK, 0, ["jt"])
     iota(T.nt[:], [[1, M]], 0, 0, ["nt"])
     p1 = T.pi[:, 0:1]
     ts(T.ii[:, 0:1], p1, 15, A.bitwise_and, ["pi"], ["i0"])
     ts(T.ii[:, 1:2], p1, 1, A.arith_shift_right, ["pi"], ["i1"], 7, A.bitwise_and)
     ts(T.ii[:, 2:3], p1, 1, A.bitwise_and, ["pi"], ["i2"])
     ts(T.ii[:, 3:4], p1, 1, A.arith_shift_right, ["pi"], ["i3"], 1, A.bitwise_and)
-    quant("qg1", "sg1", 0, 128, T.zt[:, 0:512], ["zt"], ["qg1"])
+    fill(T.k2[:], 0.0, ["k2"])
     cp(T.cf[:, 0:4], T.ii[:, 0:4], ["i0", "i1", "i2", "i3"], ["cf"])
     cq, ch, cc, cpar = [T.cf[:, k:k + 1] for k in range(4)]
-    h6, sig, mb = T.cf[:, 5:6], T.cf[:, 6:7], T.cf[:, 7:8]
-    cp(T.ul16[:, 8:32], T.ul[:], ["ul"], ["ula"])
+    cq1, h6, sig, mb, low = [T.cf[:, k:k + 1] for k in range(4, 9)]
+    cp(T.ul16[:, 0:8], T.ul[:, 0:8], ["ul"], ["ula"])
+    cp(T.ul16[:, 16:32], T.ul[:, 8:24], ["ul"], ["ula"])
+    fill(T.k2[:, 0:C:16], -4 * BIG, ["k2"])
+    ts(T.ul16[:, 8:16], T.ul[:, 8:16], cpar, A.add, ["ul", "cf"], ["ulb"])
     ts(h6, ch, 6.0, A.mult, ["cf"], ["h6"])
-    ts(T.ul16[:, 0:8], T.ul[:, 8:16], cpar, A.add, ["ul", "cf"], ["ulb"])
+    ts(cq1, cq, 1.0, A.add, ["cf"], ["cq1"])
+    ts(T.kp[:], T.rt[:], cq, A.not_equal, ["rt", "cf"], ["kp"], BIG, A.mult)
+    fill(T.k16[:], 1.0, ["k16"])
+    fill(T.on[:], 1.0, ["on"])
+    fill(T.rs[:], 0.0, ["rs%d" % t for t in range(NT)])
+    fill(T.k16[:, 0:2 * C:16], 0.0, ["k16"])
 
     for w in range(4):
         n = 320 if w == 3 else 192
-        act(T["gt%d" % w][:, 0:n], T.zt[:, 0:n], F.Copy, ["zt"], ["g%d.%d" % (w, e) for e in range(4)])
+        act(T["gt%d" % w][:, 4 * GW[w] - n:], T.zt[:, 0:n], F.Copy, ["zt"], ["g%d.%d" % (w, e) for e in range(4)])
     act(sig, cc, F.Identity, ["cf"], ["sig"], scale=2.0, bias=-1.0)
-    act(mb, cc, F.Identity, ["cf"], ["mb"], scale=-2 * JUMP, bias=JUMP)
-    act(T.k16[:, 0:C], T.rt[:], F.Sign, ["rt"], ["k16"])
-    act(T.k2[:], T.k16[:, 0:C], F.Identity, ["k16"], ["k2"], scale=-4 * BIG, bias=4 * BIG)
+    act(mb, cc, F.Identity, ["cf"], ["mb"], scale=-2 * TINY, bias=TINY)
+    act(T.rl[:, 32 * (RL - 1):], T.zt[:, 0:32], F.Copy, ["zt"], ["rl%d" % t for t in SUM_V])
+    act(T.so[:, 294:384], T.zt[:, 0:90], F.Copy, ["zt"], ["soz"])
+    act(T.yt[:, 4 * M:512], T.zt[:, 0:128], F.Copy, ["zt"], ["ytz"])
+    act(T.ht[:, 4 * M:512], T.zt[:, 0:128], F.Copy, ["zt"], ["htz"])
+    for b in range(4):
+        act(T.f4[:, FS * b:FS * b + FZ], T.zt[:, 0:FZ], F.Copy, ["zt"], ["f4z%d" % b])
 
     c0, c1, c2, c3, c4, c5 = [T.c48[:, 48 * k:48 * k + 48] for k in range(6)]
     ts(c0, T.p48[:], h6, A.subtract, ["p48", "h6"], ["c0"])
-    quant("qg2", "sg2", 0, 128, T.zt[:, 0:512], ["zt"], ["qg2"])
+    ts(T.cx[:, 0:C], T.rt[:], cq, A.not_equal, ["rt", "cf"], ["cxa"])
     ts(c1, c0, 48.0, A.is_ge, ["c0"], ["c1"], -48.0, A.mult)
-    quant("qg3", "sg3", 0, 160, T.zt[:, 0:640], ["zt"], ["qg3"])
+    ts(T.cx[:, C:], T.rt[:], cq1, A.is_equal, ["rt", "cq1"], ["cxb"], LIFT, A.mult)
     tt(c2, c0, c1, A.add, ["c0", "c1"], ["c2"])
-    ts(T.kp[:], T.rt[:], cq, A.not_equal, ["rt", "cf"], ["kp"], BIG, A.mult)
+    tt(T.cw[:], T.cx[:, 0:C], T.cx[:, C:], A.max, ["cxa", "cxb"], ["cw"])
     ts(c4, c2, 11.0, A.is_equal, ["c2"], ["c4"], JUMP, A.mult)
     ts(c5, c2, 47.0, A.is_equal, ["c2"], ["c5"], DROP, A.mult)
     ts(c3, c2, 10.0, A.is_le, ["c2"], ["c3"], STEP, A.mult)
-    tt(c0, c4, c5, A.add, ["c4", "c5"], ["c0"])
     quant("qu", "su", 0, 128, T.ut[:], ["ut"], ["qu"])
+    tt(c0, c4, c5, A.add, ["c4", "c5"], ["c0"])
+    pick_u(0, 128)
     tt(T.ca[:, 0:48], c0, c3, A.add, ["c0", "c3"], ["ca"])
-    pick_u(0, 256)
     tt(T.cb[:, 0:48], c0, c3, A.subtract, ["c0", "c3"], ["cb"])
+    pick_u(128, 256)
     for a, b in ((48, 96), (96, 192), (192, 294)):
         for n in ("ca", "cb"):
             act(T[n][:, a:b], T[n][:, 0:b - a], F.Copy, [n], [n])
 
-    wait("s", last["xt0"])
+    wait("s", last["xb"])
     op("s", lambda: g.sync.dma_start(T.qw[:].bitcast(dt.uint8), T.wc[:]), [], [], sem="lw")
     op("s", lambda: g.sync.dma_start(T.sw[:], T.ws[:]), [], ["qw"], sem="lw")
     op("s", lambda: g.sync.dma_start(T.vt[:], T.v[:]), [], ["vt"], sem="lv")
 
     def slot(t):
-        w, e = (t + 1) // 4, (t + 1) % 4
-        a = 16 * (t + 1)
-        return a, "g%d.%d" % (w, e), T["gt%d" % w][:, 4 * (a - G0[w]) + e:4 * (C - G0[w]):4]
+        w, e = (NT - t) // 4, (NT - t) % 4
+        return "g%d.%d" % (w, e), T["gt%d" % w][:, e:64 * t:4]
 
     def sjc(t):
-        return T.sj[:, 16 * t + 15:16 * t + 16]
+        return T.sj[:, 16 * t + 15:16 * t + 16], "sja" if 16 * t >= CB else "sjb"
 
     def sign(t):
-        a = 16 * (t + 1)
-        act(T.sg[:, C * t + a:C * t + C], T.p1[:, a:C], F.Sign, ["P1", "sj"], ["sgn%d" % t], scale=-1.0, bias=sjc(t))
+        s, n = sjc(t)
+        k = t % 6
+        act(T.sg[:, C * k:C * k + 16 * t], T.p1[:, 0:16 * t], F.Sign, ["P1", n], ["sgn%d" % k], scale=-1.0, bias=s)
 
     def relu(t):
-        a, name, view = slot(t)
-        act(view, T.sg[:, C * t + a:C * t + C], F.Relu, ["sgn%d" % t], [name, "rs%d" % t], scale=-1.0, accum_out=T.rs[:, t:t + 1])
+        name, view = slot(t)
+        k = t % 6
+        act(view, T.sg[:, C * k:C * k + 16 * t], F.Relu, ["sgn%d" % k], [name, "rs%d" % t], accum_out=T.rs[:, t:t + 1])
 
     def row(t):
-        a, name, view = slot(t)
-        ts(view, T.p0[:, a:C], sjc(t), A.is_gt, ["P0", "sj"], [name])
-        act(T.jk[:, C * t + a:C * t + C], view, F.Identity, [name], ["rs%d" % t], accum_out=T.rs[:, t:t + 1])
+        name, view = slot(t)
+        s, n = sjc(t)
+        ts(view, T.p0[:, 0:16 * t], s, A.is_lt, ["P0", n], [name])
+
+    def rowsum(t):
+        name, view = slot(t)
+        if t in SUM_V:
+            scan(T.rl[:, 32 * (RL - 16 * t) + t:32 * RL:32], T.on[:, 0:16 * t], view, A.mult, A.add, ["on", name], ["rl%d" % t])
+        else:
+            act(T.jk[:, 128 * t:144 * t], view, F.Identity, [name], ["rs%d" % t, "jk%d" % t], accum_out=T.rs[:, t:t + 1])
+
+    def pack(w):
+        quant("qg%d" % w, "sg%d" % w, 0, GW[w], T["gt%d" % w][:], ["g%d.%d" % (w, e) for e in range(4)] + ["dga"] * (w == 0), ["qg%d" % w])
 
     def colsum(w, start, stop):
-        quant("qg%d" % w, "sg%d" % w, G0[w], C, T["gt%d" % w][:], ["g%d.%d" % (w, e) for e in range(4)], ["qg%d" % w])
-        mm(2, "qk", "sk", 0, "qg%d" % w, "sg%d" % w, C, ["qk", "qg%d" % w], start, stop)
+        mm(2, "qk", "sk", 0, "qg%d" % w, "sg%d" % w, 0, GW[w], ["qk", "qg%d" % w], start, stop)
+
+    def quant_x():
+        quant("qx", "sx", CA, C, T.xt[:, 4 * CA:], XT[:3] + ["xa"], ["qxa"])
+        quant("qx", "sx", 0, CA, T.xt[:, 0:4 * CA], XT[:3] + ["xb"], ["qxb"])
+
+    def marks(a, b):
+        tt(T.val[:, a:b], T.jt[:, a:b], T.m1[:, a:b], A.mult, ["m1", "jt"], ["val%d" % a])
 
     for r in range(R):
-        quant("qx", "sx", 0, C, T.xt[:], XT, ["qx"])
-        mm(0, "qp", "sp", U0, "qx", "sx", C, UA + ["qx"])
-        mm(3, "qp", "sp", UC, "qx", "sx", C, UA + ["qx"])
-        mm(1, "qp", "sp", U0, "qx", "sx", C, UA + ["qx"])
+        quant_x()
+        mm(4, "qp", "sp", U0, "qx", "sx", CA, C, UA + ["qxa"])
+        mm(0, "qp", "sp", U0, "qx", "sx", 0, CB, UA + QX)
+        mm(1, "qp", "sp", U0, "qx", "sx", 0, C - 16, UA + QX)
+        mm(3, "qp", "sp", UC, "qx", "sx", 0, C, UB + QX)
+        late = T.p4[:, CB - CA:C - CA]
+        tt(T.d1[:, CB:], late, T.kp[:, CB:], A.subtract, ["P4", "kp"], ["d1a"])
+        scan(T.sj[:, CB:], T.k2[:, CB:], T.d1[:, CB:], A.add, A.max, ["k2", "d1a"], ["sja"])
+        tt(T.d1[:, 0:CB], T.p0[:, 0:CB], T.kp[:, 0:CB], A.subtract, ["P0", "kp"], ["d1b"])
+        tt(T.gt0[:, 4 * CB:4 * C:4], late, T.sj[:, CB:], A.is_le, ["P4", "sja"], ["dga"])
+        scan(T.sj[:, 0:CB], T.k2[:, 0:CB], T.d1[:, 0:CB], A.add, A.max, ["k2", "d1b"], ["sjb"])
         if r == 0:
             for b in range(4):
                 quant("qe", "se", 128 * b, 128 * b + 128, T.et[:, 3 - b:515 - b], ["et"], ["qe%d" % b])
-        for b in range(4):
-            mm(4 + b, "qe", "se", 128 * b, "qx", "sx", C, ["qe%d" % b, "qx"])
-        act(T.m1[:], T.p3[:, 0:C], F.Sign, ["P3", "sig"], ["m1"], scale=sig)
-        act(T.m2[:], T.m1[:], F.Relu, ["m1", "mb"], ["m2"], scale=2 * JUMP, bias=mb)
-        tt(T.d1[:], T.p0[:, 0:C], T.kp[:], A.add, ["P0", "kp"], ["d1"])
-        scan(T.sj[:], T.k2[:], T.d1[:], A.add, A.min, ["k2", "d1"], ["sj"])
+            quant("qk", "sk", 0, 128, T.bk[:], ["bk"], ["qk"])
+            ts(T.jq[:], T.jc[:], 47.0, A.max, ["jc", "cf"], ["jq"], cq, A.subtract)
+        for b in (1, 2, 3, 0):
+            mm(4 + b, "qe", "se", 128 * b, "qx", "sx", 0, C, ["qe%d" % b] + QX)
         for k, t in enumerate(ON_ACT):
             sign(t)
             if k:
                 relu(ON_ACT[k - 1])
         relu(ON_ACT[-1])
-        dg = T.gt0[:, 0:4 * C:4]
-        tt(dg, T.p0[:, 0:C], T.sj[:], A.is_gt, ["P0", "sj"], ["g0.0"])
-        for t in range(0, 7):
-            if t not in ON_ACT:
-                row(t)
-        if r == 0:
-            quant("qk", "sk", 0, 128, T.bk[:], ["bk"], ["qk"])
-            ts(T.jq[:], T.jc[:], 240.0, A.min, ["jc", "cf"], ["jq"], cq, A.add)
-        scan(T.rd[:], T.k16[:, 0:C], dg, A.mult, A.add, ["k16", "g0.0"], ["rd"])
-        colsum(1, True, False)
-        for t in range(7, 11):
+        act(T.m1[:], T.p3[:, 0:C], F.Sign, ["P3", "sig", "mb"], ["m1"], scale=sig, bias=mb)
+        tt(T.gt0[:, 0:4 * CB:4], T.p0[:, 0:CB], T.sj[:, 0:CB], A.is_le, ["P0", "sjb"], ["g0.0"])
+        for t in range(ON_ACT[-1] - 1, 2, -1):
             row(t)
-        tt(T.rdj[:], T.rd[:, 15:C:16], T.jq[:], A.add, ["rd", "jq"], ["rdj"])
-        colsum(2, False, False)
-        for t in range(11, 15):
-            row(t)
-        colsum(0, False, False)
-        ts(T.spc[:, 0:32], T.p0[:, 256:288], sjc(15), A.is_gt, ["P0", "sj"], ["spc0"])
-        colsum(3, False, True)
-        ts(T.spc[:, 32:48], T.p0[:, 240:256], sjc(16), A.is_ge, ["P0", "sj"], ["spc1"])
-        ts(T.spc[:, 48:64], T.p0[:, 272:288], sjc(16), A.is_gt, ["P0", "sj"], ["spc1b"])
-        ts(T.spc[:, 64:96], T.p0[:, 240:272], sjc(17), A.is_ge, ["P0", "sj"], ["spc2"])
+        ts(T.spc[:, 0:32], T.p0[:, 16:48], sjc(0)[0], A.is_le, ["P0", "sjb"], ["spc0"])
+        ts(T.spc[:, 32:48], T.p0[:, 0:16], sjc(1)[0], A.is_lt, ["P0", "sjb"], ["spc1"])
+        ts(T.spc[:, 48:64], T.p0[:, 32:48], sjc(1)[0], A.is_le, ["P0", "sjb"], ["spc1b"])
+        ts(T.spc[:, 64:96], T.p0[:, 0:32], sjc(2)[0], A.is_lt, ["P0", "sjb"], ["spc2"])
+        pack(0)
+        colsum(0, True, False)
+        for w in (2, 3, 1):
+            pack(w)
+            colsum(w, False, w == 1)
+        scan(T.rd[:], T.k16[:, 0:C], T.gt0[:, 0:4 * C:4], A.mult, A.add, ["k16", "g0.0", "dga"], ["rd"])
+        for t in range(ON_ACT[-1] - 1, 2, -1):
+            rowsum(t)
         for k in range(3):
-            act(T.jk[:, C * (15 + k):C * (15 + k) + 32], T.spc[:, 32 * k:32 * k + 32], F.Identity,
-                ["spc%d" % k] + (["spc1b"] if k == 1 else []), ["rs%d" % (15 + k)], accum_out=T.rs[:, 15 + k:16 + k])
-        for b in range(4):
-            act(T.f4[:, FS * b + 1:FS * b + 1 + C], T["p%d" % (4 + b)][:, 0:C], F.Copy, ["P%d" % (4 + b)], ["f4%d" % b], scale=0.25)
-        tt(T.x1[:], T.p2[:, 0:C], T.kp[:], A.add, ["P2", "kp"], ["x1"])
-        scan(T.cs[:], T.k2[:], T.x1[:], A.add, A.min, ["k2", "x1"], ["cs"])
-        tt(T.val[:], T.m2[:], T.jt[:], A.min, ["m2", "jt"], ["val"])
-        tt(T.pre[:], T.rs[:], T.rdj[:], A.add, ["rs%d" % t for t in range(NT)] + ["rdj"], ["pre"])
-        tt(T.pl[:], T.pre[:], T.cs[:, 15:C:16], A.subtract, ["pre", "cs"], ["pl"])
+            act(T.jk[:, 128 * k:128 * k + 32], T.spc[:, 32 * k:32 * k + 32], F.Identity,
+                ["spc%d" % k] + (["spc1b"] if k == 1 else []), ["rs%d" % k, "jk%d" % k], accum_out=T.rs[:, k:k + 1])
+        tt(T.rdj[:], T.jq[:], T.rd[:, 15:C:16], A.subtract, ["rd", "jq"], ["rdj"])
+        scan(T.cs[:], T.cw[:], T.p2[:, 0:C], A.mult, A.add, ["cw", "P2"], ["cs"])
+        tt(T.pre[:, 0:NT], T.rdj[:], T.rl[:, 32 * (RL - 1):32 * (RL - 1) + NT], A.subtract, ["rdj"] + ["rl%d" % t for t in SUM_V], ["pre0"])
+        marks(0, 96)
+        tt(T.pre[:, NT:], T.pre[:, 0:NT], T.rs[:], A.subtract, ["rs%d" % t for t in range(NT)] + ["pre0"], ["pre"])
+        marks(96, 192)
+        tt(T.pl[:], T.pre[:, NT:], T.cs[:, 15:C:16], A.add, ["pre", "cs"], ["pl"])
+        marks(192, C)
         cp(T.pl16[:], T.pl[:], ["pl"], ["pl16"])
-        act(T.ab[:, 0:NT], T.pl[:], F.Identity, ["pl"], ["ab0"], scale=1.0 / 12, bias=-5.5 / 12)
-        act(T.ab[:, NT:], T.pl[:], F.Identity, ["pl"], ["ab1"], scale=1.0 / 12, bias=-11.5 / 12)
-        act(T.ar[:], T.ab[:], F.Identity, ["ab0", "ab1"], ["ar"], bias=WHOLE)
-        act(T.b3[:], T.ar[:, NT:], F.Identity, ["ar"], ["b3"], bias=-WHOLE)
-        act(T.b4[:, 0:NT], T.ar[:, 0:NT], F.Identity, ["ar"], ["b40"], scale=4.0, bias=-4 * WHOLE)
-        act(T.b5[:], T.b3[:], F.Identity, ["b3"], ["b5"], scale=4.0, bias=2.0)
-        act(T.zz[:], T.b3[:], F.Relu, ["b3"], ["zz"], scale=-float(M))
-        cp(T.srt[:, 0:C].indirect(T.pl16[:]), T.val[:], ["pl16", "val"], ["srt"])
-        cp(T.srt[:, C:C + 6], T.srt[:, 0:6], ["srt"], ["srt6"])
-        scan(T.so[:, 0:294], T.srt[:, 0:294], T.ca[:, 0:294], A.max, A.add, ["srt", "srt6", "ca"], ["so0"])
-        scan(T.so[:, 384:678], T.srt[:, 0:294], T.cb[:, 0:294], A.max, A.add, ["srt", "srt6", "cb"], ["so1"])
-        tt(T.ni[:], T.so[:, 41:678:48], T.so[:, 53:678:48], A.max, ["so0", "so1", "soz"], ["ni"])
-        ts(T.nj[:], T.ni[:], int(STEP) - 1, A.bitwise_and, ["ni"], ["nj"])
-        cp(T.nl16[:], T.nj[:], ["nj"], ["nl16"])
+        cp(T.srt[:, 0:C].indirect(T.pl16[:]), T.val[:], ["pl16", "val0", "val96", "val192"], ["srt"])
         for b in range(4):
-            win = T.f4[:, FS * b:FS * b + 1 + C]
-            act(T.ga[:, M * b:M * b + M], win.indirect(T.nl16[:, 0:6]), F.Copy, ["f4%d" % b, "f4z", "nl16"], ["ga%d" % b])
-            tt(T.zh[:, b:4 * M:4], win.indirect(T.nl16[:, 8:14]), T.ga[:, M * b:M * b + M], A.add,
-               ["f4%d" % b, "f4z", "nl16", "ga%d" % b], ["zh%d" % b])
+            if b == 3:
+                act(T.srt[:, C:C + 6], T.srt[:, 0:6], F.Copy, ["srt"], ["srt6"])
+            act(T.f4[:, FS * b + FZ:FS * b + FZ + C], T["p%d" % (4 + b)][:, 0:C], F.Copy, ["P%d" % (4 + b)], ["f4%d" % b], scale=0.25)
+        scan(T.so[:, 0:C], T.srt[:, 0:C], T.ca[:, 0:C], A.max, A.add, ["srt", "ca"], ["so0"])
+        scan(T.so[:, 384:678], T.srt[:, 0:294], T.cb[:, 0:294], A.max, A.add, ["srt", "srt6", "cb"], ["so1"])
+        scan(T.so[:, C:294], T.srt[:, C:294], T.ca[:, C:294], A.max, A.add, ["srt6", "ca", "so0"], ["so2"], first=T.so[:, C - 1:C])
+        tt(T.ni[:], T.so[:, 41:678:48], T.so[:, 53:678:48], A.max, ["so0", "so1", "so2", "soz"], ["ni"])
+        ts(T.nj[:], T.ni[:], int(STEP) - 1, A.bitwise_and, ["ni"], ["nj"])
+        ts(T.nl16[:], T.nj[:], float(FO), A.subtract, ["nj"], ["nl16"])
+        for b in range(4):
+            win, first = T.f4[:, FS * b:FS * b + FZ + C], T.ga[:, M * b:M * b + M]
+            if b == 0:
+                cp(first, win.indirect(T.nl16[:, 0:6]), ["f40", "f4z0", "nl16"], ["ga0"])
+            else:
+                act(first, win.indirect(T.nl16[:, 0:6]), F.Copy, ["f4%d" % b, "f4z%d" % b, "nl16"], ["ga%d" % b])
+        for b in range(4):
+            tt(T.zh[:, b:4 * M:4], T.f4[:, FS * b:FS * b + FZ + C].indirect(T.nl16[:, 8:14]), T.ga[:, M * b:M * b + M], A.add,
+               ["f4%d" % b, "f4z%d" % b, "nl16", "ga%d" % b], ["zh%d" % b])
         ZH = ["zh%d" % b for b in range(4)]
-        tt(T.yt[:, 0:4 * M - 8], T.zh[:, 0:4 * M - 8], T.zh[:, 8:4 * M], A.add, ZH, ["yt0"])
         tt(T.yt[:, 4 * M - 8:4 * M], T.zh[:, 4 * M - 8:4 * M], T.zh[:, 0:8], A.add, ZH, ["yt1"])
+        tt(T.yt[:, 0:4 * M - 8], T.zh[:, 0:4 * M - 8], T.zh[:, 8:4 * M], A.add, ZH, ["yt0"])
         quant("qy", "sy", 0, 128, T.yt[:], ["yt0", "yt1", "ytz"], ["qy"])
         wait("g", last["qy"])
         lc, ls, arr = "lc%d" % r, "ls%d" % r, "arr%d" % r
@@ -323,56 +362,74 @@ def rank_program(g, core, T, topo):
         last["land%d" % r] = (arr, 2 * ne)
         if r == 0:
             pick_u(256, 512)
+            fill(T.wl[:], 0.0, ["wla", "wlb", "wll"])
+            cp(T.kc[:, 0:2 * C:2], T.cx[:, 0:C], ["cxa"], ["kc"])
+            ts(T.cx[:, C:], T.rt[:], cq, A.is_equal, ["rt", "cf", "cw"], ["cxb"], LIFT, A.mult)
+            ts(low, cq, 15.0, A.is_equal, ["cf"], ["low"], 1.0 / LIFT, A.max)
+            ts(T.kc[:, 1:2 * C:2], T.cx[:, C:], 1.0, A.max, ["cxb"], ["kco"])
+        mm(0, "qp", "sp", U1, "qx", "sx", 0, C, UD + QX)
+        mm(1, "qp", "sp", U2, "qx", "sx", 0, C, UD + QX)
+        act(T.ab[:, 0:NT], T.pl[:], F.Identity, ["pl"], ["ab0"], scale=1.0 / 12, bias=-5.5 / 12)
+        act(T.ab[:, NT:], T.pl[:], F.Identity, ["pl"], ["ab1"], scale=1.0 / 12, bias=-11.5 / 12)
+        act(T.ar[:], T.ab[:], F.Identity, ["ab0", "ab1"], ["ar"], bias=WHOLE)
+        act(T.b3[:], T.ar[:, NT:], F.Identity, ["ar"], ["b3"], bias=-WHOLE)
+        act(T.b4[:, 0:NT], T.ar[:, 0:NT], F.Identity, ["ar"], ["b40"], scale=4.0, bias=-4 * WHOLE)
+        act(T.b5[:], T.b3[:], F.Identity, ["b3"], ["b5"], scale=4.0, bias=2.0)
+        act(T.zz[:], T.b3[:], F.Relu, ["b3"], ["zz"], scale=-float(M))
         for b in range(2):
             act(T.fs[:, C * b:C * b + C], T["p%d" % (4 + b)][:, 0:C], F.Copy, ["P%d" % (4 + b)], ["fs%d" % b])
-        mm(0, "qp", "sp", U1, "qx", "sx", C, UB + ["qx"])
-        mm(1, "qp", "sp", U2, "qx", "sx", C, UB + ["qx"])
         quant(lc, ls, M, M + 128, T.zt[:, 0:512], ["zt"], ["pad%d" % r])
-        tt(T.b4[:, NT:], T.b5[:], T.zz[:], A.add, ["b5", "zz"], ["b41"])
         tt(T.col[:, 0:C], T.p0[:, 0:C], T.kp[:], A.is_gt, ["P0", "kp"], ["col0"])
         tt(T.col[:, C:], T.p1[:, 0:C], T.kp[:], A.is_gt, ["P1", "kp"], ["col1"])
-        scan(T.co[:], T.k16[:], T.col[:], A.mult, A.add, ["k16", "k16b", "col0", "col1"], ["co"])
-        tt(T.nn[:], T.b4[:], T.co[:, 15:2 * C:16], A.add, ["b40", "b41", "co"], ["nn"])
+        scan(T.co[:], T.k16[:], T.col[:], A.mult, A.add, ["k16", "col0", "col1"], ["co"])
+        tt(T.b4[:, NT:], T.b5[:], T.zz[:], A.add, ["b5", "zz"], ["b41"])
         if r == 1:
             quant("qv", "sv", 0, 128, T.vt[:], ["vt"], ["qv"])
+        tt(T.nn[:], T.b4[:], T.co[:, 15:2 * C:16], A.add, ["b40", "b41", "co"], ["nn"])
         tt(T.lh[:, 0:NT], T.nn[:, 0:NT], T.nn[:, NT:], A.min, ["nn"], ["lo"])
         tt(T.lh[:, NT:], T.nn[:, 0:NT], T.nn[:, NT:], A.max, ["nn"], ["hi"])
         tt(T.wl[:, 31:2 * C:32], T.nn[:, 0:NT], T.nn[:, NT:], A.min, ["nn"], ["wll"])
+        tt(T.zz[:], T.lh[:, NT:], T.lh[:, 0:NT], A.subtract, ["lo", "hi"], ["zz"])
         cp(T.lh16[:], T.lh[:], ["lo", "hi"], ["lh16"])
-        tt(T.kc[:, 31:2 * C:32], T.lh[:, NT:], T.lh[:, 0:NT], A.subtract, ["lo", "hi", "kc"], ["kcd"])
+        ts(T.kc[:, 31:2 * C:32], T.zz[:], low, A.mult, ["zz", "low", "kco"], ["kcd"])
         for b in range(4):
-            mm(2 + b, "qw", "sw", 128 * b, lc, ls, 128, ["qw", "land%d" % r, "pad%d" % r])
+            mm(2 + b, "qw", "sw", 128 * b, lc, ls, 0, 128, ["qw", "land%d" % r, "pad%d" % r])
             src, dst = T["p%d" % (2 + b)][:, 0:M], T.ht[:, b:4 * M:4]
             if b % 2 == 0:
                 act(dst, src, F.Copy, ["P%d" % (2 + b)], ["ht%d" % b], scale=0.03125)
             else:
                 ts(dst, src, 0.03125, A.mult, ["P%d" % (2 + b)], ["ht%d" % b])
         quant("qh", "sh", 0, 128, T.ht[:], ["ht0", "ht1", "ht2", "ht3", "htz"], ["qh"])
-        mm(0, "qp", "sp", U0, "qh", "sh", 128, UA + ["qh"])
-        for b in range(4):
+        mm(0, "qp", "sp", U0, "qh", "sh", 0, 128, UA + ["qh"])
+        for b in range(3):
             act(T.hp[:, M * b:M * b + M], T.ht[:, b:4 * M:4], F.Copy, ["ht%d" % b], ["hp%d" % b])
+        cp(T.hp[:, 3 * M:], T.ht[:, 3:4 * M:4], ["ht3"], ["hp3"])
         cp(T.vs[:], T.p0[:, 0:M], ["P0"], ["vs"])
-        tt(T.g1[:], T.vs[:].indirect(T.lh16[:, 0:NT]), T.kp[:], A.add, ["vs", "lh16", "kp"], ["g1"])
-        tt(T.wl[:, 0:2 * C:2], T.vs[:].indirect(T.lh16[:, NT:]), T.g1[:], A.is_gt, ["vs", "lh16", "g1"], ["wlw"])
-        scan(T.ns[:], T.kc[:], T.wl[:], A.mult, A.add, ["kc", "kcd", "wlw", "wll"], ["ns"])
+        cp(T.g1[:, 0:16 * GV], T.vs[:].indirect(T.lh16[:, 0:GV]), ["vs", "lh16"], ["g1a"])
+        act(T.g1[:, 16 * GV:], T.vs[:].indirect(T.lh16[:, GV:NT]), F.Copy, ["vs", "lh16"], ["g1b"])
+        tt(T.wl[:, 0:32 * GV:2], T.vs[:].indirect(T.lh16[:, NT:NT + GV]), T.g1[:, 0:16 * GV], A.is_gt, ["vs", "lh16", "g1a"], ["wla"])
+        tt(T.wl[:, 32 * GV:2 * C:2], T.vs[:].indirect(T.lh16[:, NT + GV:]), T.g1[:, 16 * GV:], A.is_gt, ["vs", "lh16", "g1b"], ["wlb"])
+        scan(T.ns[:], T.kc[:], T.wl[:], A.mult, A.add, ["kc", "kco", "kcd", "wla", "wlb", "wll"], ["ns"])
         cp(T.n16[:], T.ns[:, 31:2 * C:32], ["ns"], ["n16"])
         for b in (2, 3):
             act(T.hg[:, C * (b - 2):C * (b - 1)], T.hp[:, M * b:M * b + M].indirect(T.n16[:]), F.Copy, ["hp%d" % b, "n16"], ["hg%d" % b])
         for b in (0, 1):
             tt(T.xt[:, b:4 * C:4], T.hp[:, M * b:M * b + M].indirect(T.n16[:]), T.fs[:, C * b:C * b + C], A.add,
                ["hp%d" % b, "n16", "fs%d" % b], [XT[b]])
-        for b in (2, 3):
-            tt(T.xt[:, b:4 * C:4], T["p%d" % (4 + b)][:, 0:C], T.hg[:, C * (b - 2):C * (b - 1)], A.add,
-               ["P%d" % (4 + b), "hg%d" % b], [XT[b]])
+        tt(T.xt[:, 2:4 * C:4], T.p6[:, 0:C], T.hg[:, 0:C], A.add, ["P6", "hg2"], [XT[2]])
+        tt(T.xt[:, 4 * CA + 3:4 * C:4], T.p7[:, CA:C], T.hg[:, C + CA:], A.add, ["P7", "hg3"], ["xa"])
+        tt(T.xt[:, 3:4 * CA:4], T.p7[:, 0:CA], T.hg[:, C:C + CA], A.add, ["P7", "hg3"], ["xb"])
 
     act(T.ndu[:], T.nt[:].indirect(T.n16[:]), F.Copy, ["nt", "n16"], ["ndu"])
     op("s", lambda: g.sync.dma_start(T.nd[:], T.ndu[0:128:16, :]), ["ndu"], [], sem="outs")
-    quant("qx", "sx", 0, C, T.xt[:], XT, ["qx"])
-    mm(1, "qv", "sv", 0, "qx", "sx", C, ["qv", "qx"])
-    op("s", lambda: g.sync.dma_start(T.oc[:], T.qx[:].bitcast(dt.uint8)), ["qx"], [], sem="outs")
+    quant_x()
+    mm(1, "qv", "sv", 0, "qx", "sx", CA, C, ["qv", "qxa"])
+    mm(0, "qv", "sv", 0, "qx", "sx", 0, CA, ["qv", "qxb"])
+    act(T.ys[:, CA:], T.p1[:, 0:C - CA], F.Copy, ["P1"], ["ysa"])
+    cp(T.ys[:, 0:CA], T.p0[:, 0:CA], ["P0"], ["ysb"])
+    op("s", lambda: g.sync.dma_start(T.oc[:], T.qx[:].bitcast(dt.uint8)), QX, [], sem="outs")
+    op("s", lambda: g.sync.dma_start(T.y[:], T.ys[:]), ["ysa", "ysb"], [], sem="outs")
     for k in range(4):
-        op("a", lambda: S.dma_start(T.osc[4 * k:4 * k + 4, :], T.sx[32 * k:32 * k + 4, :]), ["qx"], [], sem="outs")
-    cp(T.ys[:], T.p1[:, 0:C], ["P1"], ["ys"])
-    op("s", lambda: g.sync.dma_start(T.y[:], T.ys[:]), ["ys"], [], sem="outs")
+        op("a", lambda: S.dma_start(T.osc[4 * k:4 * k + 4, :], T.sx[32 * k:32 * k + 4, :]), QX, [], sem="outs")
     for s in ("g", "sent", "t", "a", "v", "outs"):
         wait("s", (s, count[s]))

@@ -2,19 +2,21 @@ from concourse.mybir import dt, AluOpType, ActivationFunctionType
 
 C, M, R = 288, 96, 3
 NT = C // 16
-CA, CB = 160, 192
+CA, CB = 160, 208
+PART = {"a": (CA, C), "b": (0, CA)}
 BIG = 1.0e29
 TINY = 1.0e-36
-FS, FZ, FO = 592, 289, 224
+FS, FZ, FO = 592, 304, 216
 STEP, JUMP, DROP = 1024.0, 65536.0, -1048576.0
 MARK = 16 * 1024 + FO + FZ
+HALF = 150
 LIFT = 16384.0
 WHOLE = 12582912.0
-GW = (288, 224, 160, 128)
-ON_ACT = (17, 16, 15, 14, 13)
-SUM_V = (12, 11, 10, 9, 8)
-GV = 6
-RL = 192
+TILES = ((NT, 13, 12, 11), (17, 16, 15, 14), (10, 9, 8, 7), (6, 5, 4, 3))
+GW = (288, 272, 160, 128)
+ON_ACT = TILES[1]
+SUM_V = (13, 12, 11, 10, 9, 8)
+RL = 208
 
 F8, U8, BF, F32, I32, U16 = "float8_e4m3fn_x4", "uint8", "bfloat16", "float32", "int32", "uint16"
 SCRATCH = {}
@@ -31,16 +33,17 @@ for _n, _w, _t in (
         ("qy", 128, F8), ("sy", 128, U8), ("qh", 128, F8), ("sh", 128, U8),
         ("zt", 640, BF), ("et", 516, BF), ("bk", 512, BF), ("wt", 512, BF), ("on", RL, BF),
         ("pi", 8, I32), ("ii", 8, I32), ("cf", 16, F32), ("ul", 24, F32), ("ul16", 32, U16),
-        ("rt", C, BF), ("kp", C, BF), ("k2", C, BF), ("k16", 2 * C, BF), ("cw", C, BF), ("cx", 2 * C, BF),
-        ("p48", 48, F32), ("c48", 48 * 6, F32),
-        ("ca", 296, F32), ("cb", 296, F32), ("jt", C, F32), ("jc", NT, F32), ("jq", NT, F32), ("nt", M, F32),
+        ("rt", C, BF), ("kp", C, BF), ("k2", C, BF), ("k16", C, BF), ("cw", 2 * C, BF), ("cx", 3 * C, BF),
+        ("p24", 24, F32), ("c24", 24 * 7, F32),
+        ("ca", 152, F32), ("jt", C, F32), ("jc", NT, F32), ("jq", NT, F32), ("nt", M, F32),
         ("d1", C, F32), ("sj", C, F32), ("sg", 6 * C, BF), ("jk", 128 * NT, BF), ("spc", 96, BF), ("rs", NT, F32), ("rd", C, BF),
         ("rl", 32 * RL, BF), ("rdj", NT, F32), ("pre", 2 * NT, F32), ("cs", C, F32), ("pl", NT, F32), ("pl16", NT, U16),
-        ("m1", C, BF), ("val", C, F32), ("srt", 296, F32), ("so", 768, F32),
-        ("ni", 14, I32), ("nj", 14, I32), ("nl16", 14, U16), ("f4", 4 * FS, BF), ("fs", 2 * C, BF),
-        ("ga", 4 * M, BF), ("zh", 4 * M, BF), ("yt", 512, BF), ("ht", 512, BF), ("hp", 4 * M, BF), ("hg", 2 * C, BF),
+        ("m1", C, BF), ("val", C, F32), ("srt", 296, F32), ("so", 320, F32),
+        ("ni", 12, I32), ("nj", 12, I32), ("nl16", 12, U16), ("f4", 4 * FS, BF), ("fs", 2 * C, BF),
+        ("ga", 8 * M, BF), ("zh", 4 * M, BF), ("yt", 512, BF), ("ht", 512, BF), ("hp", 4 * M, BF), ("hg", 2 * C, BF),
         ("col", 2 * C, BF), ("co", 2 * C, BF), ("ab", 2 * NT, F32), ("ar", 2 * NT, F32), ("b4", 2 * NT, F32),
-        ("b3", NT, F32), ("b5", NT, F32), ("zz", NT, F32), ("nn", 2 * NT, F32), ("lh", 2 * NT, F32), ("lh16", 2 * NT, U16),
+        ("b3", NT, F32), ("b5", NT, F32), ("zz", NT, F32), ("dd", NT, F32), ("bit", 2 * NT, F32), ("nn", 2 * NT, F32),
+        ("lh", 2 * NT, F32), ("lh16", 2 * NT, U16),
         ("vs", M, F32), ("g1", C, F32), ("kc", 2 * C, BF), ("wl", 2 * C, BF), ("ns", 2 * C, BF), ("n16", NT, U16),
         ("ndu", C, F32), ("ys", C, F32)):
     _buf(_n, _w, _t)
@@ -119,8 +122,8 @@ def rank_program(g, core, T, topo):
     def cp(out, a, rd, wr):
         op("v", lambda: V.tensor_copy(out, a), rd, wr)
 
-    def fill(out, x, wr):
-        op("v", lambda: V.memset(out, x), [], wr)
+    def fill(out, x, wr, rd=()):
+        op("v", lambda: V.memset(out, x), list(rd), wr)
 
     def scan(out, a, b, o0, o1, rd, wr, first=0.0):
         op("v", lambda: V.tensor_tensor_scan(out, a, b, first, o0, o1), rd, wr)
@@ -147,98 +150,102 @@ def rank_program(g, core, T, topo):
     def words(name, a, b):
         return T[name][:, a:b].bitcast(dt.uint32)
 
-    def pick_u(a, b):
+    def pick_u(a, b, lst):
         off = T.ul16[:, a // 16:b // 16]
-        op("v", lambda: V.tensor_copy(words("qp", a, b), words("qu", 0, 128).indirect(off)), ["qu", "ula", "ulb"], ["qp%d" % a])
-        act(T.sp[:, a:b], T.su[:, 0:128].indirect(off), F.Copy, ["qu", "ula", "ulb"], ["sp%d" % a])
+        op("v", lambda: V.tensor_copy(words("qp", a, b), words("qu", 0, 128).indirect(off)), ["qu", lst], ["qp%d" % a])
+        act(T.sp[:, a:b], T.su[:, 0:128].indirect(off), F.Copy, ["qu", lst], ["sp%d" % a])
 
-    XT = ["xt0", "xt1", "xt2", "xt3"]
     U0, UC, U1, U2 = 0, 128, 256, 384
-    UA, UB, UD = ["qp0", "sp0"], ["qp128", "sp128"], ["qp256", "sp256"]
+    UA, UB = ["qp0", "sp0"], ["qp128", "sp128"]
     QX = ["qxa", "qxb"]
 
     op("a", lambda: S.dma_start(T.ut[:], T.u[:]), [], ["ut"], sem="lu")
-    op("s", lambda: g.sync.dma_start(T.xt[:, 4 * CA:], T.x[:, 4 * CA:]), [], ["xa"], sem="lxa")
-    op("s", lambda: g.sync.dma_start(T.xt[:, 0:4 * CA], T.x[:, 0:4 * CA]), [], ["xb"], sem="lxb")
-
-    fill(T.zt[:], 0.0, ["zt"])
-    iota(T.pi[:, 0:1], [[0, 1]], 0, 1, ["pi"], small=False)
-    iota(T.ul[:], [[1, 3], [16, 8]], 0, 0, ["ul"])
-    iota(T.rt[:], [[0, NT], [1, 16]], 0, 0, ["rt"])
-    iota(T.p48[:], [[1, 48]], 48, 0, ["p48"])
-    select(T.et[:], T.zt[:, 0:516], [[-1, 516]], A.not_equal, 1.0, 3, 4, ["zt"], ["et"])
-    fill(T.wt[:], 1.0 / LIFT, ["wt"])
-    for e in range(4):
-        op("v", lambda: V.memset(T.wt[:, 60 + e:512:64], 1.0), ["wt"], ["wt%d" % e])
-    select(T.bk[:], T.wt[:], [[-16, 8], [0, 64]], A.is_ge, 0.0, 0, 1, ["wt%d" % e for e in range(4)], ["bk"])
-    select(T.bk[:], T.bk[:], [[16, 8], [0, 64]], A.is_ge, 0.0, 15, -1, ["bk"], ["bk"])
-    iota(T.jc[:], [[16, NT]], 15, 0, ["jc"])
-    iota(T.jt[:], [[1, C]], MARK, 0, ["jt"])
-    iota(T.nt[:], [[1, M]], 0, 0, ["nt"])
-    p1 = T.pi[:, 0:1]
-    ts(T.ii[:, 0:1], p1, 15, A.bitwise_and, ["pi"], ["i0"])
-    ts(T.ii[:, 1:2], p1, 1, A.arith_shift_right, ["pi"], ["i1"], 7, A.bitwise_and)
-    ts(T.ii[:, 2:3], p1, 1, A.bitwise_and, ["pi"], ["i2"])
-    ts(T.ii[:, 3:4], p1, 1, A.arith_shift_right, ["pi"], ["i3"], 1, A.bitwise_and)
-    fill(T.k2[:], 0.0, ["k2"])
-    cp(T.cf[:, 0:4], T.ii[:, 0:4], ["i0", "i1", "i2", "i3"], ["cf"])
-    cq, ch, cc, cpar = [T.cf[:, k:k + 1] for k in range(4)]
-    cq1, h6, sig, mb, low = [T.cf[:, k:k + 1] for k in range(4, 9)]
-    cp(T.ul16[:, 0:8], T.ul[:, 0:8], ["ul"], ["ula"])
-    cp(T.ul16[:, 16:32], T.ul[:, 8:24], ["ul"], ["ula"])
-    fill(T.k2[:, 0:C:16], -4 * BIG, ["k2"])
-    ts(T.ul16[:, 8:16], T.ul[:, 8:16], cpar, A.add, ["ul", "cf"], ["ulb"])
-    ts(h6, ch, 6.0, A.mult, ["cf"], ["h6"])
-    ts(cq1, cq, 1.0, A.add, ["cf"], ["cq1"])
-    ts(T.kp[:], T.rt[:], cq, A.not_equal, ["rt", "cf"], ["kp"], BIG, A.mult)
-    fill(T.k16[:], 1.0, ["k16"])
-    fill(T.on[:], 1.0, ["on"])
-    fill(T.rs[:], 0.0, ["rs%d" % t for t in range(NT)])
-    fill(T.k16[:, 0:2 * C:16], 0.0, ["k16"])
-
-    for w in range(4):
-        n = 320 if w == 3 else 192
-        act(T["gt%d" % w][:, 4 * GW[w] - n:], T.zt[:, 0:n], F.Copy, ["zt"], ["g%d.%d" % (w, e) for e in range(4)])
-    act(sig, cc, F.Identity, ["cf"], ["sig"], scale=2.0, bias=-1.0)
-    act(mb, cc, F.Identity, ["cf"], ["mb"], scale=-2 * TINY, bias=TINY)
-    act(T.rl[:, 32 * (RL - 1):], T.zt[:, 0:32], F.Copy, ["zt"], ["rl%d" % t for t in SUM_V])
-    act(T.so[:, 294:384], T.zt[:, 0:90], F.Copy, ["zt"], ["soz"])
-    act(T.yt[:, 4 * M:512], T.zt[:, 0:128], F.Copy, ["zt"], ["ytz"])
-    act(T.ht[:, 4 * M:512], T.zt[:, 0:128], F.Copy, ["zt"], ["htz"])
-    for b in range(4):
-        act(T.f4[:, FS * b:FS * b + FZ], T.zt[:, 0:FZ], F.Copy, ["zt"], ["f4z%d" % b])
-
-    c0, c1, c2, c3, c4, c5 = [T.c48[:, 48 * k:48 * k + 48] for k in range(6)]
-    ts(c0, T.p48[:], h6, A.subtract, ["p48", "h6"], ["c0"])
-    ts(T.cx[:, 0:C], T.rt[:], cq, A.not_equal, ["rt", "cf"], ["cxa"])
-    ts(c1, c0, 48.0, A.is_ge, ["c0"], ["c1"], -48.0, A.mult)
-    ts(T.cx[:, C:], T.rt[:], cq1, A.is_equal, ["rt", "cq1"], ["cxb"], LIFT, A.mult)
-    tt(c2, c0, c1, A.add, ["c0", "c1"], ["c2"])
-    tt(T.cw[:], T.cx[:, 0:C], T.cx[:, C:], A.max, ["cxa", "cxb"], ["cw"])
-    ts(c4, c2, 11.0, A.is_equal, ["c2"], ["c4"], JUMP, A.mult)
-    ts(c5, c2, 47.0, A.is_equal, ["c2"], ["c5"], DROP, A.mult)
-    ts(c3, c2, 10.0, A.is_le, ["c2"], ["c3"], STEP, A.mult)
-    quant("qu", "su", 0, 128, T.ut[:], ["ut"], ["qu"])
-    tt(c0, c4, c5, A.add, ["c4", "c5"], ["c0"])
-    pick_u(0, 128)
-    tt(T.ca[:, 0:48], c0, c3, A.add, ["c0", "c3"], ["ca"])
-    tt(T.cb[:, 0:48], c0, c3, A.subtract, ["c0", "c3"], ["cb"])
-    pick_u(128, 256)
-    for a, b in ((48, 96), (96, 192), (192, 294)):
-        for n in ("ca", "cb"):
-            act(T[n][:, a:b], T[n][:, 0:b - a], F.Copy, [n], [n])
-
-    wait("s", last["xb"])
+    op("s", lambda: g.sync.dma_start(T.xt[:, 4 * CA:], T.x[:, 4 * CA:]), [], ["x0a"], sem="lxa")
+    op("s", lambda: g.sync.dma_start(T.xt[:, 0:4 * CA], T.x[:, 0:4 * CA]), [], ["x0b"], sem="lxb")
+    wait("s", last["x0b"])
     op("s", lambda: g.sync.dma_start(T.qw[:].bitcast(dt.uint8), T.wc[:]), [], [], sem="lw")
     op("s", lambda: g.sync.dma_start(T.sw[:], T.ws[:]), [], ["qw"], sem="lw")
     op("s", lambda: g.sync.dma_start(T.vt[:], T.v[:]), [], ["vt"], sem="lv")
 
+    fill(T.zt[:], 0.0, ["zt"])
+    fill(T.wt[:], 1.0 / LIFT, ["wt"])
+    fill(T.k2[:], 0.0, ["k2"])
+    iota(T.pi[:, 0:1], [[0, 1]], 0, 1, ["pi"], small=False)
+    iota(T.ul[:], [[1, 3], [16, 8]], 0, 0, ["ul"])
+    iota(T.rt[:], [[0, NT], [1, 16]], 0, 0, ["rt"])
+    iota(T.p24[:], [[1, 24]], 24, 0, ["p24"])
+    select(T.et[:], T.zt[:, 0:516], [[-1, 516]], A.not_equal, 1.0, 3, 4, ["zt"], ["et"])
+    p1 = T.pi[:, 0:1]
+    ts(T.ii[:, 0:1], p1, 15, A.bitwise_and, ["pi"], ["i0"])
+    ts(T.ii[:, 1:2], p1, 2, A.arith_shift_right, ["pi"], ["i1"], 3, A.bitwise_and)
+    ts(T.ii[:, 2:3], p1, 1, A.arith_shift_right, ["pi"], ["i2"], 1, A.bitwise_and)
+    ts(T.ii[:, 3:4], p1, 2, A.arith_shift_right, ["pi"], ["i3"], 1, A.bitwise_and)
+    ts(T.ii[:, 4:5], p1, 1, A.bitwise_and, ["pi"], ["i4"])
+    for e in range(4):
+        fill(T.wt[:, 60 + e:512:64], 1.0, ["wt%d" % e], ["wt"])
+    cp(T.cf[:, 0:5], T.ii[:, 0:5], ["i0", "i1", "i2", "i3", "i4"], ["cf"])
+    cq, ch, cc, cpar, cfl = [T.cf[:, k:k + 1] for k in range(5)]
+    cq1, h6, sig, mb, low, stp = [T.cf[:, k:k + 1] for k in range(5, 11)]
+    cp(T.ul16[:, 0:8], T.ul[:, 0:8], ["ul"], ["ul0"])
+    fill(T.k2[:, 0:C:16], -4 * BIG, ["k2"])
+    cp(T.ul16[:, 16:32], T.ul[:, 8:24], ["ul"], ["ul2"])
+    fill(T.rs[:], 0.0, ["rs%d" % t for t in range(NT)])
+    ts(T.kp[:], T.rt[:], cq, A.not_equal, ["rt", "cf"], ["kp"], BIG, A.mult)
+    ts(T.ul16[:, 8:16], T.ul[:, 8:16], cpar, A.add, ["ul", "cf"], ["ul1"])
+    select(T.bk[:], T.wt[:], [[-16, 8], [0, 64]], A.is_ge, 0.0, 0, 1, ["wt%d" % e for e in range(4)], ["bk"])
+    select(T.bk[:], T.bk[:], [[16, 8], [0, 64]], A.is_ge, 0.0, 15, -1, ["bk"], ["bk"])
+    iota(T.jc[:], [[16, NT]], 15, 0, ["jc"])
+    iota(T.jt[:], [[1, C]], MARK, 0, ["jt"])
+    iota(T.rl[:, 32 * (RL - 1):], [[0, 32]], 0, 0, ["rl%d" % t for t in SUM_V])
+    for b in range(4):
+        iota(T.f4[:, FS * b:FS * b + FZ], [[0, FZ]], 0, 0, ["f4z%d" % b])
+    iota(T.yt[:, 4 * M:512], [[0, 128]], 0, 0, ["ytz"])
+    iota(T.ht[:, 4 * M:512], [[0, 128]], 0, 0, ["htz"])
+    iota(T.nt[:], [[1, M]], 0, 0, ["nt"])
+
+    for w in range(4):
+        n = 4 * GW[w] - 64 * TILES[w][3]
+        act(T["gt%d" % w][:, 4 * GW[w] - n:], T.zt[:, 0:n], F.Copy, ["zt"], ["g%d.%d" % (w, e) for e in range(4)])
+    act(h6, ch, F.Identity, ["cf"], ["h6"], scale=6.0)
+    act(cq1, cq, F.Identity, ["cf"], ["cq1"], bias=1.0)
+    act(stp, cfl, F.Identity, ["cf"], ["stp"], scale=-2 * STEP, bias=STEP)
+
+    quant("qu", "su", 0, 128, T.ut[:], ["ut"], ["qu"])
+    c0, c1, c2, c3, c4, c5, c6 = [T.c24[:, 24 * k:24 * k + 24] for k in range(7)]
+    ts(T.cx[:, 0:C], T.rt[:], cq, A.not_equal, ["rt", "cf"], ["cxa"])
+    ts(c0, T.p24[:], h6, A.subtract, ["p24", "h6"], ["c0"])
+    pick_u(0, 128, "ul0")
+
+    def later_constants():
+        ts(c1, c0, 24.0, A.is_ge, ["c0"], ["c1"], -24.0, A.mult)
+        ts(T.cx[:, C:2 * C], T.rt[:], cq1, A.is_equal, ["rt", "cq1"], ["cxb"], LIFT, A.mult)
+        pick_u(128, 256, "ul1")
+        act(sig, cc, F.Identity, ["cf"], ["sig"], scale=2.0, bias=-1.0)
+        act(mb, cc, F.Identity, ["cf"], ["mb"], scale=-2 * TINY, bias=TINY)
+        act(T.on[:], T.zt[:, 0:RL], F.Identity, ["zt"], ["on"], bias=1.0)
+        act(T.k16[:], T.rt[:], F.Sign, ["rt"], ["k16"])
+        tt(c2, c0, c1, A.add, ["c0", "c1"], ["c2"])
+        tt(T.cw[:, 0:C], T.cx[:, 0:C], T.cx[:, C:2 * C], A.max, ["cxa", "cxb"], ["cw"])
+        yield
+        ts(c4, c2, 11.0, A.is_equal, ["c2"], ["c4"], JUMP, A.mult)
+        ts(c5, c2, 23.0, A.is_equal, ["c2"], ["c5"], DROP, A.mult)
+        ts(c3, c2, 10.0, A.is_le, ["c2", "stp"], ["c3"], stp, A.mult)
+        yield
+        for b in (1, 2):
+            quant("qe", "se", 128 * b, 128 * b + 128, T.et[:, 3 - b:515 - b], ["et"], ["qe%d" % b])
+        tt(c6, c4, c5, A.add, ["c4", "c5"], ["c6"])
+        yield
+        for b in (3, 0):
+            quant("qe", "se", 128 * b, 128 * b + 128, T.et[:, 3 - b:515 - b], ["et"], ["qe%d" % b])
+        tt(T.ca[:, 0:24], c6, c3, A.add, ["c6", "c3"], ["ca"])
+        yield
+
     def slot(t):
-        w, e = (NT - t) // 4, (NT - t) % 4
+        w, e = [(w, k.index(t)) for w, k in enumerate(TILES) if t in k][0]
         return "g%d.%d" % (w, e), T["gt%d" % w][:, e:64 * t:4]
 
     def sjc(t):
-        return T.sj[:, 16 * t + 15:16 * t + 16], "sja" if 16 * t >= CB else "sjb"
+        return T.sj[:, 16 * t + 15:16 * t + 16], "sja" if 16 * t >= CA else "sjb"
 
     def sign(t):
         s, n = sjc(t)
@@ -268,30 +275,59 @@ def rank_program(g, core, T, topo):
     def colsum(w, start, stop):
         mm(2, "qk", "sk", 0, "qg%d" % w, "sg%d" % w, 0, GW[w], ["qk", "qg%d" % w], start, stop)
 
-    def quant_x():
-        quant("qx", "sx", CA, C, T.xt[:, 4 * CA:], XT[:3] + ["xa"], ["qxa"])
-        quant("qx", "sx", 0, CA, T.xt[:, 0:4 * CA], XT[:3] + ["xb"], ["qxb"])
+    def quant_x(k):
+        a, b = PART[k]
+        quant("qx", "sx", a, b, T.xt[:, 4 * a:4 * b], ["x%d%s" % (e, k) for e in range(4)], ["qx" + k])
 
     def marks(a, b):
         tt(T.val[:, a:b], T.jt[:, a:b], T.m1[:, a:b], A.mult, ["m1", "jt"], ["val%d" % a])
 
+    def wrap1(k):
+        a, b = PART[k]
+        src, bank = (T.p4[:, 0:b - a], "P4") if k == "a" else (T.p0[:, a:b], "P0")
+        tt(T.d1[:, a:b], src, T.kp[:, a:b], A.subtract, [bank, "kp"], ["d1" + k])
+
+    def wrap2(k):
+        a, b = PART[k]
+        scan(T.sj[:, a:b], T.k2[:, a:b], T.d1[:, a:b], A.add, A.max, ["k2", "d1" + k], ["sj" + k])
+
+    def plane(b):
+        act(T.f4[:, FS * b + FZ:FS * b + FZ + C], T["p%d" % (4 + b)][:, 0:C], F.Copy, ["P%d" % (4 + b)], ["f4%d" % b], scale=0.25)
+
+    def new_x(e, k):
+        a, b = PART[k]
+        out, name = T.xt[:, 4 * a + e:4 * b:4], "x%d%s" % (e, k)
+        if e < 2:
+            tt(out, T.hp[:, M * e:M * e + M].indirect(T.n16[:, a // 16:b // 16]), T.fs[:, C * e + a:C * e + b], A.add,
+               ["hp%d" % e, "n16" + k, "fs%d" % e], [name])
+        else:
+            tt(out, T["p%d" % (4 + e)][:, a:b], T.hg[:, C * (e - 2) + a:C * (e - 2) + b], A.add, ["P%d" % (4 + e), "hg%d%s" % (e, k)], [name])
+
+    more = later_constants()
+    quant_x("a")
     for r in range(R):
-        quant_x()
         mm(4, "qp", "sp", U0, "qx", "sx", CA, C, UA + ["qxa"])
+        if r == 0:
+            next(more)
+        quant_x("b")
+        wrap1("a")
         mm(0, "qp", "sp", U0, "qx", "sx", 0, CB, UA + QX)
         mm(1, "qp", "sp", U0, "qx", "sx", 0, C - 16, UA + QX)
         mm(3, "qp", "sp", UC, "qx", "sx", 0, C, UB + QX)
-        late = T.p4[:, CB - CA:C - CA]
-        tt(T.d1[:, CB:], late, T.kp[:, CB:], A.subtract, ["P4", "kp"], ["d1a"])
-        scan(T.sj[:, CB:], T.k2[:, CB:], T.d1[:, CB:], A.add, A.max, ["k2", "d1a"], ["sja"])
-        tt(T.d1[:, 0:CB], T.p0[:, 0:CB], T.kp[:, 0:CB], A.subtract, ["P0", "kp"], ["d1b"])
-        tt(T.gt0[:, 4 * CB:4 * C:4], late, T.sj[:, CB:], A.is_le, ["P4", "sja"], ["dga"])
-        scan(T.sj[:, 0:CB], T.k2[:, 0:CB], T.d1[:, 0:CB], A.add, A.max, ["k2", "d1b"], ["sjb"])
         if r == 0:
-            for b in range(4):
-                quant("qe", "se", 128 * b, 128 * b + 128, T.et[:, 3 - b:515 - b], ["et"], ["qe%d" % b])
-            quant("qk", "sk", 0, 128, T.bk[:], ["bk"], ["qk"])
-            ts(T.jq[:], T.jc[:], 47.0, A.max, ["jc", "cf"], ["jq"], cq, A.subtract)
+            next(more)
+        wrap2("a")
+        if r == 0:
+            next(more)
+        wrap1("b")
+        tt(T.gt0[:, 4 * CA:4 * C:4], T.p4[:, 0:C - CA], T.sj[:, CA:], A.is_le, ["P4", "sja"], ["dga"])
+        row(13)
+        wrap2("b")
+        row(12)
+        row(11)
+        row(10)
+        if r == 0:
+            next(more)
         for b in (1, 2, 3, 0):
             mm(4 + b, "qe", "se", 128 * b, "qx", "sx", 0, C, ["qe%d" % b] + QX)
         for k, t in enumerate(ON_ACT):
@@ -300,56 +336,93 @@ def rank_program(g, core, T, topo):
                 relu(ON_ACT[k - 1])
         relu(ON_ACT[-1])
         act(T.m1[:], T.p3[:, 0:C], F.Sign, ["P3", "sig", "mb"], ["m1"], scale=sig, bias=mb)
-        tt(T.gt0[:, 0:4 * CB:4], T.p0[:, 0:CB], T.sj[:, 0:CB], A.is_le, ["P0", "sjb"], ["g0.0"])
-        for t in range(ON_ACT[-1] - 1, 2, -1):
+        tt(T.gt0[:, 0:4 * CA:4], T.p0[:, 0:CA], T.sj[:, 0:CA], A.is_le, ["P0", "sjb"], ["g0.0"])
+        for t in range(9, 2, -1):
             row(t)
         ts(T.spc[:, 0:32], T.p0[:, 16:48], sjc(0)[0], A.is_le, ["P0", "sjb"], ["spc0"])
         ts(T.spc[:, 32:48], T.p0[:, 0:16], sjc(1)[0], A.is_lt, ["P0", "sjb"], ["spc1"])
         ts(T.spc[:, 48:64], T.p0[:, 32:48], sjc(1)[0], A.is_le, ["P0", "sjb"], ["spc1b"])
         ts(T.spc[:, 64:96], T.p0[:, 0:32], sjc(2)[0], A.is_lt, ["P0", "sjb"], ["spc2"])
-        pack(0)
-        colsum(0, True, False)
-        for w in (2, 3, 1):
+        if r == 0:
+            quant("qk", "sk", 0, 128, T.bk[:], ["bk"], ["qk"])
+            ts(T.jq[:], T.jc[:], 47.0, A.max, ["jc", "cf"], ["jq"], cq, A.subtract)
+        scan(T.rd[:], T.k16[:], T.gt0[:, 0:4 * C:4], A.mult, A.add, ["k16", "g0.0", "dga"], ["rd"])
+        for w in (0, 2, 3):
             pack(w)
-            colsum(w, False, w == 1)
-        scan(T.rd[:], T.k16[:, 0:C], T.gt0[:, 0:4 * C:4], A.mult, A.add, ["k16", "g0.0", "dga"], ["rd"])
-        for t in range(ON_ACT[-1] - 1, 2, -1):
+            colsum(w, w == 0, False)
+        tt(T.rdj[:], T.jq[:], T.rd[:, 15:C:16], A.subtract, ["rd", "jq"], ["rdj"])
+        pack(1)
+        colsum(1, False, True)
+        for t in range(13, 2, -1):
             rowsum(t)
         for k in range(3):
             act(T.jk[:, 128 * k:128 * k + 32], T.spc[:, 32 * k:32 * k + 32], F.Identity,
                 ["spc%d" % k] + (["spc1b"] if k == 1 else []), ["rs%d" % k, "jk%d" % k], accum_out=T.rs[:, k:k + 1])
-        tt(T.rdj[:], T.jq[:], T.rd[:, 15:C:16], A.subtract, ["rd", "jq"], ["rdj"])
-        scan(T.cs[:], T.cw[:], T.p2[:, 0:C], A.mult, A.add, ["cw", "P2"], ["cs"])
-        tt(T.pre[:, 0:NT], T.rdj[:], T.rl[:, 32 * (RL - 1):32 * (RL - 1) + NT], A.subtract, ["rdj"] + ["rl%d" % t for t in SUM_V], ["pre0"])
+        if r == 0:
+            for a, b in ((24, 48), (48, 96), (96, HALF)):
+                act(T.ca[:, a:b], T.ca[:, 0:b - a], F.Copy, ["ca"], ["ca"])
+            act(T.cw[:, C:], T.cw[:, 0:C], F.Copy, ["cw"], ["cwb"])
         marks(0, 96)
+        tt(T.pre[:, 0:NT], T.rdj[:], T.rl[:, 32 * (RL - 1):32 * (RL - 1) + NT], A.subtract, ["rdj"] + ["rl%d" % t for t in SUM_V], ["pre0"])
+        scan(T.cs[:], T.cw[:, 0:C], T.p2[:, 0:C], A.mult, A.add, ["cw", "P2"], ["cs"])
         tt(T.pre[:, NT:], T.pre[:, 0:NT], T.rs[:], A.subtract, ["rs%d" % t for t in range(NT)] + ["pre0"], ["pre"])
         marks(96, 192)
         tt(T.pl[:], T.pre[:, NT:], T.cs[:, 15:C:16], A.add, ["pre", "cs"], ["pl"])
         marks(192, C)
         cp(T.pl16[:], T.pl[:], ["pl"], ["pl16"])
+        if r == 0:
+            pick_u(256, 384, "ul2")
         cp(T.srt[:, 0:C].indirect(T.pl16[:]), T.val[:], ["pl16", "val0", "val96", "val192"], ["srt"])
+        if r == 0:
+            pick_u(384, 512, "ul2")
+        mm(0, "qp", "sp", U1, "qx", "sx", 0, C, ["qp256", "sp256"] + QX)
+        mm(1, "qp", "sp", U2, "qx", "sx", 0, C, ["qp384", "sp384"] + QX)
+        plane(0)
+        act(T.ab[:, 0:NT], T.pl[:], F.Identity, ["pl"], ["ab0"], scale=1.0 / 12, bias=-5.5 / 12)
+        act(T.ab[:, NT:], T.pl[:], F.Identity, ["pl"], ["ab1"], scale=1.0 / 12, bias=-11.5 / 12)
+        plane(1)
+        act(T.ar[:], T.ab[:], F.Identity, ["ab0", "ab1"], ["ar"], bias=WHOLE)
+        plane(2)
+        act(T.b3[:], T.ar[:, NT:], F.Identity, ["ar"], ["b3"], bias=-WHOLE)
+        act(T.b4[:, 0:NT], T.ar[:, 0:NT], F.Identity, ["ar"], ["b40"], scale=4.0, bias=-4 * WHOLE)
+        plane(3)
+        act(T.b5[:], T.b3[:], F.Identity, ["b3"], ["b5"], scale=4.0, bias=2.0)
+        act(T.zz[:], T.b3[:], F.Relu, ["b3"], ["zz"], scale=-float(M))
+        act(T.col[:, 0:C], T.p0[:, 0:C], F.Sign, ["P0"], ["col0"], bias=-TINY)
+        act(T.col[:, C:], T.p1[:, 0:C], F.Sign, ["P1"], ["col1"], bias=-TINY)
+        cp(T.srt[:, C:C + 6], T.srt[:, 0:6], ["srt"], ["srt6"])
+        for h in range(2):
+            scan(T.so[:, 160 * h:160 * h + HALF], T.srt[:, 144 * h:144 * h + HALF], T.ca[:, 0:HALF], A.max, A.add,
+                 ["srt", "ca"] + ["srt6"] * h, ["so%d" % h], first=DROP)
+        for h in range(2):
+            tt(T.ni[:, 6 * h:6 * h + 6], T.so[:, 160 * h + 20:160 * h + HALF:24], T.so[:, 160 * h + 29:160 * h + HALF:24], A.max,
+               ["so%d" % h], ["ni%d" % h])
+        if r == 0:
+            ts(T.cx[:, 2 * C:], T.rt[:], cq, A.is_equal, ["rt", "cf"], ["cxc"], LIFT, A.mult)
+        for h in range(2):
+            ts(T.nj[:, 6 * h:6 * h + 6], T.ni[:, 6 * h:6 * h + 6], int(STEP) - 1, A.bitwise_and, ["ni%d" % h], ["nj%d" % h])
+        if r == 0:
+            cp(T.kc[:, 0:2 * C:2], T.cx[:, 0:C], ["cxa"], ["kc"])
+        for h in range(2):
+            ts(T.nl16[:, 6 * h:6 * h + 6], T.nj[:, 6 * h:6 * h + 6], float(FO), A.subtract, ["nj%d" % h], ["nl%d" % h])
+        for h in range(2):
+            for b in range(4):
+                out, src = T.ga[:, M * (2 * b + h):M * (2 * b + h + 1)], T.f4[:, FS * b:FS * b + FZ + C].indirect(T.nl16[:, 6 * h:6 * h + 6])
+                rd, wr = ["f4%d" % b, "f4z%d" % b, "nl%d" % h], ["ga%d%d" % (b, h)]
+                if b < 2:
+                    cp(out, src, rd, wr)
+                else:
+                    act(out, src, F.Copy, rd, wr)
+        scan(T.co[:, 0:C], T.cw[:, 0:C], T.col[:, 0:C], A.mult, A.add, ["cw", "col0"], ["co0"])
         for b in range(4):
-            if b == 3:
-                act(T.srt[:, C:C + 6], T.srt[:, 0:6], F.Copy, ["srt"], ["srt6"])
-            act(T.f4[:, FS * b + FZ:FS * b + FZ + C], T["p%d" % (4 + b)][:, 0:C], F.Copy, ["P%d" % (4 + b)], ["f4%d" % b], scale=0.25)
-        scan(T.so[:, 0:C], T.srt[:, 0:C], T.ca[:, 0:C], A.max, A.add, ["srt", "ca"], ["so0"])
-        scan(T.so[:, 384:678], T.srt[:, 0:294], T.cb[:, 0:294], A.max, A.add, ["srt", "srt6", "cb"], ["so1"])
-        scan(T.so[:, C:294], T.srt[:, C:294], T.ca[:, C:294], A.max, A.add, ["srt6", "ca", "so0"], ["so2"], first=T.so[:, C - 1:C])
-        tt(T.ni[:], T.so[:, 41:678:48], T.so[:, 53:678:48], A.max, ["so0", "so1", "so2", "soz"], ["ni"])
-        ts(T.nj[:], T.ni[:], int(STEP) - 1, A.bitwise_and, ["ni"], ["nj"])
-        ts(T.nl16[:], T.nj[:], float(FO), A.subtract, ["nj"], ["nl16"])
-        for b in range(4):
-            win, first = T.f4[:, FS * b:FS * b + FZ + C], T.ga[:, M * b:M * b + M]
-            if b == 0:
-                cp(first, win.indirect(T.nl16[:, 0:6]), ["f40", "f4z0", "nl16"], ["ga0"])
-            else:
-                act(first, win.indirect(T.nl16[:, 0:6]), F.Copy, ["f4%d" % b, "f4z%d" % b, "nl16"], ["ga%d" % b])
-        for b in range(4):
-            tt(T.zh[:, b:4 * M:4], T.f4[:, FS * b:FS * b + FZ + C].indirect(T.nl16[:, 8:14]), T.ga[:, M * b:M * b + M], A.add,
-               ["f4%d" % b, "f4z%d" % b, "nl16", "ga%d" % b], ["zh%d" % b])
+            tt(T.zh[:, b:4 * M:4], T.ga[:, 2 * M * b:2 * M * (b + 1):2], T.ga[:, 2 * M * b + 1:2 * M * (b + 1):2], A.add,
+               ["ga%d0" % b, "ga%d1" % b], ["zh%d" % b])
+        scan(T.co[:, C:], T.cw[:, C:], T.col[:, C:], A.mult, A.add, ["cwb", "col1"], ["co1"])
+        tt(T.b4[:, NT:], T.b5[:], T.zz[:], A.add, ["b5", "zz"], ["b41"])
         ZH = ["zh%d" % b for b in range(4)]
         tt(T.yt[:, 4 * M - 8:4 * M], T.zh[:, 4 * M - 8:4 * M], T.zh[:, 0:8], A.add, ZH, ["yt1"])
         tt(T.yt[:, 0:4 * M - 8], T.zh[:, 0:4 * M - 8], T.zh[:, 8:4 * M], A.add, ZH, ["yt0"])
+        ts(T.bit[:], T.co[:, 15:2 * C:16], 0.0, A.is_gt, ["co0", "co1"], ["bit"])
         quant("qy", "sy", 0, 128, T.yt[:], ["yt0", "yt1", "ytz"], ["qy"])
         wait("g", last["qy"])
         lc, ls, arr = "lc%d" % r, "ls%d" % r, "arr%d" % r
@@ -360,38 +433,22 @@ def rank_program(g, core, T, topo):
         readers["qy"] = {"sent": count["sent"]}
         snap[(arr, 2 * ne)] = {arr: 2 * ne}
         last["land%d" % r] = (arr, 2 * ne)
-        if r == 0:
-            pick_u(256, 512)
-            fill(T.wl[:], 0.0, ["wla", "wlb", "wll"])
-            cp(T.kc[:, 0:2 * C:2], T.cx[:, 0:C], ["cxa"], ["kc"])
-            ts(T.cx[:, C:], T.rt[:], cq, A.is_equal, ["rt", "cf", "cw"], ["cxb"], LIFT, A.mult)
-            ts(low, cq, 15.0, A.is_equal, ["cf"], ["low"], 1.0 / LIFT, A.max)
-            ts(T.kc[:, 1:2 * C:2], T.cx[:, C:], 1.0, A.max, ["cxb"], ["kco"])
-        mm(0, "qp", "sp", U1, "qx", "sx", 0, C, UD + QX)
-        mm(1, "qp", "sp", U2, "qx", "sx", 0, C, UD + QX)
-        act(T.ab[:, 0:NT], T.pl[:], F.Identity, ["pl"], ["ab0"], scale=1.0 / 12, bias=-5.5 / 12)
-        act(T.ab[:, NT:], T.pl[:], F.Identity, ["pl"], ["ab1"], scale=1.0 / 12, bias=-11.5 / 12)
-        act(T.ar[:], T.ab[:], F.Identity, ["ab0", "ab1"], ["ar"], bias=WHOLE)
-        act(T.b3[:], T.ar[:, NT:], F.Identity, ["ar"], ["b3"], bias=-WHOLE)
-        act(T.b4[:, 0:NT], T.ar[:, 0:NT], F.Identity, ["ar"], ["b40"], scale=4.0, bias=-4 * WHOLE)
-        act(T.b5[:], T.b3[:], F.Identity, ["b3"], ["b5"], scale=4.0, bias=2.0)
-        act(T.zz[:], T.b3[:], F.Relu, ["b3"], ["zz"], scale=-float(M))
         for b in range(2):
             act(T.fs[:, C * b:C * b + C], T["p%d" % (4 + b)][:, 0:C], F.Copy, ["P%d" % (4 + b)], ["fs%d" % b])
+        tt(T.nn[:], T.b4[:], T.bit[:], A.add, ["b40", "b41", "bit"], ["nn"])
         quant(lc, ls, M, M + 128, T.zt[:, 0:512], ["zt"], ["pad%d" % r])
-        tt(T.col[:, 0:C], T.p0[:, 0:C], T.kp[:], A.is_gt, ["P0", "kp"], ["col0"])
-        tt(T.col[:, C:], T.p1[:, 0:C], T.kp[:], A.is_gt, ["P1", "kp"], ["col1"])
-        scan(T.co[:], T.k16[:], T.col[:], A.mult, A.add, ["k16", "col0", "col1"], ["co"])
-        tt(T.b4[:, NT:], T.b5[:], T.zz[:], A.add, ["b5", "zz"], ["b41"])
-        if r == 1:
-            quant("qv", "sv", 0, 128, T.vt[:], ["vt"], ["qv"])
-        tt(T.nn[:], T.b4[:], T.co[:, 15:2 * C:16], A.add, ["b40", "b41", "co"], ["nn"])
+        if r == 0:
+            fill(T.wl[:], 0.0, ["wla", "wlb", "wll"])
+            ts(low, cq, 15.0, A.is_equal, ["cf"], ["low"], 1.0 / LIFT, A.max)
         tt(T.lh[:, 0:NT], T.nn[:, 0:NT], T.nn[:, NT:], A.min, ["nn"], ["lo"])
         tt(T.lh[:, NT:], T.nn[:, 0:NT], T.nn[:, NT:], A.max, ["nn"], ["hi"])
+        if r == 0:
+            ts(T.kc[:, 1:2 * C:2], T.cx[:, 2 * C:], 1.0, A.max, ["cxc"], ["kco"])
+        if r == 1:
+            quant("qv", "sv", 0, 128, T.vt[:], ["vt"], ["qv"])
         tt(T.wl[:, 31:2 * C:32], T.nn[:, 0:NT], T.nn[:, NT:], A.min, ["nn"], ["wll"])
-        tt(T.zz[:], T.lh[:, NT:], T.lh[:, 0:NT], A.subtract, ["lo", "hi"], ["zz"])
+        tt(T.dd[:], T.lh[:, NT:], T.lh[:, 0:NT], A.subtract, ["lo", "hi"], ["dd"])
         cp(T.lh16[:], T.lh[:], ["lo", "hi"], ["lh16"])
-        ts(T.kc[:, 31:2 * C:32], T.zz[:], low, A.mult, ["zz", "low", "kco"], ["kcd"])
         for b in range(4):
             mm(2 + b, "qw", "sw", 128 * b, lc, ls, 0, 128, ["qw", "land%d" % r, "pad%d" % r])
             src, dst = T["p%d" % (2 + b)][:, 0:M], T.ht[:, b:4 * M:4]
@@ -399,37 +456,51 @@ def rank_program(g, core, T, topo):
                 act(dst, src, F.Copy, ["P%d" % (2 + b)], ["ht%d" % b], scale=0.03125)
             else:
                 ts(dst, src, 0.03125, A.mult, ["P%d" % (2 + b)], ["ht%d" % b])
+        ts(T.kc[:, 31:2 * C:32], T.dd[:], low, A.mult, ["dd", "low", "kco"], ["kcd"])
         quant("qh", "sh", 0, 128, T.ht[:], ["ht0", "ht1", "ht2", "ht3", "htz"], ["qh"])
         mm(0, "qp", "sp", U0, "qh", "sh", 0, 128, UA + ["qh"])
-        for b in range(3):
-            act(T.hp[:, M * b:M * b + M], T.ht[:, b:4 * M:4], F.Copy, ["ht%d" % b], ["hp%d" % b])
-        cp(T.hp[:, 3 * M:], T.ht[:, 3:4 * M:4], ["ht3"], ["hp3"])
+        for b in range(4):
+            if b < 2:
+                cp(T.hp[:, M * b:M * b + M], T.ht[:, b:4 * M:4], ["ht%d" % b], ["hp%d" % b])
+            else:
+                act(T.hp[:, M * b:M * b + M], T.ht[:, b:4 * M:4], F.Copy, ["ht%d" % b], ["hp%d" % b])
         cp(T.vs[:], T.p0[:, 0:M], ["P0"], ["vs"])
-        cp(T.g1[:, 0:16 * GV], T.vs[:].indirect(T.lh16[:, 0:GV]), ["vs", "lh16"], ["g1a"])
-        act(T.g1[:, 16 * GV:], T.vs[:].indirect(T.lh16[:, GV:NT]), F.Copy, ["vs", "lh16"], ["g1b"])
-        tt(T.wl[:, 0:32 * GV:2], T.vs[:].indirect(T.lh16[:, NT:NT + GV]), T.g1[:, 0:16 * GV], A.is_gt, ["vs", "lh16", "g1a"], ["wla"])
-        tt(T.wl[:, 32 * GV:2 * C:2], T.vs[:].indirect(T.lh16[:, NT + GV:]), T.g1[:, 16 * GV:], A.is_gt, ["vs", "lh16", "g1b"], ["wlb"])
-        scan(T.ns[:], T.kc[:], T.wl[:], A.mult, A.add, ["kc", "kco", "kcd", "wla", "wlb", "wll"], ["ns"])
-        cp(T.n16[:], T.ns[:, 31:2 * C:32], ["ns"], ["n16"])
-        for b in (2, 3):
-            act(T.hg[:, C * (b - 2):C * (b - 1)], T.hp[:, M * b:M * b + M].indirect(T.n16[:]), F.Copy, ["hp%d" % b, "n16"], ["hg%d" % b])
-        for b in (0, 1):
-            tt(T.xt[:, b:4 * C:4], T.hp[:, M * b:M * b + M].indirect(T.n16[:]), T.fs[:, C * b:C * b + C], A.add,
-               ["hp%d" % b, "n16", "fs%d" % b], [XT[b]])
-        tt(T.xt[:, 2:4 * C:4], T.p6[:, 0:C], T.hg[:, 0:C], A.add, ["P6", "hg2"], [XT[2]])
-        tt(T.xt[:, 4 * CA + 3:4 * C:4], T.p7[:, CA:C], T.hg[:, C + CA:], A.add, ["P7", "hg3"], ["xa"])
-        tt(T.xt[:, 3:4 * CA:4], T.p7[:, 0:CA], T.hg[:, C:C + CA], A.add, ["P7", "hg3"], ["xb"])
+        ta = CA // 16
+        cp(T.g1[:, CA:], T.vs[:].indirect(T.lh16[:, ta:NT]), ["vs", "lh16"], ["g1a"])
+        act(T.g1[:, 0:CA], T.vs[:].indirect(T.lh16[:, 0:ta]), F.Copy, ["vs", "lh16"], ["g1b"])
+        for k in "ab":
+            a, b = PART[k]
+            tt(T.wl[:, 2 * a:2 * b:2], T.vs[:].indirect(T.lh16[:, NT + a // 16:NT + b // 16]), T.g1[:, a:b], A.is_gt,
+               ["vs", "lh16", "g1" + k], ["wl" + k])
+        for k in "ab":
+            a, b = PART[k]
+            scan(T.ns[:, 2 * a:2 * b], T.kc[:, 2 * a:2 * b], T.wl[:, 2 * a:2 * b], A.mult, A.add,
+                 ["kc", "kco", "kcd", "wl" + k, "wll"], ["ns" + k])
+        for k in "ab":
+            a, b = PART[k]
+            cp(T.n16[:, a // 16:b // 16], T.ns[:, 2 * a + 31:2 * b:32], ["ns" + k], ["n16" + k])
+        for k in "ab":
+            a, b = PART[k]
+            for e in (2, 3):
+                act(T.hg[:, C * (e - 2) + a:C * (e - 2) + b], T.hp[:, M * e:M * e + M].indirect(T.n16[:, a // 16:b // 16]), F.Copy,
+                    ["hp%d" % e, "n16" + k], ["hg%d%s" % (e, k)])
+        for e, k in ((0, "a"), (1, "a"), (0, "b"), (2, "a"), (3, "a"), (1, "b")):
+            new_x(e, k)
+        quant_x("a")
+        new_x(2, "b")
+        new_x(3, "b")
 
-    act(T.ndu[:], T.nt[:].indirect(T.n16[:]), F.Copy, ["nt", "n16"], ["ndu"])
-    op("s", lambda: g.sync.dma_start(T.nd[:], T.ndu[0:128:16, :]), ["ndu"], [], sem="outs")
-    quant_x()
     mm(1, "qv", "sv", 0, "qx", "sx", CA, C, ["qv", "qxa"])
+    act(T.ndu[:], T.nt[:].indirect(T.n16[:]), F.Copy, ["nt", "n16a", "n16b"], ["ndu"])
+    op("s", lambda: g.sync.dma_start(T.nd[:], T.ndu[0:128:16, :]), ["ndu"], [], sem="outs")
+    quant_x("b")
     mm(0, "qv", "sv", 0, "qx", "sx", 0, CA, ["qv", "qxb"])
     act(T.ys[:, CA:], T.p1[:, 0:C - CA], F.Copy, ["P1"], ["ysa"])
+    op("a", lambda: S.dma_start(T.y[:, CA:], T.ys[:, CA:]), ["ysa"], [], sem="outs")
     cp(T.ys[:, 0:CA], T.p0[:, 0:CA], ["P0"], ["ysb"])
     op("s", lambda: g.sync.dma_start(T.oc[:], T.qx[:].bitcast(dt.uint8)), QX, [], sem="outs")
-    op("s", lambda: g.sync.dma_start(T.y[:], T.ys[:]), ["ysa", "ysb"], [], sem="outs")
     for k in range(4):
         op("a", lambda: S.dma_start(T.osc[4 * k:4 * k + 4, :], T.sx[32 * k:32 * k + 4, :]), QX, [], sem="outs")
+    op("s", lambda: g.sync.dma_start(T.y[:, 0:CA], T.ys[:, 0:CA]), ["ysb"], [], sem="outs")
     for s in ("g", "sent", "t", "a", "v", "outs"):
         wait("s", (s, count[s]))

@@ -2,21 +2,30 @@ from concourse.mybir import dt, AluOpType, ActivationFunctionType
 
 C, M, R = 288, 96, 3
 NT = C // 16
-CA, CB = 160, 208
+CA = 160
 PART = {"a": (CA, C), "b": (0, CA)}
-BIG = 1.0e29
+BIG = 2.0 ** 96
 TINY = 1.0e-36
-FS, FZ, FO = 592, 304, 216
+FS, FZ, FO = 304, 2, 512
 STEP, JUMP, DROP = 1024.0, 65536.0, -1048576.0
 MARK = 16 * 1024 + FO + FZ
-HALF = 150
+HALF = (150, 174)
+LIST = ((0, 6), (6, 13))
 LIFT = 16384.0
-WHOLE = 12582912.0
-TILES = ((NT, 13, 12, 11), (17, 16, 15, 14), (10, 9, 8, 7), (6, 5, 4, 3))
-GW = (288, 272, 160, 128)
-ON_ACT = TILES[1]
-SUM_V = (13, 12, 11, 10, 9, 8)
-RL = 208
+WHOLE = 4 * 12582912.0
+MID = C // 2
+CUT, CUT1 = 176, 224
+TILES = ((NT, 13, 12, 11), (10, 9, 8, 7), (17, 16, 15, 14), (6, 5, 4, 3))
+XT, EXT = 0, (2, 1)
+ON_ACT = TILES[2]
+GW = [max(128, 16 * max(_t)) for _t in TILES]
+ON_VEC = [_t for _t in range(NT - 1, 0, -1) if _t not in ON_ACT]
+SUM_VEC = ON_VEC[:6]
+RL = 8 * ON_VEC[0]
+ORDER = "11 10 in 2 1 9 8 p0 7 6 5 4 p1 3 p2 p3".split()
+BY_ACT, AHEAD = ((3, 0), (1, 1), (2, 1), (3, 1)), ((0, 0), (1, 0), (2, 0), (3, 0), (0, 1))
+LOW = 128
+LAND = 128
 
 F8, U8, BF, F32, I32, U16 = "float8_e4m3fn_x4", "uint8", "bfloat16", "float32", "int32", "uint16"
 SCRATCH = {}
@@ -28,32 +37,31 @@ def _buf(name, n, ty, where="sbuf"):
 
 for _n, _w, _t in (
         ("xt", 4 * C, BF), ("ut", 512, BF), ("vt", 512, BF), ("qx", C, F8), ("sx", C, U8),
-        ("qu", 128, F8), ("su", 128, U8), ("qp", 512, F8), ("sp", 512, U8), ("qv", 128, F8), ("sv", 128, U8),
+        ("qu", 128, F8), ("su", 128, U8), ("qp", 384, F8), ("sp", 384, U8), ("qv", 128, F8), ("sv", 128, U8),
         ("qw", 512, F8), ("sw", 512, U8), ("qe", 512, F8), ("se", 512, U8), ("qk", 128, F8), ("sk", 128, U8),
-        ("qy", 128, F8), ("sy", 128, U8), ("qh", 128, F8), ("sh", 128, U8),
-        ("zt", 640, BF), ("et", 516, BF), ("bk", 512, BF), ("wt", 512, BF), ("on", RL, BF),
-        ("pi", 8, I32), ("ii", 8, I32), ("cf", 16, F32), ("ul", 24, F32), ("ul16", 32, U16),
-        ("rt", C, BF), ("kp", C, BF), ("k2", C, BF), ("k16", C, BF), ("cw", 2 * C, BF), ("cx", 3 * C, BF),
-        ("p24", 24, F32), ("c24", 24 * 7, F32),
-        ("ca", 152, F32), ("jt", C, F32), ("jc", NT, F32), ("jq", NT, F32), ("nt", M, F32),
-        ("d1", C, F32), ("sj", C, F32), ("sg", 6 * C, BF), ("jk", 128 * NT, BF), ("spc", 96, BF), ("rs", NT, F32), ("rd", C, BF),
-        ("rl", 32 * RL, BF), ("rdj", NT, F32), ("pre", 2 * NT, F32), ("cs", C, F32), ("pl", NT, F32), ("pl16", NT, U16),
-        ("m1", C, BF), ("val", C, F32), ("srt", 296, F32), ("so", 320, F32),
-        ("ni", 12, I32), ("nj", 12, I32), ("nl16", 12, U16), ("f4", 4 * FS, BF), ("fs", 2 * C, BF),
-        ("ga", 8 * M, BF), ("zh", 4 * M, BF), ("yt", 512, BF), ("ht", 512, BF), ("hp", 4 * M, BF), ("hg", 2 * C, BF),
-        ("col", 2 * C, BF), ("co", 2 * C, BF), ("ab", 2 * NT, F32), ("ar", 2 * NT, F32), ("b4", 2 * NT, F32),
-        ("b3", NT, F32), ("b5", NT, F32), ("zz", NT, F32), ("dd", NT, F32), ("bit", 2 * NT, F32), ("nn", 2 * NT, F32),
-        ("lh", 2 * NT, F32), ("lh16", 2 * NT, U16),
-        ("vs", M, F32), ("g1", C, F32), ("kc", 2 * C, BF), ("wl", 2 * C, BF), ("ns", 2 * C, BF), ("n16", NT, U16),
-        ("ndu", C, F32), ("ys", C, F32)):
+        ("qn", 128, F8), ("sn", 128, U8), ("qy", 128, F8), ("sy", 128, U8), ("qh", 128, F8), ("sh", 128, U8),
+        ("lc", LAND + R * M, F8), ("ls", LAND + R * M, U8),
+        ("zt", 516, BF), ("et", 516, BF), ("en", 512, BF), ("bk", 512, BF), ("wt", 128, BF),
+        ("pi", 8, I32), ("ii", 8, I32), ("cf", 24, F32), ("ul", 16, F32), ("ul16", 24, U16),
+        ("rt", 32, BF), ("k32", 32, BF), ("q16", NT, U16), ("kp", C, BF), ("k2", C, BF), ("cw", C, BF), ("kx", 80, BF),
+        ("p24", 24, F32), ("c24", 24 * 6, F32),
+        ("ca", 176, F32), ("jt", C, F32), ("jc", NT, F32), ("jq", NT, F32), ("nt", M, F32),
+        ("d1", C, F32), ("sj", C, F32), ("sg", 4 * C, BF), ("rs", NT, F32), ("jk", 256 * 14, BF),
+        ("rl", 32 * RL, BF), ("pre", NT, F32), ("cs", C, F32), ("pl", NT, F32), ("pl16", NT, U16),
+        ("m1", C, BF), ("val", C, F32), ("srt", 320, F32), ("so", 352, F32),
+        ("ni", 14, I32), ("nj", 14, I32), ("nl16", 14, U16), ("f4", 4 * FS, BF),
+        ("zh", 4 * (M + 4), BF), ("yt", 512, BF), ("ht", 512, BF), ("hp", 4 * M, BF), ("hg", 4 * C, BF),
+        ("col", C, BF), ("co", 2 * C, BF), ("ab", 2 * NT, F32), ("ar", 2 * NT, F32), ("zz", 2 * NT, F32), ("b4", 2 * NT, F32),
+        ("dd", NT, F32), ("bit", 2 * NT, F32), ("nn", 2 * NT, F32), ("lh", 2 * NT, F32), ("lh16", 2 * NT, U16),
+        ("vs", M, F32), ("g1", C, F32), ("n16", NT, U16), ("ndu", C, F32), ("ys", C, F32)):
     _buf(_n, _w, _t)
+SCRATCH["ga"] = ("sbuf", [128, 16 * LIST[1][1], 4], BF)
+for _n in ("kc", "wl", "ns"):
+    _buf(_n, 2 * C, BF)
 for _w in range(4):
-    _buf("gt%d" % _w, 4 * GW[_w], BF)
-    _buf("qg%d" % _w, GW[_w], F8)
-    _buf("sg%d" % _w, GW[_w], U8)
-for _r in range(R):
-    _buf("lc%d" % _r, M + 128, F8)
-    _buf("ls%d" % _r, M + 128, U8)
+    _buf("gt%d" % _w, 4 * (GW[_w] + 32 * (_w == XT)), BF)
+    _buf("qg%d" % _w, GW[_w] + 160, F8)
+    _buf("sg%d" % _w, GW[_w] + 160, U8)
 for _b in range(8):
     _buf("p%d" % _b, 512, F32, "psum")
 
@@ -68,7 +76,9 @@ def rank_program(g, core, T, topo):
     nxt = T.cores[(rank + 1) % len(T.cores)]
     rid, pid = topo.addr(nxt, core)
     mask = topo.mask(core, nxt)
-    ne = len(topo.engines(core, nxt))
+    engines = topo.engines(core, nxt)
+    ne = len(engines)
+    halves = [sum(1 << e for e in engines[k::2]) for k in range(2)]
     V, S, P = g.vector, g.scalar, g.tensor
     queue = {"v": V, "a": S, "t": P, "g": g, "s": g.sync}
     count, known, snap, last, readers = {}, {e: {} for e in queue}, {}, {}, {}
@@ -84,8 +94,7 @@ def rank_program(g, core, T, topo):
     def op(e, call, rd, wr, sem=None):
         need = []
         for x in rd:
-            if x in last:
-                need.append(last[x])
+            need.append(last[x])
             if x[0] == "P":
                 need += [(s, n) for s, n in readers.get(x, {}).items() if s != e]
         for x in wr:
@@ -144,143 +153,200 @@ def rank_program(g, core, T, topo):
         else:
             op("g", lambda: g.iota(out, pat, base, mult), [], wr)
 
+    def zeros(out, n, wr):
+        iota(out, [[0, n]], 0, 0, wr)
+
     def select(out, a, pat, cmp, x, base, mult, rd, wr):
         op("g", lambda: g.affine_select(out, a, pat, cmp, x, base, mult), rd, wr)
 
     def words(name, a, b):
         return T[name][:, a:b].bitcast(dt.uint32)
 
-    def pick_u(a, b, lst):
-        off = T.ul16[:, a // 16:b // 16]
-        op("v", lambda: V.tensor_copy(words("qp", a, b), words("qu", 0, 128).indirect(off)), ["qu", lst], ["qp%d" % a])
-        act(T.sp[:, a:b], T.su[:, 0:128].indirect(off), F.Copy, ["qu", lst], ["sp%d" % a])
+    def pick_codes(a, lst):
+        op("v", lambda: V.tensor_copy(words("qp", a, a + 128), words("qu", 0, 128).indirect(T.ul16[:, a // 16:a // 16 + 8])),
+           ["qu", lst], ["qp%d" % a])
 
-    U0, UC, U1, U2 = 0, 128, 256, 384
-    UA, UB = ["qp0", "sp0"], ["qp128", "sp128"]
+    def pick_scales(a, lst):
+        act(T.sp[:, a:a + 128], T.su[:, 0:128].indirect(T.ul16[:, a // 16:a // 16 + 8]), F.Copy, ["qu", lst], ["sp%d" % a])
+
+    U0, UC, UD = 0, 128, 256
+    UU = {a: ["qp%d" % a, "sp%d" % a] for a in (U0, UC, UD)}
     QX = ["qxa", "qxb"]
+    ENDS = T.rl[:, 32 * (RL - 1):32 * (RL - 1) + NT]
+
+    def slot(t):
+        if t in EXT:
+            w, e, a = XT, EXT.index(t), 4 * GW[XT]
+        else:
+            w, e, a = [(w, k.index(t), 0) for w, k in enumerate(TILES) if t in k][0]
+        return "g%d" % t, T["gt%d" % w], a + e
+
+    def rows_of(w):
+        return ["g%d" % t for t in TILES[w] + (EXT if w == XT else ())]
+
+    def pad(w):
+        a, b = 64 * min(TILES[w]), 4 * (GW[w] + 32 * (w == XT))
+        if w:
+            zeros(T["gt%d" % w][:, a:b], b - a, rows_of(w))
+        else:
+            fill(T.gt0[:, a:4 * GW[0]], 0.0, ["g%d" % t for t in TILES[0]] + ["z0"])
+
+    def quant_e(b):
+        quant("qe", "se", 128 * b, 128 * b + 128, T.et[:, 3 - b:515 - b], ["et"], ["qe%d" % b])
+
+    def spread(a, b):
+        act(T.ca[:, a:b], T.ca[:, 0:b - a], F.Copy, ["ca"], ["ca"])
 
     op("a", lambda: S.dma_start(T.ut[:], T.u[:]), [], ["ut"], sem="lu")
-    op("s", lambda: g.sync.dma_start(T.xt[:, 4 * CA:], T.x[:, 4 * CA:]), [], ["x0a"], sem="lxa")
-    op("s", lambda: g.sync.dma_start(T.xt[:, 0:4 * CA], T.x[:, 0:4 * CA]), [], ["x0b"], sem="lxb")
+    op("s", lambda: g.sync.dma_start(T.xt[:, 4 * CA:], T.x[:, 4 * CA:]), [], ["x%da" % e for e in range(4)], sem="lxa")
+    op("s", lambda: g.sync.dma_start(T.xt[:, 0:4 * CA], T.x[:, 0:4 * CA]), [], ["x%db" % e for e in range(4)], sem="lxb")
     wait("s", last["x0b"])
     op("s", lambda: g.sync.dma_start(T.qw[:].bitcast(dt.uint8), T.wc[:]), [], [], sem="lw")
     op("s", lambda: g.sync.dma_start(T.sw[:], T.ws[:]), [], ["qw"], sem="lw")
     op("s", lambda: g.sync.dma_start(T.vt[:], T.v[:]), [], ["vt"], sem="lv")
-
-    fill(T.zt[:], 0.0, ["zt"])
-    fill(T.wt[:], 1.0 / LIFT, ["wt"])
-    fill(T.k2[:], 0.0, ["k2"])
-    iota(T.pi[:, 0:1], [[0, 1]], 0, 1, ["pi"], small=False)
-    iota(T.ul[:], [[1, 3], [16, 8]], 0, 0, ["ul"])
-    iota(T.rt[:], [[0, NT], [1, 16]], 0, 0, ["rt"])
-    iota(T.p24[:], [[1, 24]], 24, 0, ["p24"])
-    select(T.et[:], T.zt[:, 0:516], [[-1, 516]], A.not_equal, 1.0, 3, 4, ["zt"], ["et"])
     p1 = T.pi[:, 0:1]
+    cq, ch, cc, cpar, cfl = [T.cf[:, k:k + 1] for k in range(5)]
+    h6, sig, mb, low, stp, cya, cyb, cdb, csh, own, ow1, ow2 = [T.cf[:, k:k + 1] for k in range(5, 17)]
+    c0, c1, c2, c3, c4, c5 = [T.c24[:, 24 * k:24 * k + 24] for k in range(6)]
+    fill(T.zt[:], 0.0, ["zt"])
+    iota(T.pi[:, 0:1], [[0, 1]], 0, 1, ["pi"], small=False)
+    fill(T.et[:], 0.0, ["et"])
+    iota(T.rt[:], [[0, 2], [1, 16]], 0, 0, ["rt"])
+    iota(T.ul[:], [[1, 2], [16, 8]], 0, 0, ["ul"])
+    select(T.et[:, 3:515:4], T.zt[:, 0:128], [[-1, 128]], A.not_equal, 1.0, 0, 1, ["zt", "et"], ["et"])
+    act(T.wt[:], T.zt[:, 0:128], F.Identity, ["zt"], ["wt"], bias=1.0 / LIFT)
+    act(T.wt[:, 15:128:16], T.zt[:, 0:8], F.Identity, ["zt", "wt"], ["wt"], bias=1.0)
+    act(T.en[:], T.zt[:, 0:512], F.Copy, ["zt"], ["en"])
+    select(T.wt[:], T.wt[:], [[-16, 8], [0, 16]], A.is_ge, 0.0, 0, 1, ["wt"], ["wt"])
+    select(T.en[:, 0:512:4], T.zt[:, 0:128], [[-1, 128]], A.not_equal, -1.0, 0, 1, ["zt", "en"], ["en"])
+    select(T.wt[:], T.wt[:], [[16, 8], [0, 16]], A.is_ge, 0.0, 15, -1, ["wt"], ["wt"])
+    iota(T.p24[:], [[1, 24]], 24, 0, ["p24"])
+    pad(2)
+    pad(1)
+    zeros(T.rs[:], NT, ["rs%d" % t for t in range(1, NT)])
+    iota(T.jc[:], [[-16, NT]], MID - 15, 0, ["jc"])
+    zeros(T.gt0[:, 4 * GW[0]:], 128, ["g%d" % t for t in EXT])
+    pad(3)
+    iota(T.jt[:], [[1, C]], MARK, 0, ["jt"])
+    for k in range(FZ):
+        zeros(T.f4[:, k:4 * FS:FS], 4, ["f4z%d" % k])
+    zeros(T.yt[:, 4 * M:512], 128, ["ytz"])
+    zeros(T.ht[:, 4 * M:512], 128, ["htz"])
+    zeros(T.wl[:], 2 * C, ["wla", "wlb", "wll"])
+    iota(T.nt[:], [[1, M]], 0, 0, ["nt"])
+
+    fill(T.k2[:], 0.0, ["k2"])
     ts(T.ii[:, 0:1], p1, 15, A.bitwise_and, ["pi"], ["i0"])
     ts(T.ii[:, 1:2], p1, 2, A.arith_shift_right, ["pi"], ["i1"], 3, A.bitwise_and)
     ts(T.ii[:, 2:3], p1, 1, A.arith_shift_right, ["pi"], ["i2"], 1, A.bitwise_and)
     ts(T.ii[:, 3:4], p1, 2, A.arith_shift_right, ["pi"], ["i3"], 1, A.bitwise_and)
     ts(T.ii[:, 4:5], p1, 1, A.bitwise_and, ["pi"], ["i4"])
-    for e in range(4):
-        fill(T.wt[:, 60 + e:512:64], 1.0, ["wt%d" % e], ["wt"])
-    cp(T.cf[:, 0:5], T.ii[:, 0:5], ["i0", "i1", "i2", "i3", "i4"], ["cf"])
-    cq, ch, cc, cpar, cfl = [T.cf[:, k:k + 1] for k in range(5)]
-    cq1, h6, sig, mb, low, stp = [T.cf[:, k:k + 1] for k in range(5, 11)]
-    cp(T.ul16[:, 0:8], T.ul[:, 0:8], ["ul"], ["ul0"])
     fill(T.k2[:, 0:C:16], -4 * BIG, ["k2"])
-    cp(T.ul16[:, 16:32], T.ul[:, 8:24], ["ul"], ["ul2"])
-    fill(T.rs[:], 0.0, ["rs%d" % t for t in range(NT)])
-    ts(T.kp[:], T.rt[:], cq, A.not_equal, ["rt", "cf"], ["kp"], BIG, A.mult)
+    cp(T.ul16[:, 0:8], T.ul[:, 0:8], ["ul"], ["ul0"])
+    cp(T.cf[:, 0:5], T.ii[:, 0:5], ["i0", "i1", "i2", "i3", "i4"], ["cf"])
+    quant("qg%d" % XT, "sg%d" % XT, GW[XT] + 32, GW[XT] + 160, T.zt[:, 0:512], ["zt"], ["qgz"])
+    quant("qg1", "sg1", GW[1], GW[1] + 128, T.zt[:, 0:512], ["zt"], ["qgz1"])
+    ts(T.q16[:], T.zt[:, 0:NT], cq, A.add, ["zt", "cf"], ["q16"])
+    ts(T.k32[:], T.rt[:], cq, A.not_equal, ["rt", "cf"], ["k32"], BIG, A.mult)
+    act(h6, ch, F.Identity, ["cf"], ["h6"], scale=-6.0)
+    act(stp, cfl, F.Identity, ["cf"], ["stp"], scale=-2 * STEP, bias=STEP - JUMP)
     ts(T.ul16[:, 8:16], T.ul[:, 8:16], cpar, A.add, ["ul", "cf"], ["ul1"])
-    select(T.bk[:], T.wt[:], [[-16, 8], [0, 64]], A.is_ge, 0.0, 0, 1, ["wt%d" % e for e in range(4)], ["bk"])
-    select(T.bk[:], T.bk[:], [[16, 8], [0, 64]], A.is_ge, 0.0, 15, -1, ["bk"], ["bk"])
-    iota(T.jc[:], [[16, NT]], 15, 0, ["jc"])
-    iota(T.jt[:], [[1, C]], MARK, 0, ["jt"])
-    iota(T.rl[:, 32 * (RL - 1):], [[0, 32]], 0, 0, ["rl%d" % t for t in SUM_V])
-    for b in range(4):
-        iota(T.f4[:, FS * b:FS * b + FZ], [[0, FZ]], 0, 0, ["f4z%d" % b])
-    iota(T.yt[:, 4 * M:512], [[0, 128]], 0, 0, ["ytz"])
-    iota(T.ht[:, 4 * M:512], [[0, 128]], 0, 0, ["htz"])
-    iota(T.nt[:], [[1, M]], 0, 0, ["nt"])
-
-    for w in range(4):
-        n = 4 * GW[w] - 64 * TILES[w][3]
-        act(T["gt%d" % w][:, 4 * GW[w] - n:], T.zt[:, 0:n], F.Copy, ["zt"], ["g%d.%d" % (w, e) for e in range(4)])
-    act(h6, ch, F.Identity, ["cf"], ["h6"], scale=6.0)
-    act(cq1, cq, F.Identity, ["cf"], ["cq1"], bias=1.0)
-    act(stp, cfl, F.Identity, ["cf"], ["stp"], scale=-2 * STEP, bias=STEP)
-
+    for b in (1, 2, 3):
+        quant_e(b)
+    act(T.kx[:, 0:32], T.k32[:], F.Sign, ["k32"], ["kx"])
+    act(T.kp[:], T.k32[:, 0:16].indirect(T.q16[:]), F.Copy, ["k32", "q16"], ["kp"])
+    act(T.kx[:, 32:64], T.kx[:, 0:32], F.Identity, ["kx"], ["kxo"], scale=1.0 - LIFT, bias=LIFT)
     quant("qu", "su", 0, 128, T.ut[:], ["ut"], ["qu"])
-    c0, c1, c2, c3, c4, c5, c6 = [T.c24[:, 24 * k:24 * k + 24] for k in range(7)]
-    ts(T.cx[:, 0:C], T.rt[:], cq, A.not_equal, ["rt", "cf"], ["cxa"])
-    ts(c0, T.p24[:], h6, A.subtract, ["p24", "h6"], ["c0"])
-    pick_u(0, 128, "ul0")
+    quant_e(0)
+    pick_codes(U0, "ul0")
+    pick_scales(U0, "ul0")
+    pick_scales(UC, "ul1")
+    for e in range(4):
+        act(T.bk[:, e:512:4], T.wt[:], F.Copy, ["wt"], ["bk%d" % e])
+    act(c0, T.p24[:], F.Identity, ["p24", "h6"], ["c0"], bias=h6)
+    act(sig, cc, F.Identity, ["cf"], ["sig"], scale=2.0, bias=-1.0)
+    act(mb, cc, F.Identity, ["cf"], ["mb"], scale=-2 * TINY, bias=TINY)
 
-    def later_constants():
-        ts(c1, c0, 24.0, A.is_ge, ["c0"], ["c1"], -24.0, A.mult)
-        ts(T.cx[:, C:2 * C], T.rt[:], cq1, A.is_equal, ["rt", "cq1"], ["cxb"], LIFT, A.mult)
-        pick_u(128, 256, "ul1")
-        act(sig, cc, F.Identity, ["cf"], ["sig"], scale=2.0, bias=-1.0)
-        act(mb, cc, F.Identity, ["cf"], ["mb"], scale=-2 * TINY, bias=TINY)
-        act(T.on[:], T.zt[:, 0:RL], F.Identity, ["zt"], ["on"], bias=1.0)
-        act(T.k16[:], T.rt[:], F.Sign, ["rt"], ["k16"])
-        tt(c2, c0, c1, A.add, ["c0", "c1"], ["c2"])
-        tt(T.cw[:, 0:C], T.cx[:, 0:C], T.cx[:, C:2 * C], A.max, ["cxa", "cxb"], ["cw"])
-        yield
-        ts(c4, c2, 11.0, A.is_equal, ["c2"], ["c4"], JUMP, A.mult)
-        ts(c5, c2, 23.0, A.is_equal, ["c2"], ["c5"], DROP, A.mult)
-        ts(c3, c2, 10.0, A.is_le, ["c2", "stp"], ["c3"], stp, A.mult)
-        yield
-        for b in (1, 2):
-            quant("qe", "se", 128 * b, 128 * b + 128, T.et[:, 3 - b:515 - b], ["et"], ["qe%d" % b])
-        tt(c6, c4, c5, A.add, ["c4", "c5"], ["c6"])
-        yield
-        for b in (3, 0):
-            quant("qe", "se", 128 * b, 128 * b + 128, T.et[:, 3 - b:515 - b], ["et"], ["qe%d" % b])
-        tt(T.ca[:, 0:24], c6, c3, A.add, ["c6", "c3"], ["ca"])
-        yield
+    FIRST = {
+        "scores a": [lambda: tt(T.kx[:, 64:80], T.kx[:, 16:32], T.kx[:, 47:63], A.mult, ["kx", "kxo"], ["cw16"]),
+                     lambda: pick_codes(UC, "ul1"),
+                     lambda: act(T.cw[:], T.kx[:, 64:80].indirect(T.q16[:]), F.Copy, ["cw16", "q16"], ["cw"])],
+        "codes b": [lambda: pad(0)],
+        "wrap 1": [lambda: quant("qn", "sn", 0, 128, T.en[:], ["en"], ["qn"]),
+                   lambda: ts(c1, c0, 24.0, A.is_ge, ["c0"], ["c1"], -24.0, A.mult)],
+        "wrap 2": [lambda: quant("qk", "sk", 0, 128, T.bk[:], ["bk%d" % e for e in range(4)], ["qk"]),
+                   lambda: tt(c2, c0, c1, A.add, ["c0", "c1"], ["c2"])],
+        "sums": [lambda: ts(c3, c2, 10.0, A.is_le, ["c2", "stp"], ["c3"], stp, A.mult),
+                     lambda: ts(c4, c2, 23.0, A.is_ge, ["c2"], ["c4"], DROP - JUMP, A.mult)],
+        "pre": [lambda: tt(c5, c3, c4, A.add, ["c3", "c4"], ["c5"])],
+        "rows on Scalar": [
+            lambda: act(T.jq[:], T.jc[:], F.Identity, ["jc", "cf"], ["jq"], bias=cq),
+            lambda: act(ENDS, T.jc[:], F.Identity, ["jc", "cf"], ["rl%d" % t for t in SUM_VEC], bias=cq),
+            lambda: act(own, T.kx[:, 15:16], F.Identity, ["kx"], ["own"], scale=LIFT - 1.0, bias=float(MID))],
+    }
 
-    def slot(t):
-        w, e = [(w, k.index(t)) for w, k in enumerate(TILES) if t in k][0]
-        return "g%d.%d" % (w, e), T["gt%d" % w][:, e:64 * t:4]
+    def first(r, name):
+        for f in FIRST.get(name, ()) if r == 0 else ():
+            f()
 
     def sjc(t):
         return T.sj[:, 16 * t + 15:16 * t + 16], "sja" if 16 * t >= CA else "sjb"
 
-    def sign(t):
+    def sign(t, part):
         s, n = sjc(t)
-        k = t % 6
-        act(T.sg[:, C * k:C * k + 16 * t], T.p1[:, 0:16 * t], F.Sign, ["P1", n], ["sgn%d" % k], scale=-1.0, bias=s)
-
-    def relu(t):
-        name, view = slot(t)
-        k = t % 6
-        act(view, T.sg[:, C * k:C * k + 16 * t], F.Relu, ["sgn%d" % k], [name, "rs%d" % t], accum_out=T.rs[:, t:t + 1])
-
-    def row(t):
-        name, view = slot(t)
-        s, n = sjc(t)
-        ts(view, T.p0[:, 0:16 * t], s, A.is_lt, ["P0", n], [name])
-
-    def rowsum(t):
-        name, view = slot(t)
-        if t in SUM_V:
-            scan(T.rl[:, 32 * (RL - 16 * t) + t:32 * RL:32], T.on[:, 0:16 * t], view, A.mult, A.add, ["on", name], ["rl%d" % t])
+        k = ON_ACT.index(t)
+        if part == "b":
+            act(T.sg[:, C * k:C * k + CA], T.p1[:, 0:CA], F.Sign, ["P1", n], ["sgb%d" % k], scale=-1.0, bias=s)
         else:
-            act(T.jk[:, 128 * t:144 * t], view, F.Identity, [name], ["rs%d" % t, "jk%d" % t], accum_out=T.rs[:, t:t + 1])
+            act(T.sg[:, C * k + CA:C * k + 16 * t], T.p2[:, 0:16 * t - CA], F.Sign, ["P2", n], ["sga%d" % k], scale=-1.0, bias=s)
+
+    def relu(t, rs):
+        name, buf, a = slot(t)
+        k = ON_ACT.index(t)
+        act(buf[:, a:a + 64 * t:4], T.sg[:, C * k:C * k + 16 * t], F.Relu, ["sga%d" % k, "sgb%d" % k], [name, rs + "%d" % t],
+            accum_out=T[rs][:, t:t + 1])
+
+    def row(t, part="b"):
+        name, buf, a = slot(t)
+        s, n = sjc(t)
+        if part == "b":
+            ts(buf[:, a:a + 4 * min(CA, 16 * t):4], T.p0[:, 0:min(CA, 16 * t)], s, A.is_lt, ["P0", n], [name])
+        else:
+            ts(buf[:, a + 4 * CA:a + 64 * t:4], T.p4[:, 0:16 * t - CA], s, A.is_lt, ["P4", n, "z0"], [name + "a"])
+
+    def rowsum(t, rs=None):
+        name, buf, a = slot(t)
+        rd = [name] + [name + "a"] * (16 * t > CA)
+        if rs:
+            act(T.jk[:, 256 * t:272 * t], buf[:, a:a + 64 * t:4], F.Identity, rd, [rs + "%d" % t], accum_out=T[rs][:, t:t + 1])
+        else:
+            scan(T.rl[:, 32 * (RL - 8 * t) + t:32 * RL:32], buf[:, a:a + 32 * t:4], buf[:, a + 32 * t:a + 64 * t:4], A.add, A.add,
+                 rd + ["jq"], ["rl%d" % t], first=T.jq[:, t:t + 1])
+
+    def inside(k):
+        a, b = PART[k]
+        _, buf, e = slot(NT)
+        src, bank = (T.p4[:, 0:b - a], "P4") if k == "a" else (T.p0[:, a:b], "P0")
+        tt(buf[:, 4 * a + e:4 * b:4], src, T.sj[:, a:b], A.is_le, [bank, "sj" + k, "z0"], ["dg" + k])
 
     def pack(w):
-        quant("qg%d" % w, "sg%d" % w, 0, GW[w], T["gt%d" % w][:], ["g%d.%d" % (w, e) for e in range(4)] + ["dga"] * (w == 0), ["qg%d" % w])
+        n = GW[w] + 32 * (w == XT)
+        quant("qg%d" % w, "sg%d" % w, 0, n, T["gt%d" % w][:], rows_of(w) + ["dga", "dgb"] * (NT in TILES[w])
+              + ["g%da" % t for t in TILES[w] if t in ON_VEC and 16 * t > CA], ["qg%d" % w])
 
-    def colsum(w, start, stop):
-        mm(2, "qk", "sk", 0, "qg%d" % w, "sg%d" % w, 0, GW[w], ["qk", "qg%d" % w], start, stop)
+    def colsum(w):
+        if GW[w] > LOW:
+            mm(4, "qk", "sk", 0, "qg%d" % w, "sg%d" % w, LOW, max(GW[w], 2 * LOW), ["qk", "qg%d" % w, "qgz1"], w == 0, w == 2)
+        mm(2, "qk", "sk", 0, "qg%d" % w, "sg%d" % w, 0, LOW, ["qk", "qg%d" % w], w == 0, w == 3)
+        if w == XT:
+            mm(2, "qk", "sk", 0, "qg%d" % w, "sg%d" % w, GW[w], GW[w] + 128, ["qk", "qg%d" % w, "qgz"], False, False)
 
     def quant_x(k):
         a, b = PART[k]
         quant("qx", "sx", a, b, T.xt[:, 4 * a:4 * b], ["x%d%s" % (e, k) for e in range(4)], ["qx" + k])
 
     def marks(a, b):
-        tt(T.val[:, a:b], T.jt[:, a:b], T.m1[:, a:b], A.mult, ["m1", "jt"], ["val%d" % a])
+        scan(T.val[:, a:b], T.jt[:, a:b], T.m1[:, a:b], A.max, A.mult, ["m1", "jt"], ["val%d" % a])
 
     def wrap1(k):
         a, b = PART[k]
@@ -291,216 +357,264 @@ def rank_program(g, core, T, topo):
         a, b = PART[k]
         scan(T.sj[:, a:b], T.k2[:, a:b], T.d1[:, a:b], A.add, A.max, ["k2", "d1" + k], ["sj" + k])
 
-    def plane(b):
-        act(T.f4[:, FS * b + FZ:FS * b + FZ + C], T["p%d" % (4 + b)][:, 0:C], F.Copy, ["P%d" % (4 + b)], ["f4%d" % b], scale=0.25)
+    def planes_to_psum(bs):
+        for b in bs:
+            mm(4 + b, "qe", "se", 128 * b, "qx", "sx", 0, C, ["qe%d" % b] + QX)
 
-    def new_x(e, k):
+    def plane(b):
+        act(T.f4[:, FS * b + FZ:FS * b + FZ + C], T["p%d" % (4 + b)][:, 0:C], F.Copy, ["P%d" % (4 + b)], ["f4%d" % b])
+
+    def other_colour():
+        mm(1, "qp", "sp", UD, "qx", "sx", 0, C, UU[UD] + QX)
+        act(T.col[:], T.p1[:, 0:C], F.Sign, ["P1"], ["col"], bias=-TINY)
+
+    def colour(k, a=0, b=C):
+        scan(T.co[:, C * k + a:C * k + b], T.cw[:, a:b], (T.col if k else T.m1)[:, a:b], A.mult, A.add, ["cw", "col" if k else "m1"],
+             ["co%d.%d" % (k, a)])
+
+    def bits(k):
+        if k:
+            ts(T.bit[:, NT:], T.co[:, C + 15:2 * C:16], 0.0, A.is_gt, ["co1.0", "co1.%d" % CUT1, "cdb"], ["bit1"], cdb, A.add)
+        else:
+            ts(T.bit[:, 0:NT], T.co[:, 15:C:16], sig, A.mult, ["co0.0", "co0.%d" % MID, "sig"], ["bit0"], 0.0, A.is_gt)
+
+    def interval(k):
+        if k == 0:
+            act(T.ab[:, 0:NT], T.pl[:], F.Identity, ["pl", "cya"], ["ab0"], scale=1.0 / 3, bias=cya)
+            act(T.ab[:, NT:], T.pl[:], F.Identity, ["pl", "cyb"], ["ab1"], scale=1.0 / 3, bias=cyb)
+        elif k == 1:
+            act(T.zz[:], T.ab[:], F.Identity, ["ab0", "ab1"], ["zz"], bias=WHOLE)
+        elif k == 2:
+            act(T.ar[:], T.zz[:], F.Identity, ["zz"], ["ar"], bias=-WHOLE)
+        elif k == 3:
+            act(T.zz[:], T.ar[:], F.Relu, ["ar"], ["zz"], scale=-M / 4.0)
+        else:
+            tt(T.b4[:], T.ar[:], T.zz[:], A.add, ["ar", "zz"], ["b4"])
+
+    def new_x(e, k, gathered):
         a, b = PART[k]
         out, name = T.xt[:, 4 * a + e:4 * b:4], "x%d%s" % (e, k)
-        if e < 2:
-            tt(out, T.hp[:, M * e:M * e + M].indirect(T.n16[:, a // 16:b // 16]), T.fs[:, C * e + a:C * e + b], A.add,
-               ["hp%d" % e, "n16" + k, "fs%d" % e], [name])
+        if gathered:
+            tt(out, T["p%d" % (4 + e)][:, a:b], T.hg[:, C * e + a:C * e + b], A.add, ["P%d" % (4 + e), "hg%d%s" % (e, k)], [name])
         else:
-            tt(out, T["p%d" % (4 + e)][:, a:b], T.hg[:, C * (e - 2) + a:C * (e - 2) + b], A.add, ["P%d" % (4 + e), "hg%d%s" % (e, k)], [name])
+            tt(out, T.hp[:, M * e:M * e + M].indirect(T.n16[:, a // 16:b // 16]), T.f4[:, FS * e + FZ + a:FS * e + FZ + b], A.add,
+               ["hp%d" % e, "n16" + k, "f4%d" % e], [name])
 
-    more = later_constants()
     quant_x("a")
     for r in range(R):
-        mm(4, "qp", "sp", U0, "qx", "sx", CA, C, UA + ["qxa"])
+        for b in (4, 2):
+            mm(b, "qp", "sp", U0, "qx", "sx", CA, C, UU[U0] + ["qxa"])
         if r == 0:
-            next(more)
-        quant_x("b")
-        wrap1("a")
-        mm(0, "qp", "sp", U0, "qx", "sx", 0, CB, UA + QX)
-        mm(1, "qp", "sp", U0, "qx", "sx", 0, C - 16, UA + QX)
-        mm(3, "qp", "sp", UC, "qx", "sx", 0, C, UB + QX)
-        if r == 0:
-            next(more)
+            first(r, "scores a")
+            quant_x("b")
+            first(r, "codes b")
+            wrap1("a")
+        else:
+            wrap1("a")
+            quant_x("b")
+        for b in (0, 1):
+            mm(b, "qp", "sp", U0, "qx", "sx", 0, CA, UU[U0] + ["qxb"])
+        mm(3, "qp", "sp", UC, "qx", "sx", 0, C, UU[UC] + QX)
+        first(r, "wrap 1")
         wrap2("a")
-        if r == 0:
-            next(more)
+        first(r, "wrap 2")
+        for t in ON_ACT:
+            sign(t, "a")
+        inside("a")
+        for t in ON_VEC:
+            if 16 * t > CA:
+                row(t, "a")
+        first(r, "inside a")
         wrap1("b")
-        tt(T.gt0[:, 4 * CA:4 * C:4], T.p4[:, 0:C - CA], T.sj[:, CA:], A.is_le, ["P4", "sja"], ["dga"])
-        row(13)
+        row(ON_VEC[0])
+        row(ON_VEC[1])
         wrap2("b")
-        row(12)
-        row(11)
-        row(10)
-        if r == 0:
-            next(more)
-        for b in (1, 2, 3, 0):
-            mm(4 + b, "qe", "se", 128 * b, "qx", "sx", 0, C, ["qe%d" % b] + QX)
+        first(r, "wrap b")
+        planes_to_psum((1, 2))
+        rs, left = "rs", list(SUM_VEC)
+        by_act = ON_VEC[len(left):]
         for k, t in enumerate(ON_ACT):
-            sign(t)
-            if k:
-                relu(ON_ACT[k - 1])
-        relu(ON_ACT[-1])
-        act(T.m1[:], T.p3[:, 0:C], F.Sign, ["P3", "sig", "mb"], ["m1"], scale=sig, bias=mb)
-        tt(T.gt0[:, 0:4 * CA:4], T.p0[:, 0:CA], T.sj[:, 0:CA], A.is_le, ["P0", "sjb"], ["g0.0"])
-        for t in range(9, 2, -1):
-            row(t)
-        ts(T.spc[:, 0:32], T.p0[:, 16:48], sjc(0)[0], A.is_le, ["P0", "sjb"], ["spc0"])
-        ts(T.spc[:, 32:48], T.p0[:, 0:16], sjc(1)[0], A.is_lt, ["P0", "sjb"], ["spc1"])
-        ts(T.spc[:, 48:64], T.p0[:, 32:48], sjc(1)[0], A.is_le, ["P0", "sjb"], ["spc1b"])
-        ts(T.spc[:, 64:96], T.p0[:, 0:32], sjc(2)[0], A.is_lt, ["P0", "sjb"], ["spc2"])
-        if r == 0:
-            quant("qk", "sk", 0, 128, T.bk[:], ["bk"], ["qk"])
-            ts(T.jq[:], T.jc[:], 47.0, A.max, ["jc", "cf"], ["jq"], cq, A.subtract)
-        scan(T.rd[:], T.k16[:], T.gt0[:, 0:4 * C:4], A.mult, A.add, ["k16", "g0.0", "dga"], ["rd"])
-        for w in (0, 2, 3):
-            pack(w)
-            colsum(w, w == 0, False)
-        tt(T.rdj[:], T.jq[:], T.rd[:, 15:C:16], A.subtract, ["rd", "jq"], ["rdj"])
-        pack(1)
-        colsum(1, False, True)
-        for t in range(13, 2, -1):
+            sign(t, "b")
+            if k > 1:
+                relu(ON_ACT[k - 2], rs)
+        for t in ON_ACT[-2:]:
+            relu(t, rs)
+        first(r, "rows on Scalar")
+        for x in ORDER:
+            if x == "in":
+                inside("b")
+            elif x == "s":
+                rowsum(left.pop(0))
+            elif x[0] == "p":
+                pack(int(x[1]))
+                first(r, x)
+                if x == "p1":
+                    mm(4, "qn", "sn", 0, "qg0", "sg0", LOW, C, ["qn", "qg0"], False, False)
+                    mm(2, "qn", "sn", 0, "qg0", "sg0", 0, LOW, ["qn", "qg0"], False, False)
+                colsum(int(x[1]))
+            else:
+                row(int(x))
+        for t in left:
             rowsum(t)
-        for k in range(3):
-            act(T.jk[:, 128 * k:128 * k + 32], T.spc[:, 32 * k:32 * k + 32], F.Identity,
-                ["spc%d" % k] + (["spc1b"] if k == 1 else []), ["rs%d" % k, "jk%d" % k], accum_out=T.rs[:, k:k + 1])
+        for t in by_act:
+            rowsum(t, rs)
+        act(T.m1[:], T.p3[:, 0:C], F.Sign, ["P3", "sig", "mb"], ["m1"], scale=sig, bias=mb)
+        if r:
+            other_colour()
+        planes_to_psum((3,))
+        first(r, "sums")
+        scan(T.cs[:, LOW:], T.cw[:, LOW:], T.p4[:, 0:C - LOW], A.mult, A.add, ["cw", "P4"], ["cs1"])
+        planes_to_psum((0,))
+        scan(T.cs[:, 0:LOW], T.cw[:, 0:LOW], T.p2[:, 0:LOW], A.mult, A.add, ["cw", "P2"], ["cs"])
+        tt(T.pre[:], ENDS, T[rs][:], A.add, [rs + "%d" % t for t in list(ON_ACT) + by_act] + ["rl%d" % t for t in SUM_VEC], ["pre"])
+        first(r, "pre")
+        marks(0, CUT)
+        tt(T.pl[:], T.cs[:, 15:C:16], T.pre[:], A.subtract, ["pre", "cs", "cs1"], ["pl"])
+        marks(CUT, C)
+        colour(0, 0, MID)
+        ts(T.pl16[:], T.pl[:], own, A.add, ["pl", "own"], ["pl16"])
+        colour(0, MID, C)
+        if r:
+            colour(1, 0, CUT1)
+        else:
+            ts(T.ul16[:, 16:24], T.ul[:, 8:16], cpar, A.subtract, ["ul", "cf"], ["ul2"], 1.0, A.add)
+            ts(low, cq, 15.0, A.is_equal, ["cf"], ["low"], 1.0 / LIFT, A.max)
+        cp(T.srt[:, 0:C].indirect(T.pl16[:]), T.val[:], ["pl16", "val0", "val%d" % CUT], ["srt"])
         if r == 0:
-            for a, b in ((24, 48), (48, 96), (96, HALF)):
-                act(T.ca[:, a:b], T.ca[:, 0:b - a], F.Copy, ["ca"], ["ca"])
-            act(T.cw[:, C:], T.cw[:, 0:C], F.Copy, ["cw"], ["cwb"])
-        marks(0, 96)
-        tt(T.pre[:, 0:NT], T.rdj[:], T.rl[:, 32 * (RL - 1):32 * (RL - 1) + NT], A.subtract, ["rdj"] + ["rl%d" % t for t in SUM_V], ["pre0"])
-        scan(T.cs[:], T.cw[:, 0:C], T.p2[:, 0:C], A.mult, A.add, ["cw", "P2"], ["cs"])
-        tt(T.pre[:, NT:], T.pre[:, 0:NT], T.rs[:], A.subtract, ["rs%d" % t for t in range(NT)] + ["pre0"], ["pre"])
-        marks(96, 192)
-        tt(T.pl[:], T.pre[:, NT:], T.cs[:, 15:C:16], A.add, ["pre", "cs"], ["pl"])
-        marks(192, C)
-        cp(T.pl16[:], T.pl[:], ["pl"], ["pl16"])
-        if r == 0:
-            pick_u(256, 384, "ul2")
-        cp(T.srt[:, 0:C].indirect(T.pl16[:]), T.val[:], ["pl16", "val0", "val96", "val192"], ["srt"])
-        if r == 0:
-            pick_u(384, 512, "ul2")
-        mm(0, "qp", "sp", U1, "qx", "sx", 0, C, ["qp256", "sp256"] + QX)
-        mm(1, "qp", "sp", U2, "qx", "sx", 0, C, ["qp384", "sp384"] + QX)
-        plane(0)
-        act(T.ab[:, 0:NT], T.pl[:], F.Identity, ["pl"], ["ab0"], scale=1.0 / 12, bias=-5.5 / 12)
-        act(T.ab[:, NT:], T.pl[:], F.Identity, ["pl"], ["ab1"], scale=1.0 / 12, bias=-11.5 / 12)
-        plane(1)
-        act(T.ar[:], T.ab[:], F.Identity, ["ab0", "ab1"], ["ar"], bias=WHOLE)
-        plane(2)
-        act(T.b3[:], T.ar[:, NT:], F.Identity, ["ar"], ["b3"], bias=-WHOLE)
-        act(T.b4[:, 0:NT], T.ar[:, 0:NT], F.Identity, ["ar"], ["b40"], scale=4.0, bias=-4 * WHOLE)
-        plane(3)
-        act(T.b5[:], T.b3[:], F.Identity, ["b3"], ["b5"], scale=4.0, bias=2.0)
-        act(T.zz[:], T.b3[:], F.Relu, ["b3"], ["zz"], scale=-float(M))
-        act(T.col[:, 0:C], T.p0[:, 0:C], F.Sign, ["P0"], ["col0"], bias=-TINY)
-        act(T.col[:, C:], T.p1[:, 0:C], F.Sign, ["P1"], ["col1"], bias=-TINY)
-        cp(T.srt[:, C:C + 6], T.srt[:, 0:6], ["srt"], ["srt6"])
-        for h in range(2):
-            scan(T.so[:, 160 * h:160 * h + HALF], T.srt[:, 144 * h:144 * h + HALF], T.ca[:, 0:HALF], A.max, A.add,
+            plane(1)
+            act(T.ca[:, 0:24], c5, F.Identity, ["c5"], ["ca"], bias=JUMP)
+            for b, n in ((2, 24), (3, 48), (0, 96)):
+                plane(b)
+                spread(n, min(2 * n, HALF[1]))
+            act(T.kc[:, 0:2 * C:2], T.kx[:, 0:16].indirect(T.q16[:]), F.Copy, ["kx", "q16"], ["kc"])
+            act(T.kc[:, 1:2 * C:2], T.kx[:, 32:48].indirect(T.q16[:]), F.Copy, ["kxo", "q16"], ["kco", "kcd"])
+            pick_codes(UD, "ul2")
+        else:
+            for k, b in enumerate((1, 2, 3, 0)):
+                plane(b)
+                interval(k)
+            colour(1, CUT1, C)
+        cp(T.srt[:, C:C + HALF[1] - MID], T.srt[:, 0:HALF[1] - MID], ["srt"], ["srt6"])
+        for h, n in enumerate(HALF):
+            scan(T.so[:, 176 * h:176 * h + n], T.srt[:, MID * h:MID * h + n], T.ca[:, 0:n], A.max, A.add,
                  ["srt", "ca"] + ["srt6"] * h, ["so%d" % h], first=DROP)
-        for h in range(2):
-            tt(T.ni[:, 6 * h:6 * h + 6], T.so[:, 160 * h + 20:160 * h + HALF:24], T.so[:, 160 * h + 29:160 * h + HALF:24], A.max,
-               ["so%d" % h], ["ni%d" % h])
-        if r == 0:
-            ts(T.cx[:, 2 * C:], T.rt[:], cq, A.is_equal, ["rt", "cf"], ["cxc"], LIFT, A.mult)
-        for h in range(2):
-            ts(T.nj[:, 6 * h:6 * h + 6], T.ni[:, 6 * h:6 * h + 6], int(STEP) - 1, A.bitwise_and, ["ni%d" % h], ["nj%d" % h])
-        if r == 0:
-            cp(T.kc[:, 0:2 * C:2], T.cx[:, 0:C], ["cxa"], ["kc"])
-        for h in range(2):
-            ts(T.nl16[:, 6 * h:6 * h + 6], T.nj[:, 6 * h:6 * h + 6], float(FO), A.subtract, ["nj%d" % h], ["nl%d" % h])
-        for h in range(2):
-            for b in range(4):
-                out, src = T.ga[:, M * (2 * b + h):M * (2 * b + h + 1)], T.f4[:, FS * b:FS * b + FZ + C].indirect(T.nl16[:, 6 * h:6 * h + 6])
-                rd, wr = ["f4%d" % b, "f4z%d" % b, "nl%d" % h], ["ga%d%d" % (b, h)]
-                if b < 2:
-                    cp(out, src, rd, wr)
-                else:
-                    act(out, src, F.Copy, rd, wr)
-        scan(T.co[:, 0:C], T.cw[:, 0:C], T.col[:, 0:C], A.mult, A.add, ["cw", "col0"], ["co0"])
-        for b in range(4):
-            tt(T.zh[:, b:4 * M:4], T.ga[:, 2 * M * b:2 * M * (b + 1):2], T.ga[:, 2 * M * b + 1:2 * M * (b + 1):2], A.add,
-               ["ga%d0" % b, "ga%d1" % b], ["zh%d" % b])
-        scan(T.co[:, C:], T.cw[:, C:], T.col[:, C:], A.mult, A.add, ["cwb", "col1"], ["co1"])
-        tt(T.b4[:, NT:], T.b5[:], T.zz[:], A.add, ["b5", "zz"], ["b41"])
-        ZH = ["zh%d" % b for b in range(4)]
-        tt(T.yt[:, 4 * M - 8:4 * M], T.zh[:, 4 * M - 8:4 * M], T.zh[:, 0:8], A.add, ZH, ["yt1"])
-        tt(T.yt[:, 0:4 * M - 8], T.zh[:, 0:4 * M - 8], T.zh[:, 8:4 * M], A.add, ZH, ["yt0"])
-        ts(T.bit[:], T.co[:, 15:2 * C:16], 0.0, A.is_gt, ["co0", "co1"], ["bit"])
+        for h, (a, b) in enumerate(LIST):
+            n = 176 * h + HALF[h]
+            tt(T.ni[:, a:b], T.so[:, 176 * h + 20:n:24], T.so[:, 176 * h + 29:n:24], A.max, ["so%d" % h], ["ni%d" % h])
+        for h, (a, b) in enumerate(LIST):
+            ts(T.nj[:, a:b], T.ni[:, a:b], int(STEP) - 1, A.bitwise_and, ["ni%d" % h], ["nj%d" % h])
+        for h, (a, b) in enumerate(LIST):
+            ts(T.nl16[:, a:b], T.nj[:, a:b], float(FO), A.subtract, ["nj%d" % h], ["nl%d" % h], 0.0, A.max)
+        for h, (a, b) in enumerate(LIST):
+            for e in range(2):
+                for x in (e, e + 2):
+                    out, src = T.ga[:, 16 * a:16 * b, x], T.f4[:, FS * x:FS * x + FZ + C].indirect(T.nl16[:, a:b])
+                    rd, wr = ["f4%d" % x, "nl%d" % h] + ["f4z%d" % k for k in range(FZ)], ["ga%d%d" % (x, h)]
+                    if x < 2:
+                        ts(out, src, 0.25, A.mult, rd, wr)
+                    else:
+                        act(out, src, F.Copy, rd, wr, scale=0.25)
+        for h, (a, b) in enumerate(((0, M // 2), (M // 2, M + 2))):
+            tt(T.zh[:, 4 * a:4 * b], T.ga[:, 2 * a:2 * b:2, :], T.ga[:, 2 * a + 1:2 * b:2, :], A.add,
+               ["ga%d%d" % (x, h) for x in range(4)], ["zh%d" % h])
+        for h, (a, b) in enumerate(((0, M // 2 - 2), (M // 2 - 2, M))):
+            tt(T.yt[:, 4 * a:4 * b], T.zh[:, 4 * a:4 * b], T.zh[:, 4 * a + 8:4 * b + 8], A.add, ["zh0", "zh1"][:h + 1], ["yt%d" % h])
+        bits(0)
+        if r:
+            interval(4)
+            bits(1)
+        else:
+            quant("lc", "ls", 0, LAND, T.zt[:, 0:512], ["zt"], ["pad"])
+            pick_scales(UD, "ul2")
+            act(ow1, own, F.Identity, ["own"], ["ow1"], scale=1.0 / 3, bias=-5.5 / 3)
+            act(ow2, own, F.Identity, ["own"], ["ow2"], scale=1.0 / 3, bias=-11.5 / 3)
+            act(cdb, cpar, F.Identity, ["cf"], ["cdb"], scale=-4.0, bias=2.0)
+            act(csh, cpar, F.Identity, ["cf"], ["csh"], scale=2.0)
+            act(cya, cpar, F.Identity, ["cf", "ow1"], ["cya"], scale=-2.0, bias=ow1)
+            act(cyb, cpar, F.Identity, ["cf", "ow2"], ["cyb"], scale=2.0, bias=ow2)
+            interval(0)
+            interval(1)
+            other_colour()
+            interval(2)
+            interval(3)
         quant("qy", "sy", 0, 128, T.yt[:], ["yt0", "yt1", "ytz"], ["qy"])
         wait("g", last["qy"])
-        lc, ls, arr = "lc%d" % r, "ls%d" % r, "arr%d" % r
-        g.remote_dma(T[lc][:, 0:M].bitcast(dt.uint8), T.qy[:, 0:M].bitcast(dt.uint8), T.sem[arr], T.sem.sent, pid, rid, mask)
-        g.remote_dma(T[ls][:, 0:M], T.sy[:, 0:M], T.sem[arr], T.sem.sent, pid, rid, mask)
-        count["sent"] = 2 * ne * (r + 1)
+        at, arr = LAND + M * r, "arr%d" % r
+        masks, n = ((mask, mask), 2 * ne) if r else (halves, ne)
+        g.remote_dma(T.lc[:, at:at + M].bitcast(dt.uint8), T.qy[:, 0:M].bitcast(dt.uint8), T.sem[arr], T.sem.sent, pid, rid, masks[0])
+        g.remote_dma(T.ls[:, at:at + M], T.sy[:, 0:M], T.sem[arr], T.sem.sent, pid, rid, masks[1])
+        count["sent"] = count.get("sent", 0) + n
         snap[("sent", count["sent"])] = {"sent": count["sent"]}
         readers["qy"] = {"sent": count["sent"]}
-        snap[(arr, 2 * ne)] = {arr: 2 * ne}
-        last["land%d" % r] = (arr, 2 * ne)
-        for b in range(2):
-            act(T.fs[:, C * b:C * b + C], T["p%d" % (4 + b)][:, 0:C], F.Copy, ["P%d" % (4 + b)], ["fs%d" % b])
-        tt(T.nn[:], T.b4[:], T.bit[:], A.add, ["b40", "b41", "bit"], ["nn"])
-        quant(lc, ls, M, M + 128, T.zt[:, 0:512], ["zt"], ["pad%d" % r])
+        snap[(arr, n)] = {arr: n}
+        last["land%d" % r] = (arr, n)
         if r == 0:
-            fill(T.wl[:], 0.0, ["wla", "wlb", "wll"])
-            ts(low, cq, 15.0, A.is_equal, ["cf"], ["low"], 1.0 / LIFT, A.max)
-        tt(T.lh[:, 0:NT], T.nn[:, 0:NT], T.nn[:, NT:], A.min, ["nn"], ["lo"])
-        tt(T.lh[:, NT:], T.nn[:, 0:NT], T.nn[:, NT:], A.max, ["nn"], ["hi"])
-        if r == 0:
-            ts(T.kc[:, 1:2 * C:2], T.cx[:, 2 * C:], 1.0, A.max, ["cxc"], ["kco"])
+            colour(1, 0, CUT1)
+            colour(1, CUT1, C)
+            interval(4)
+            bits(1)
+        tt(T.nn[:], T.b4[:], T.bit[:], A.add, ["b4", "bit0", "bit1"], ["nn"])
         if r == 1:
             quant("qv", "sv", 0, 128, T.vt[:], ["vt"], ["qv"])
-        tt(T.wl[:, 31:2 * C:32], T.nn[:, 0:NT], T.nn[:, NT:], A.min, ["nn"], ["wll"])
-        tt(T.dd[:], T.lh[:, NT:], T.lh[:, 0:NT], A.subtract, ["lo", "hi"], ["dd"])
-        cp(T.lh16[:], T.lh[:], ["lo", "hi"], ["lh16"])
+        tt(T.lh[:, 0:NT], T.nn[:, 0:NT], T.nn[:, NT:], A.min, ["nn"], ["lo"])
+        tt(T.lh[:, NT:], T.nn[:, 0:NT], T.nn[:, NT:], A.max, ["nn"], ["hi"])
+        z = 128 - M
         for b in range(4):
-            mm(2 + b, "qw", "sw", 128 * b, lc, ls, 0, 128, ["qw", "land%d" % r, "pad%d" % r])
-            src, dst = T["p%d" % (2 + b)][:, 0:M], T.ht[:, b:4 * M:4]
+            mm(b, "qw", "sw", 128 * b, "lc", "ls", at - z, at + M, ["qw", "land%d" % r, "pad"])
+            src, dst = T["p%d" % b][:, z:128], T.ht[:, b:4 * M:4]
             if b % 2 == 0:
-                act(dst, src, F.Copy, ["P%d" % (2 + b)], ["ht%d" % b], scale=0.03125)
+                act(dst, src, F.Copy, ["P%d" % b], ["ht%d" % b], scale=0.03125)
             else:
-                ts(dst, src, 0.03125, A.mult, ["P%d" % (2 + b)], ["ht%d" % b])
-        ts(T.kc[:, 31:2 * C:32], T.dd[:], low, A.mult, ["dd", "low", "kco"], ["kcd"])
+                ts(dst, src, 0.03125, A.mult, ["P%d" % b], ["ht%d" % b])
+        tt(T.dd[:], T.lh[:, NT:], T.lh[:, 0:NT], A.subtract, ["lo", "hi"], ["dd"])
+        ts(T.lh16[:], T.lh[:], csh, A.add, ["lo", "hi", "csh"], ["lh16"])
+        tt(T.wl[:, 31:2 * C:32], T.nn[:, 0:NT], T.nn[:, NT:], A.min, ["nn"], ["wll"])
         quant("qh", "sh", 0, 128, T.ht[:], ["ht0", "ht1", "ht2", "ht3", "htz"], ["qh"])
-        mm(0, "qp", "sp", U0, "qh", "sh", 0, 128, UA + ["qh"])
-        for b in range(4):
-            if b < 2:
-                cp(T.hp[:, M * b:M * b + M], T.ht[:, b:4 * M:4], ["ht%d" % b], ["hp%d" % b])
-            else:
-                act(T.hp[:, M * b:M * b + M], T.ht[:, b:4 * M:4], F.Copy, ["ht%d" % b], ["hp%d" % b])
-        cp(T.vs[:], T.p0[:, 0:M], ["P0"], ["vs"])
+        mm(4, "qp", "sp", U0, "qh", "sh", 0, 128, UU[U0] + ["qh"])
+        cp(T.vs[:], T.p4[:, 0:M], ["P4"], ["vs"])
+        for b in (0, 1):
+            cp(T.hp[:, M * b:M * b + M], T.ht[:, b:4 * M:4], ["ht%d" % b], ["hp%d" % b])
+        ts(T.kc[:, 31:2 * C:32], T.dd[:], low, A.mult, ["dd", "low"], ["kcd"])
         ta = CA // 16
         cp(T.g1[:, CA:], T.vs[:].indirect(T.lh16[:, ta:NT]), ["vs", "lh16"], ["g1a"])
         act(T.g1[:, 0:CA], T.vs[:].indirect(T.lh16[:, 0:ta]), F.Copy, ["vs", "lh16"], ["g1b"])
-        for k in "ab":
+        ab = "ab" if r < R - 1 else "ba"
+        for k in ab:
             a, b = PART[k]
             tt(T.wl[:, 2 * a:2 * b:2], T.vs[:].indirect(T.lh16[:, NT + a // 16:NT + b // 16]), T.g1[:, a:b], A.is_gt,
                ["vs", "lh16", "g1" + k], ["wl" + k])
-        for k in "ab":
+        for k in ab:
             a, b = PART[k]
             scan(T.ns[:, 2 * a:2 * b], T.kc[:, 2 * a:2 * b], T.wl[:, 2 * a:2 * b], A.mult, A.add,
                  ["kc", "kco", "kcd", "wl" + k, "wll"], ["ns" + k])
-        for k in "ab":
+        for k in ab:
             a, b = PART[k]
-            cp(T.n16[:, a // 16:b // 16], T.ns[:, 2 * a + 31:2 * b:32], ["ns" + k], ["n16" + k])
-        for k in "ab":
-            a, b = PART[k]
-            for e in (2, 3):
-                act(T.hg[:, C * (e - 2) + a:C * (e - 2) + b], T.hp[:, M * e:M * e + M].indirect(T.n16[:, a // 16:b // 16]), F.Copy,
-                    ["hp%d" % e, "n16" + k], ["hg%d%s" % (e, k)])
-        for e, k in ((0, "a"), (1, "a"), (0, "b"), (2, "a"), (3, "a"), (1, "b")):
-            new_x(e, k)
-        quant_x("a")
-        new_x(2, "b")
-        new_x(3, "b")
+            ts(T.n16[:, a // 16:b // 16], T.ns[:, 2 * a + 31:2 * b:32], csh, A.add, ["ns" + k, "csh"], ["n16" + k])
+            for b in (3, 2) if k == ab[0] else ():
+                cp(T.hp[:, M * b:M * b + M], T.ht[:, b:4 * M:4], ["ht%d" % b], ["hp%d" % b])
+        for e, i in BY_ACT:
+            a, b = PART[ab[i]]
+            act(T.hg[:, C * e + a:C * e + b], T.hp[:, M * e:M * e + M].indirect(T.n16[:, a // 16:b // 16]), F.Copy,
+                ["hp%d" % e, "n16" + ab[i]], ["hg%d%s" % (e, ab[i])])
+        for e, i in AHEAD:
+            new_x(e, ab[i], (e, i) in BY_ACT)
+        quant_x(ab[0])
+        for e in range(4):
+            if (e, 1) not in AHEAD:
+                new_x(e, ab[1], (e, 1) in BY_ACT)
 
-    mm(1, "qv", "sv", 0, "qx", "sx", CA, C, ["qv", "qxa"])
+    mm(0, "qv", "sv", 0, "qx", "sx", 0, CA, ["qv", "qxb"])
     act(T.ndu[:], T.nt[:].indirect(T.n16[:]), F.Copy, ["nt", "n16a", "n16b"], ["ndu"])
     op("s", lambda: g.sync.dma_start(T.nd[:], T.ndu[0:128:16, :]), ["ndu"], [], sem="outs")
-    quant_x("b")
-    mm(0, "qv", "sv", 0, "qx", "sx", 0, CA, ["qv", "qxb"])
-    act(T.ys[:, CA:], T.p1[:, 0:C - CA], F.Copy, ["P1"], ["ysa"])
-    op("a", lambda: S.dma_start(T.y[:, CA:], T.ys[:, CA:]), ["ysa"], [], sem="outs")
-    cp(T.ys[:, 0:CA], T.p0[:, 0:CA], ["P0"], ["ysb"])
+    quant_x("a")
+    mm(1, "qv", "sv", 0, "qx", "sx", CA, C, ["qv", "qxa"])
+    act(T.ys[:, 0:CA], T.p0[:, 0:CA], F.Copy, ["P0"], ["ysb"])
+    op("a", lambda: S.dma_start(T.y[:, 0:CA], T.ys[:, 0:CA]), ["ysb"], [], sem="outs")
+    cp(T.ys[:, CA:], T.p1[:, 0:C - CA], ["P1"], ["ysa"])
     op("s", lambda: g.sync.dma_start(T.oc[:], T.qx[:].bitcast(dt.uint8)), QX, [], sem="outs")
     for k in range(4):
-        op("a", lambda: S.dma_start(T.osc[4 * k:4 * k + 4, :], T.sx[32 * k:32 * k + 4, :]), QX, [], sem="outs")
-    op("s", lambda: g.sync.dma_start(T.y[:, 0:CA], T.ys[:, 0:CA]), ["ysb"], [], sem="outs")
+        e = "as"[k % 2]
+        op(e, lambda: queue[e].dma_start(T.osc[4 * k:4 * k + 4, :], T.sx[32 * k:32 * k + 4, :]), QX, [], sem="outs")
+    op("s", lambda: g.sync.dma_start(T.y[:, CA:], T.ys[:, CA:]), ["ysa"], [], sem="outs")
     for s in ("g", "sent", "t", "a", "v", "outs"):
         wait("s", (s, count[s]))

from concourse.mybir import dt, AluOpType, ActivationFunctionType

C, M, R = 288, 96, 3
NT = C // 16
CA = 160
PART = {"a": (CA, C), "b": (0, CA)}
BIG = 2.0 ** 96
TINY = 1.0e-36
FS, FZ, FO = 304, 2, 512
STEP, JUMP, DROP = 1024.0, 65536.0, -1048576.0
MARK = 16 * 1024 + FO + FZ
HALF = (150, 174)
LIST = ((0, 6), (6, 13))
LIFT = 16384.0
WHOLE = 4 * 12582912.0
MID = C // 2
CUT, CUT1 = 176, 224
TILES = ((NT, 13, 12, 11), (10, 9, 8, 7), (17, 16, 15, 14), (6, 5, 4, 3))
XT, EXT = 0, (2, 1)
ON_ACT = TILES[2]
GW = [max(128, 16 * max(_t)) for _t in TILES]
ON_VEC = [_t for _t in range(NT - 1, 0, -1) if _t not in ON_ACT]
SUM_VEC = ON_VEC[:6]
RL = 8 * ON_VEC[0]
ORDER = "11 10 in 2 1 9 8 p0 7 6 5 4 p1 3 p2 p3".split()
BY_ACT, AHEAD = ((3, 0), (1, 1), (2, 1), (3, 1)), ((0, 0), (1, 0), (2, 0), (3, 0), (0, 1))
LOW = 128
LAND = 128

F8, U8, BF, F32, I32, U16 = "float8_e4m3fn_x4", "uint8", "bfloat16", "float32", "int32", "uint16"
SCRATCH = {}


def _buf(name, n, ty, where="sbuf"):
    SCRATCH[name] = (where, [128, n], ty)


for _n, _w, _t in (
        ("xt", 4 * C, BF), ("ut", 512, BF), ("vt", 512, BF), ("qx", C, F8), ("sx", C, U8),
        ("qu", 128, F8), ("su", 128, U8), ("qp", 384, F8), ("sp", 384, U8), ("qv", 128, F8), ("sv", 128, U8),
        ("qw", 512, F8), ("sw", 512, U8), ("qe", 512, F8), ("se", 512, U8), ("qk", 128, F8), ("sk", 128, U8),
        ("qn", 128, F8), ("sn", 128, U8), ("qy", 128, F8), ("sy", 128, U8), ("qh", 128, F8), ("sh", 128, U8),
        ("lc", LAND + R * M, F8), ("ls", LAND + R * M, U8),
        ("zt", 516, BF), ("et", 516, BF), ("en", 512, BF), ("bk", 512, BF), ("wt", 128, BF),
        ("pi", 8, I32), ("ii", 8, I32), ("cf", 24, F32), ("ul", 16, F32), ("ul16", 24, U16),
        ("rt", 32, BF), ("k32", 32, BF), ("q16", NT, U16), ("kp", C, BF), ("k2", C, BF), ("cw", C, BF), ("kx", 80, BF),
        ("p24", 24, F32), ("c24", 24 * 6, F32),
        ("ca", 176, F32), ("jt", C, F32), ("jc", NT, F32), ("jq", NT, F32), ("nt", M, F32),
        ("d1", C, F32), ("sj", C, F32), ("sg", 4 * C, BF), ("rs", NT, F32), ("jk", 256 * 14, BF),
        ("rl", 32 * RL, BF), ("pre", NT, F32), ("cs", C, F32), ("pl", NT, F32), ("pl16", NT, U16),
        ("m1", C, BF), ("val", C, F32), ("srt", 320, F32), ("so", 352, F32),
        ("ni", 14, I32), ("nj", 14, I32), ("nl16", 14, U16), ("f4", 4 * FS, BF),
        ("zh", 4 * (M + 4), BF), ("yt", 512, BF), ("ht", 512, BF), ("hp", 4 * M, BF), ("hg", 4 * C, BF),
        ("col", C, BF), ("co", 2 * C, BF), ("ab", 2 * NT, F32), ("ar", 2 * NT, F32), ("zz", 2 * NT, F32), ("b4", 2 * NT, F32),
        ("dd", NT, F32), ("bit", 2 * NT, F32), ("nn", 2 * NT, F32), ("lh", 2 * NT, F32), ("lh16", 2 * NT, U16),
        ("vs", M, F32), ("g1", C, F32), ("n16", NT, U16), ("ndu", C, F32), ("ys", C, F32)):
    _buf(_n, _w, _t)
SCRATCH["ga"] = ("sbuf", [128, 16 * LIST[1][1], 4], BF)
for _n in ("kc", "wl", "ns"):
    _buf(_n, 2 * C, BF)
for _w in range(4):
    _buf("gt%d" % _w, 4 * (GW[_w] + 32 * (_w == XT)), BF)
    _buf("qg%d" % _w, GW[_w] + 160, F8)
    _buf("sg%d" % _w, GW[_w] + 160, U8)
for _b in range(8):
    _buf("p%d" % _b, 512, F32, "psum")

SEMAPHORES = ["v", "a", "t", "g", "lxa", "lxb", "lu", "lw", "lv", "sent", "outs"] + ["arr%d" % r for r in range(R)]


def rank_program(g, core, T, topo):
    rank = T.rank_of(core)
    if rank is None:
        return
    A, F = AluOpType, ActivationFunctionType
    nxt = T.cores[(rank + 1) % len(T.cores)]
    rid, pid = topo.addr(nxt, core)
    mask = topo.mask(core, nxt)
    engines = topo.engines(core, nxt)
    ne = len(engines)
    halves = [sum(1 << e for e in engines[k::2]) for k in range(2)]
    V, S, P = g.vector, g.scalar, g.tensor
    queue = {"v": V, "a": S, "t": P, "g": g, "s": g.sync}
    count, known, snap, last, readers = {}, {e: {} for e in queue}, {}, {}, {}

    def wait(e, ev):
        s, n = ev
        if known[e].get(s, 0) >= n:
            return
        queue[e].wait_ge(T.sem[s], n)
        for k, x in snap[ev].items():
            known[e][k] = max(known[e].get(k, 0), x)

    def op(e, call, rd, wr, sem=None):
        need = []
        for x in rd:
            need.append(last[x])
            if x[0] == "P":
                need += [(s, n) for s, n in readers.get(x, {}).items() if s != e]
        for x in wr:
            if x in last:
                need.append(last[x])
            need += list(readers.get(x, {}).items())
        top = {}
        for s, n in need:
            if not (e == "t" and s == "t"):
                top[s] = max(top.get(s, 0), n)
        for s in sorted(top, key=lambda k: k == e):
            wait(e, (s, top[s]))
        s, inc = (e, 1) if sem is None else (sem, 16)
        call().then_inc(T.sem[s], inc)
        count[s] = count.get(s, 0) + inc
        ev = (s, count[s])
        snap[ev] = dict(known[e])
        snap[ev][s] = count[s]
        for x in rd:
            readers.setdefault(x, {})[s] = count[s]
        for x in wr:
            last[x] = ev
            readers[x] = {}

    def ts(out, in0, s1, op0, rd, wr, s2=None, op1=None):
        if op1 is None:
            op("v", lambda: V.tensor_scalar(out, in0, s1, None, op0), rd, wr)
        else:
            op("v", lambda: V.tensor_scalar(out, in0, s1, s2, op0, op1), rd, wr)

    def tt(out, a, b, o, rd, wr):
        op("v", lambda: V.tensor_tensor(out, a, b, o), rd, wr)

    def cp(out, a, rd, wr):
        op("v", lambda: V.tensor_copy(out, a), rd, wr)

    def fill(out, x, wr, rd=()):
        op("v", lambda: V.memset(out, x), list(rd), wr)

    def scan(out, a, b, o0, o1, rd, wr, first=0.0):
        op("v", lambda: V.tensor_tensor_scan(out, a, b, first, o0, o1), rd, wr)

    def quant(q, s, a, b, src, rd, wr):
        op("v", lambda: V.quantize_mx(T[q][:, a:b], T[s][:, a:b], src), rd, wr)

    def act(out, a, f, rd, wr, **kw):
        op("a", lambda: S.activation(out, a, f, **kw), rd, wr)

    def mm(bank, wq, ws, a, xq, xs, c0, c1, rd, start=True, stop=True):
        op("t", lambda: P.matmul_mx(T["p%d" % bank][:, 0:c1 - c0], T[wq][:, a:a + 128], T[ws][:, a:a + 128],
                                    T[xq][:, c0:c1], T[xs][:, c0:c1], start, stop), rd, ["P%d" % bank])

    def iota(out, pat, base, mult, wr, small=True):
        if small:
            op("g", lambda: g.iota(out, pat, base, mult, allow_small_or_imprecise_dtypes=True), [], wr)
        else:
            op("g", lambda: g.iota(out, pat, base, mult), [], wr)

    def zeros(out, n, wr):
        iota(out, [[0, n]], 0, 0, wr)

    def select(out, a, pat, cmp, x, base, mult, rd, wr):
        op("g", lambda: g.affine_select(out, a, pat, cmp, x, base, mult), rd, wr)

    def words(name, a, b):
        return T[name][:, a:b].bitcast(dt.uint32)

    def pick_codes(a, lst):
        op("v", lambda: V.tensor_copy(words("qp", a, a + 128), words("qu", 0, 128).indirect(T.ul16[:, a // 16:a // 16 + 8])),
           ["qu", lst], ["qp%d" % a])

    def pick_scales(a, lst):
        act(T.sp[:, a:a + 128], T.su[:, 0:128].indirect(T.ul16[:, a // 16:a // 16 + 8]), F.Copy, ["qu", lst], ["sp%d" % a])

    U0, UC, UD = 0, 128, 256
    UU = {a: ["qp%d" % a, "sp%d" % a] for a in (U0, UC, UD)}
    QX = ["qxa", "qxb"]
    ENDS = T.rl[:, 32 * (RL - 1):32 * (RL - 1) + NT]

    def slot(t):
        if t in EXT:
            w, e, a = XT, EXT.index(t), 4 * GW[XT]
        else:
            w, e, a = [(w, k.index(t), 0) for w, k in enumerate(TILES) if t in k][0]
        return "g%d" % t, T["gt%d" % w], a + e

    def rows_of(w):
        return ["g%d" % t for t in TILES[w] + (EXT if w == XT else ())]

    def pad(w):
        a, b = 64 * min(TILES[w]), 4 * (GW[w] + 32 * (w == XT))
        if w:
            zeros(T["gt%d" % w][:, a:b], b - a, rows_of(w))
        else:
            fill(T.gt0[:, a:4 * GW[0]], 0.0, ["g%d" % t for t in TILES[0]] + ["z0"])

    def quant_e(b):
        quant("qe", "se", 128 * b, 128 * b + 128, T.et[:, 3 - b:515 - b], ["et"], ["qe%d" % b])

    def spread(a, b):
        act(T.ca[:, a:b], T.ca[:, 0:b - a], F.Copy, ["ca"], ["ca"])

    op("a", lambda: S.dma_start(T.ut[:], T.u[:]), [], ["ut"], sem="lu")
    op("s", lambda: g.sync.dma_start(T.xt[:, 4 * CA:], T.x[:, 4 * CA:]), [], ["x%da" % e for e in range(4)], sem="lxa")
    op("s", lambda: g.sync.dma_start(T.xt[:, 0:4 * CA], T.x[:, 0:4 * CA]), [], ["x%db" % e for e in range(4)], sem="lxb")
    wait("s", last["x0b"])
    op("s", lambda: g.sync.dma_start(T.qw[:].bitcast(dt.uint8), T.wc[:]), [], [], sem="lw")
    op("s", lambda: g.sync.dma_start(T.sw[:], T.ws[:]), [], ["qw"], sem="lw")
    op("s", lambda: g.sync.dma_start(T.vt[:], T.v[:]), [], ["vt"], sem="lv")
    p1 = T.pi[:, 0:1]
    cq, ch, cc, cpar, cfl = [T.cf[:, k:k + 1] for k in range(5)]
    h6, sig, mb, low, stp, cya, cyb, cdb, csh, own, ow1, ow2 = [T.cf[:, k:k + 1] for k in range(5, 17)]
    c0, c1, c2, c3, c4, c5 = [T.c24[:, 24 * k:24 * k + 24] for k in range(6)]
    fill(T.zt[:], 0.0, ["zt"])
    iota(T.pi[:, 0:1], [[0, 1]], 0, 1, ["pi"], small=False)
    fill(T.et[:], 0.0, ["et"])
    iota(T.rt[:], [[0, 2], [1, 16]], 0, 0, ["rt"])
    iota(T.ul[:], [[1, 2], [16, 8]], 0, 0, ["ul"])
    select(T.et[:, 3:515:4], T.zt[:, 0:128], [[-1, 128]], A.not_equal, 1.0, 0, 1, ["zt", "et"], ["et"])
    act(T.wt[:], T.zt[:, 0:128], F.Identity, ["zt"], ["wt"], bias=1.0 / LIFT)
    act(T.wt[:, 15:128:16], T.zt[:, 0:8], F.Identity, ["zt", "wt"], ["wt"], bias=1.0)
    act(T.en[:], T.zt[:, 0:512], F.Copy, ["zt"], ["en"])
    select(T.wt[:], T.wt[:], [[-16, 8], [0, 16]], A.is_ge, 0.0, 0, 1, ["wt"], ["wt"])
    select(T.en[:, 0:512:4], T.zt[:, 0:128], [[-1, 128]], A.not_equal, -1.0, 0, 1, ["zt", "en"], ["en"])
    select(T.wt[:], T.wt[:], [[16, 8], [0, 16]], A.is_ge, 0.0, 15, -1, ["wt"], ["wt"])
    iota(T.p24[:], [[1, 24]], 24, 0, ["p24"])
    pad(2)
    pad(1)
    zeros(T.rs[:], NT, ["rs%d" % t for t in range(1, NT)])
    iota(T.jc[:], [[-16, NT]], MID - 15, 0, ["jc"])
    zeros(T.gt0[:, 4 * GW[0]:], 128, ["g%d" % t for t in EXT])
    pad(3)
    iota(T.jt[:], [[1, C]], MARK, 0, ["jt"])
    for k in range(FZ):
        zeros(T.f4[:, k:4 * FS:FS], 4, ["f4z%d" % k])
    zeros(T.yt[:, 4 * M:512], 128, ["ytz"])
    zeros(T.ht[:, 4 * M:512], 128, ["htz"])
    zeros(T.wl[:], 2 * C, ["wla", "wlb", "wll"])
    iota(T.nt[:], [[1, M]], 0, 0, ["nt"])

    fill(T.k2[:], 0.0, ["k2"])
    ts(T.ii[:, 0:1], p1, 15, A.bitwise_and, ["pi"], ["i0"])
    ts(T.ii[:, 1:2], p1, 2, A.arith_shift_right, ["pi"], ["i1"], 3, A.bitwise_and)
    ts(T.ii[:, 2:3], p1, 1, A.arith_shift_right, ["pi"], ["i2"], 1, A.bitwise_and)
    ts(T.ii[:, 3:4], p1, 2, A.arith_shift_right, ["pi"], ["i3"], 1, A.bitwise_and)
    ts(T.ii[:, 4:5], p1, 1, A.bitwise_and, ["pi"], ["i4"])
    fill(T.k2[:, 0:C:16], -4 * BIG, ["k2"])
    cp(T.ul16[:, 0:8], T.ul[:, 0:8], ["ul"], ["ul0"])
    cp(T.cf[:, 0:5], T.ii[:, 0:5], ["i0", "i1", "i2", "i3", "i4"], ["cf"])
    quant("qg%d" % XT, "sg%d" % XT, GW[XT] + 32, GW[XT] + 160, T.zt[:, 0:512], ["zt"], ["qgz"])
    quant("qg1", "sg1", GW[1], GW[1] + 128, T.zt[:, 0:512], ["zt"], ["qgz1"])
    ts(T.q16[:], T.zt[:, 0:NT], cq, A.add, ["zt", "cf"], ["q16"])
    ts(T.k32[:], T.rt[:], cq, A.not_equal, ["rt", "cf"], ["k32"], BIG, A.mult)
    act(h6, ch, F.Identity, ["cf"], ["h6"], scale=-6.0)
    act(stp, cfl, F.Identity, ["cf"], ["stp"], scale=-2 * STEP, bias=STEP - JUMP)
    ts(T.ul16[:, 8:16], T.ul[:, 8:16], cpar, A.add, ["ul", "cf"], ["ul1"])
    for b in (1, 2, 3):
        quant_e(b)
    act(T.kx[:, 0:32], T.k32[:], F.Sign, ["k32"], ["kx"])
    act(T.kp[:], T.k32[:, 0:16].indirect(T.q16[:]), F.Copy, ["k32", "q16"], ["kp"])
    act(T.kx[:, 32:64], T.kx[:, 0:32], F.Identity, ["kx"], ["kxo"], scale=1.0 - LIFT, bias=LIFT)
    quant("qu", "su", 0, 128, T.ut[:], ["ut"], ["qu"])
    quant_e(0)
    pick_codes(U0, "ul0")
    pick_scales(U0, "ul0")
    pick_scales(UC, "ul1")
    for e in range(4):
        act(T.bk[:, e:512:4], T.wt[:], F.Copy, ["wt"], ["bk%d" % e])
    act(c0, T.p24[:], F.Identity, ["p24", "h6"], ["c0"], bias=h6)
    act(sig, cc, F.Identity, ["cf"], ["sig"], scale=2.0, bias=-1.0)
    act(mb, cc, F.Identity, ["cf"], ["mb"], scale=-2 * TINY, bias=TINY)

    FIRST = {
        "scores a": [lambda: tt(T.kx[:, 64:80], T.kx[:, 16:32], T.kx[:, 47:63], A.mult, ["kx", "kxo"], ["cw16"]),
                     lambda: pick_codes(UC, "ul1"),
                     lambda: act(T.cw[:], T.kx[:, 64:80].indirect(T.q16[:]), F.Copy, ["cw16", "q16"], ["cw"])],
        "codes b": [lambda: pad(0)],
        "wrap 1": [lambda: quant("qn", "sn", 0, 128, T.en[:], ["en"], ["qn"]),
                   lambda: ts(c1, c0, 24.0, A.is_ge, ["c0"], ["c1"], -24.0, A.mult)],
        "wrap 2": [lambda: quant("qk", "sk", 0, 128, T.bk[:], ["bk%d" % e for e in range(4)], ["qk"]),
                   lambda: tt(c2, c0, c1, A.add, ["c0", "c1"], ["c2"])],
        "sums": [lambda: ts(c3, c2, 10.0, A.is_le, ["c2", "stp"], ["c3"], stp, A.mult),
                     lambda: ts(c4, c2, 23.0, A.is_ge, ["c2"], ["c4"], DROP - JUMP, A.mult)],
        "pre": [lambda: tt(c5, c3, c4, A.add, ["c3", "c4"], ["c5"])],
        "rows on Scalar": [
            lambda: act(T.jq[:], T.jc[:], F.Identity, ["jc", "cf"], ["jq"], bias=cq),
            lambda: act(ENDS, T.jc[:], F.Identity, ["jc", "cf"], ["rl%d" % t for t in SUM_VEC], bias=cq),
            lambda: act(own, T.kx[:, 15:16], F.Identity, ["kx"], ["own"], scale=LIFT - 1.0, bias=float(MID))],
    }

    def first(r, name):
        for f in FIRST.get(name, ()) if r == 0 else ():
            f()

    def sjc(t):
        return T.sj[:, 16 * t + 15:16 * t + 16], "sja" if 16 * t >= CA else "sjb"

    def sign(t, part):
        s, n = sjc(t)
        k = ON_ACT.index(t)
        if part == "b":
            act(T.sg[:, C * k:C * k + CA], T.p1[:, 0:CA], F.Sign, ["P1", n], ["sgb%d" % k], scale=-1.0, bias=s)
        else:
            act(T.sg[:, C * k + CA:C * k + 16 * t], T.p2[:, 0:16 * t - CA], F.Sign, ["P2", n], ["sga%d" % k], scale=-1.0, bias=s)

    def relu(t, rs):
        name, buf, a = slot(t)
        k = ON_ACT.index(t)
        act(buf[:, a:a + 64 * t:4], T.sg[:, C * k:C * k + 16 * t], F.Relu, ["sga%d" % k, "sgb%d" % k], [name, rs + "%d" % t],
            accum_out=T[rs][:, t:t + 1])

    def row(t, part="b"):
        name, buf, a = slot(t)
        s, n = sjc(t)
        if part == "b":
            ts(buf[:, a:a + 4 * min(CA, 16 * t):4], T.p0[:, 0:min(CA, 16 * t)], s, A.is_lt, ["P0", n], [name])
        else:
            ts(buf[:, a + 4 * CA:a + 64 * t:4], T.p4[:, 0:16 * t - CA], s, A.is_lt, ["P4", n, "z0"], [name + "a"])

    def rowsum(t, rs=None):
        name, buf, a = slot(t)
        rd = [name] + [name + "a"] * (16 * t > CA)
        if rs:
            act(T.jk[:, 256 * t:272 * t], buf[:, a:a + 64 * t:4], F.Identity, rd, [rs + "%d" % t], accum_out=T[rs][:, t:t + 1])
        else:
            scan(T.rl[:, 32 * (RL - 8 * t) + t:32 * RL:32], buf[:, a:a + 32 * t:4], buf[:, a + 32 * t:a + 64 * t:4], A.add, A.add,
                 rd + ["jq"], ["rl%d" % t], first=T.jq[:, t:t + 1])

    def inside(k):
        a, b = PART[k]
        _, buf, e = slot(NT)
        src, bank = (T.p4[:, 0:b - a], "P4") if k == "a" else (T.p0[:, a:b], "P0")
        tt(buf[:, 4 * a + e:4 * b:4], src, T.sj[:, a:b], A.is_le, [bank, "sj" + k, "z0"], ["dg" + k])

    def pack(w):
        n = GW[w] + 32 * (w == XT)
        quant("qg%d" % w, "sg%d" % w, 0, n, T["gt%d" % w][:], rows_of(w) + ["dga", "dgb"] * (NT in TILES[w])
              + ["g%da" % t for t in TILES[w] if t in ON_VEC and 16 * t > CA], ["qg%d" % w])

    def colsum(w):
        if GW[w] > LOW:
            mm(4, "qk", "sk", 0, "qg%d" % w, "sg%d" % w, LOW, max(GW[w], 2 * LOW), ["qk", "qg%d" % w, "qgz1"], w == 0, w == 2)
        mm(2, "qk", "sk", 0, "qg%d" % w, "sg%d" % w, 0, LOW, ["qk", "qg%d" % w], w == 0, w == 3)
        if w == XT:
            mm(2, "qk", "sk", 0, "qg%d" % w, "sg%d" % w, GW[w], GW[w] + 128, ["qk", "qg%d" % w, "qgz"], False, False)

    def quant_x(k):
        a, b = PART[k]
        quant("qx", "sx", a, b, T.xt[:, 4 * a:4 * b], ["x%d%s" % (e, k) for e in range(4)], ["qx" + k])

    def marks(a, b):
        scan(T.val[:, a:b], T.jt[:, a:b], T.m1[:, a:b], A.max, A.mult, ["m1", "jt"], ["val%d" % a])

    def wrap1(k):
        a, b = PART[k]
        src, bank = (T.p4[:, 0:b - a], "P4") if k == "a" else (T.p0[:, a:b], "P0")
        tt(T.d1[:, a:b], src, T.kp[:, a:b], A.subtract, [bank, "kp"], ["d1" + k])

    def wrap2(k):
        a, b = PART[k]
        scan(T.sj[:, a:b], T.k2[:, a:b], T.d1[:, a:b], A.add, A.max, ["k2", "d1" + k], ["sj" + k])

    def planes_to_psum(bs):
        for b in bs:
            mm(4 + b, "qe", "se", 128 * b, "qx", "sx", 0, C, ["qe%d" % b] + QX)

    def plane(b):
        act(T.f4[:, FS * b + FZ:FS * b + FZ + C], T["p%d" % (4 + b)][:, 0:C], F.Copy, ["P%d" % (4 + b)], ["f4%d" % b])

    def other_colour():
        mm(1, "qp", "sp", UD, "qx", "sx", 0, C, UU[UD] + QX)
        act(T.col[:], T.p1[:, 0:C], F.Sign, ["P1"], ["col"], bias=-TINY)

    def colour(k, a=0, b=C):
        scan(T.co[:, C * k + a:C * k + b], T.cw[:, a:b], (T.col if k else T.m1)[:, a:b], A.mult, A.add, ["cw", "col" if k else "m1"],
             ["co%d.%d" % (k, a)])

    def bits(k):
        if k:
            ts(T.bit[:, NT:], T.co[:, C + 15:2 * C:16], 0.0, A.is_gt, ["co1.0", "co1.%d" % CUT1, "cdb"], ["bit1"], cdb, A.add)
        else:
            ts(T.bit[:, 0:NT], T.co[:, 15:C:16], sig, A.mult, ["co0.0", "co0.%d" % MID, "sig"], ["bit0"], 0.0, A.is_gt)

    def interval(k):
        if k == 0:
            act(T.ab[:, 0:NT], T.pl[:], F.Identity, ["pl", "cya"], ["ab0"], scale=1.0 / 3, bias=cya)
            act(T.ab[:, NT:], T.pl[:], F.Identity, ["pl", "cyb"], ["ab1"], scale=1.0 / 3, bias=cyb)
        elif k == 1:
            act(T.zz[:], T.ab[:], F.Identity, ["ab0", "ab1"], ["zz"], bias=WHOLE)
        elif k == 2:
            act(T.ar[:], T.zz[:], F.Identity, ["zz"], ["ar"], bias=-WHOLE)
        elif k == 3:
            act(T.zz[:], T.ar[:], F.Relu, ["ar"], ["zz"], scale=-M / 4.0)
        else:
            tt(T.b4[:], T.ar[:], T.zz[:], A.add, ["ar", "zz"], ["b4"])

    def new_x(e, k, gathered):
        a, b = PART[k]
        out, name = T.xt[:, 4 * a + e:4 * b:4], "x%d%s" % (e, k)
        if gathered:
            tt(out, T["p%d" % (4 + e)][:, a:b], T.hg[:, C * e + a:C * e + b], A.add, ["P%d" % (4 + e), "hg%d%s" % (e, k)], [name])
        else:
            tt(out, T.hp[:, M * e:M * e + M].indirect(T.n16[:, a // 16:b // 16]), T.f4[:, FS * e + FZ + a:FS * e + FZ + b], A.add,
               ["hp%d" % e, "n16" + k, "f4%d" % e], [name])

    quant_x("a")
    for r in range(R):
        for b in (4, 2):
            mm(b, "qp", "sp", U0, "qx", "sx", CA, C, UU[U0] + ["qxa"])
        if r == 0:
            first(r, "scores a")
            quant_x("b")
            first(r, "codes b")
            wrap1("a")
        else:
            wrap1("a")
            quant_x("b")
        for b in (0, 1):
            mm(b, "qp", "sp", U0, "qx", "sx", 0, CA, UU[U0] + ["qxb"])
        mm(3, "qp", "sp", UC, "qx", "sx", 0, C, UU[UC] + QX)
        first(r, "wrap 1")
        wrap2("a")
        first(r, "wrap 2")
        for t in ON_ACT:
            sign(t, "a")
        inside("a")
        for t in ON_VEC:
            if 16 * t > CA:
                row(t, "a")
        first(r, "inside a")
        wrap1("b")
        row(ON_VEC[0])
        row(ON_VEC[1])
        wrap2("b")
        first(r, "wrap b")
        planes_to_psum((1, 2))
        rs, left = "rs", list(SUM_VEC)
        by_act = ON_VEC[len(left):]
        for k, t in enumerate(ON_ACT):
            sign(t, "b")
            if k > 1:
                relu(ON_ACT[k - 2], rs)
        for t in ON_ACT[-2:]:
            relu(t, rs)
        first(r, "rows on Scalar")
        for x in ORDER:
            if x == "in":
                inside("b")
            elif x == "s":
                rowsum(left.pop(0))
            elif x[0] == "p":
                pack(int(x[1]))
                first(r, x)
                if x == "p1":
                    mm(4, "qn", "sn", 0, "qg0", "sg0", LOW, C, ["qn", "qg0"], False, False)
                    mm(2, "qn", "sn", 0, "qg0", "sg0", 0, LOW, ["qn", "qg0"], False, False)
                colsum(int(x[1]))
            else:
                row(int(x))
        for t in left:
            rowsum(t)
        for t in by_act:
            rowsum(t, rs)
        act(T.m1[:], T.p3[:, 0:C], F.Sign, ["P3", "sig", "mb"], ["m1"], scale=sig, bias=mb)
        if r:
            other_colour()
        planes_to_psum((3,))
        first(r, "sums")
        scan(T.cs[:, LOW:], T.cw[:, LOW:], T.p4[:, 0:C - LOW], A.mult, A.add, ["cw", "P4"], ["cs1"])
        planes_to_psum((0,))
        scan(T.cs[:, 0:LOW], T.cw[:, 0:LOW], T.p2[:, 0:LOW], A.mult, A.add, ["cw", "P2"], ["cs"])
        tt(T.pre[:], ENDS, T[rs][:], A.add, [rs + "%d" % t for t in list(ON_ACT) + by_act] + ["rl%d" % t for t in SUM_VEC], ["pre"])
        first(r, "pre")
        marks(0, CUT)
        tt(T.pl[:], T.cs[:, 15:C:16], T.pre[:], A.subtract, ["pre", "cs", "cs1"], ["pl"])
        marks(CUT, C)
        colour(0, 0, MID)
        ts(T.pl16[:], T.pl[:], own, A.add, ["pl", "own"], ["pl16"])
        colour(0, MID, C)
        if r:
            colour(1, 0, CUT1)
        else:
            ts(T.ul16[:, 16:24], T.ul[:, 8:16], cpar, A.subtract, ["ul", "cf"], ["ul2"], 1.0, A.add)
            ts(low, cq, 15.0, A.is_equal, ["cf"], ["low"], 1.0 / LIFT, A.max)
        cp(T.srt[:, 0:C].indirect(T.pl16[:]), T.val[:], ["pl16", "val0", "val%d" % CUT], ["srt"])
        if r == 0:
            plane(1)
            act(T.ca[:, 0:24], c5, F.Identity, ["c5"], ["ca"], bias=JUMP)
            for b, n in ((2, 24), (3, 48), (0, 96)):
                plane(b)
                spread(n, min(2 * n, HALF[1]))
            act(T.kc[:, 0:2 * C:2], T.kx[:, 0:16].indirect(T.q16[:]), F.Copy, ["kx", "q16"], ["kc"])
            act(T.kc[:, 1:2 * C:2], T.kx[:, 32:48].indirect(T.q16[:]), F.Copy, ["kxo", "q16"], ["kco", "kcd"])
            pick_codes(UD, "ul2")
        else:
            for k, b in enumerate((1, 2, 3, 0)):
                plane(b)
                interval(k)
            colour(1, CUT1, C)
        cp(T.srt[:, C:C + HALF[1] - MID], T.srt[:, 0:HALF[1] - MID], ["srt"], ["srt6"])
        for h, n in enumerate(HALF):
            scan(T.so[:, 176 * h:176 * h + n], T.srt[:, MID * h:MID * h + n], T.ca[:, 0:n], A.max, A.add,
                 ["srt", "ca"] + ["srt6"] * h, ["so%d" % h], first=DROP)
        for h, (a, b) in enumerate(LIST):
            n = 176 * h + HALF[h]
            tt(T.ni[:, a:b], T.so[:, 176 * h + 20:n:24], T.so[:, 176 * h + 29:n:24], A.max, ["so%d" % h], ["ni%d" % h])
        for h, (a, b) in enumerate(LIST):
            ts(T.nj[:, a:b], T.ni[:, a:b], int(STEP) - 1, A.bitwise_and, ["ni%d" % h], ["nj%d" % h])
        for h, (a, b) in enumerate(LIST):
            ts(T.nl16[:, a:b], T.nj[:, a:b], float(FO), A.subtract, ["nj%d" % h], ["nl%d" % h], 0.0, A.max)
        for h, (a, b) in enumerate(LIST):
            for e in range(2):
                for x in (e, e + 2):
                    out, src = T.ga[:, 16 * a:16 * b, x], T.f4[:, FS * x:FS * x + FZ + C].indirect(T.nl16[:, a:b])
                    rd, wr = ["f4%d" % x, "nl%d" % h] + ["f4z%d" % k for k in range(FZ)], ["ga%d%d" % (x, h)]
                    if x < 2:
                        ts(out, src, 0.25, A.mult, rd, wr)
                    else:
                        act(out, src, F.Copy, rd, wr, scale=0.25)
        for h, (a, b) in enumerate(((0, M // 2), (M // 2, M + 2))):
            tt(T.zh[:, 4 * a:4 * b], T.ga[:, 2 * a:2 * b:2, :], T.ga[:, 2 * a + 1:2 * b:2, :], A.add,
               ["ga%d%d" % (x, h) for x in range(4)], ["zh%d" % h])
        for h, (a, b) in enumerate(((0, M // 2 - 2), (M // 2 - 2, M))):
            tt(T.yt[:, 4 * a:4 * b], T.zh[:, 4 * a:4 * b], T.zh[:, 4 * a + 8:4 * b + 8], A.add, ["zh0", "zh1"][:h + 1], ["yt%d" % h])
        bits(0)
        if r:
            interval(4)
            bits(1)
        else:
            quant("lc", "ls", 0, LAND, T.zt[:, 0:512], ["zt"], ["pad"])
            pick_scales(UD, "ul2")
            act(ow1, own, F.Identity, ["own"], ["ow1"], scale=1.0 / 3, bias=-5.5 / 3)
            act(ow2, own, F.Identity, ["own"], ["ow2"], scale=1.0 / 3, bias=-11.5 / 3)
            act(cdb, cpar, F.Identity, ["cf"], ["cdb"], scale=-4.0, bias=2.0)
            act(csh, cpar, F.Identity, ["cf"], ["csh"], scale=2.0)
            act(cya, cpar, F.Identity, ["cf", "ow1"], ["cya"], scale=-2.0, bias=ow1)
            act(cyb, cpar, F.Identity, ["cf", "ow2"], ["cyb"], scale=2.0, bias=ow2)
            interval(0)
            interval(1)
            other_colour()
            interval(2)
            interval(3)
        quant("qy", "sy", 0, 128, T.yt[:], ["yt0", "yt1", "ytz"], ["qy"])
        wait("g", last["qy"])
        at, arr = LAND + M * r, "arr%d" % r
        masks, n = ((mask, mask), 2 * ne) if r else (halves, ne)
        g.remote_dma(T.lc[:, at:at + M].bitcast(dt.uint8), T.qy[:, 0:M].bitcast(dt.uint8), T.sem[arr], T.sem.sent, pid, rid, masks[0])
        g.remote_dma(T.ls[:, at:at + M], T.sy[:, 0:M], T.sem[arr], T.sem.sent, pid, rid, masks[1])
        count["sent"] = count.get("sent", 0) + n
        snap[("sent", count["sent"])] = {"sent": count["sent"]}
        readers["qy"] = {"sent": count["sent"]}
        snap[(arr, n)] = {arr: n}
        last["land%d" % r] = (arr, n)
        if r == 0:
            colour(1, 0, CUT1)
            colour(1, CUT1, C)
            interval(4)
            bits(1)
        tt(T.nn[:], T.b4[:], T.bit[:], A.add, ["b4", "bit0", "bit1"], ["nn"])
        if r == 1:
            quant("qv", "sv", 0, 128, T.vt[:], ["vt"], ["qv"])
        tt(T.lh[:, 0:NT], T.nn[:, 0:NT], T.nn[:, NT:], A.min, ["nn"], ["lo"])
        tt(T.lh[:, NT:], T.nn[:, 0:NT], T.nn[:, NT:], A.max, ["nn"], ["hi"])
        z = 128 - M
        for b in range(4):
            mm(b, "qw", "sw", 128 * b, "lc", "ls", at - z, at + M, ["qw", "land%d" % r, "pad"])
            src, dst = T["p%d" % b][:, z:128], T.ht[:, b:4 * M:4]
            if b % 2 == 0:
                act(dst, src, F.Copy, ["P%d" % b], ["ht%d" % b], scale=0.03125)
            else:
                ts(dst, src, 0.03125, A.mult, ["P%d" % b], ["ht%d" % b])
        tt(T.dd[:], T.lh[:, NT:], T.lh[:, 0:NT], A.subtract, ["lo", "hi"], ["dd"])
        ts(T.lh16[:], T.lh[:], csh, A.add, ["lo", "hi", "csh"], ["lh16"])
        tt(T.wl[:, 31:2 * C:32], T.nn[:, 0:NT], T.nn[:, NT:], A.min, ["nn"], ["wll"])
        quant("qh", "sh", 0, 128, T.ht[:], ["ht0", "ht1", "ht2", "ht3", "htz"], ["qh"])
        mm(4, "qp", "sp", U0, "qh", "sh", 0, 128, UU[U0] + ["qh"])
        cp(T.vs[:], T.p4[:, 0:M], ["P4"], ["vs"])
        for b in (0, 1):
            cp(T.hp[:, M * b:M * b + M], T.ht[:, b:4 * M:4], ["ht%d" % b], ["hp%d" % b])
        ts(T.kc[:, 31:2 * C:32], T.dd[:], low, A.mult, ["dd", "low"], ["kcd"])
        ta = CA // 16
        cp(T.g1[:, CA:], T.vs[:].indirect(T.lh16[:, ta:NT]), ["vs", "lh16"], ["g1a"])
        act(T.g1[:, 0:CA], T.vs[:].indirect(T.lh16[:, 0:ta]), F.Copy, ["vs", "lh16"], ["g1b"])
        ab = "ab" if r < R - 1 else "ba"
        for k in ab:
            a, b = PART[k]
            tt(T.wl[:, 2 * a:2 * b:2], T.vs[:].indirect(T.lh16[:, NT + a // 16:NT + b // 16]), T.g1[:, a:b], A.is_gt,
               ["vs", "lh16", "g1" + k], ["wl" + k])
        for k in ab:
            a, b = PART[k]
            scan(T.ns[:, 2 * a:2 * b], T.kc[:, 2 * a:2 * b], T.wl[:, 2 * a:2 * b], A.mult, A.add,
                 ["kc", "kco", "kcd", "wl" + k, "wll"], ["ns" + k])
        for k in ab:
            a, b = PART[k]
            ts(T.n16[:, a // 16:b // 16], T.ns[:, 2 * a + 31:2 * b:32], csh, A.add, ["ns" + k, "csh"], ["n16" + k])
            for b in (3, 2) if k == ab[0] else ():
                cp(T.hp[:, M * b:M * b + M], T.ht[:, b:4 * M:4], ["ht%d" % b], ["hp%d" % b])
        for e, i in BY_ACT:
            a, b = PART[ab[i]]
            act(T.hg[:, C * e + a:C * e + b], T.hp[:, M * e:M * e + M].indirect(T.n16[:, a // 16:b // 16]), F.Copy,
                ["hp%d" % e, "n16" + ab[i]], ["hg%d%s" % (e, ab[i])])
        for e, i in AHEAD:
            new_x(e, ab[i], (e, i) in BY_ACT)
        quant_x(ab[0])
        for e in range(4):
            if (e, 1) not in AHEAD:
                new_x(e, ab[1], (e, 1) in BY_ACT)

    mm(0, "qv", "sv", 0, "qx", "sx", 0, CA, ["qv", "qxb"])
    act(T.ndu[:], T.nt[:].indirect(T.n16[:]), F.Copy, ["nt", "n16a", "n16b"], ["ndu"])
    op("s", lambda: g.sync.dma_start(T.nd[:], T.ndu[0:128:16, :]), ["ndu"], [], sem="outs")
    quant_x("a")
    mm(1, "qv", "sv", 0, "qx", "sx", CA, C, ["qv", "qxa"])
    act(T.ys[:, 0:CA], T.p0[:, 0:CA], F.Copy, ["P0"], ["ysb"])
    op("a", lambda: S.dma_start(T.y[:, 0:CA], T.ys[:, 0:CA]), ["ysb"], [], sem="outs")
    cp(T.ys[:, CA:], T.p1[:, 0:C - CA], ["P1"], ["ysa"])
    op("s", lambda: g.sync.dma_start(T.oc[:], T.qx[:].bitcast(dt.uint8)), QX, [], sem="outs")
    for k in range(4):
        e = "as"[k % 2]
        op(e, lambda: queue[e].dma_start(T.osc[4 * k:4 * k + 4, :], T.sx[32 * k:32 * k + 4, :]), QX, [], sem="outs")
    op("s", lambda: g.sync.dma_start(T.y[:, CA:], T.ys[:, CA:]), ["ysa"], [], sem="outs")
    for s in ("g", "sent", "t", "a", "v", "outs"):
        wait("s", (s, count[s]))
